import numpy as np, ml_dtypes
CORES = [113,118,241,246]
N = 4
BF = ml_dtypes.bfloat16
V, C, S, IT, Q, RO, D = 1536, 256, 256, 5, 11, 2, 2048
P = V + 2 * C * RO
def mesh(rng, m, isb, chain):
    o = rng.permutation(V); x = np.zeros(3 * V, np.int64); sn = np.zeros(2 * S, np.int64); rest = V - 2 * m
    x[2 * V + o[0:2 * m:2]] = o[1:2 * m:2]; x[2 * V + o[1:2 * m:2]] = o[0:2 * m:2]
    up = 2 * V + o[2 * m:]; leg = rng.integers(0, 2, rest) * V + o[:rest] if chain else rng.permutation(2 * V)[:rest]
    left = np.ones(2 * V, bool); left[leg] = False
    jb, jl = np.flatnonzero(isb), np.flatnonzero(~isb); c = rng.permutation(rest); cut, keep = c[:len(jb)], c[len(jb):]
    x[up[keep]] = leg[keep] % V; x[leg[keep]] = up[keep] - 2 * V
    x[up[cut]] = P + jb; sn[jb] = up[cut] - 2 * V
    pool = np.concatenate([rng.permutation(leg[cut]), rng.permutation(np.flatnonzero(left))]); h = rng.permutation(pool[:len(jl)])
    x[h] = P + jl; sn[jl] = h % V
    k = rng.permutation(pool[len(jl):]).reshape(2, -1); x[k[0]] = k[1] % V; x[k[1]] = k[0] % V
    return x.reshape(3, V), sn, o
def meshes(rng, m, chain=False):
    x = rng.choice(4, (N, 8, S), p=[0.35, 0.35, 0.2, 0.1])
    isb = np.concatenate([np.roll((x == 1) | (x == 3), 1, axis=0), (x == 0) | (x == 3)], axis=2)
    z = [[mesh(rng, int(m[a, g]), isb[a, g], chain) for g in range(8)] for a in range(N)]
    return tuple(np.stack([np.stack([u[i] for u in row]) for row in z]) for i in range(3))
def levels(rng):
    return rng.permuted(np.tile(np.array([60, 90, 110, 130, 150, 165, 180, 200]), (N, 1)), axis=1)[:, :, None, None] + rng.integers(-20, 21, (N, 8, 16, 1))
def errors(rng):
    return (256 * (0.25 + 0.75 * rng.random((N, 8, 1, V))) * rng.random((N, 8, 16, V))).astype(np.int64)
def under(rng, th):
    return np.minimum((th * rng.random((N, 8, 16, V))).astype(np.int64), th - 1)
def plant(rng, e, t, x, y, cnt):
    on = np.argsort(rng.random((16, len(x))), axis=0) < cnt[None, :]; one = rng.random(on.shape) < 0.5
    v = np.where(rng.random(on.shape) < 0.5, t, np.minimum(t + (rng.random(on.shape) * (256 - t)).astype(np.int64), 255))
    e[:, x] = np.where(on & one, v, e[:, x]); e[:, y] = np.where(on & ~one, v, e[:, y])
def more(rng):
    return rng.integers(0, 256, (N, 8, 16, D)), rng.integers(0, 256, (N, 8, 16, 1))
def pack(err, p, sn, det, wt, th):
    b = lambda a: np.ascontiguousarray(a.reshape(N, 128, -1)).astype(np.float32).astype(BF)
    i = lambda a: np.ascontiguousarray(a).astype(np.int32)
    return {"err": b(err), "lt": i(p[:, :, 0]), "rt": i(p[:, :, 1]), "bs": i(p[:, :, 2]), "snd": i(sn), "det": b(det), "wt": i(wt.reshape(N, 128, 1)), "th": i(th.reshape(N, 128, 1))}
def setup_inputs(rng):
    p, sn, o = meshes(rng, rng.integers(V // 8, V // 3 + 1, (N, 8))); det, wt = more(rng)
    return pack(errors(rng), p, sn, det, wt, levels(rng))
def setup_inputs_room(rng):
    M = V // 3; p, sn, o = meshes(rng, np.full((N, 8), M)); det, wt = more(rng)
    th = np.repeat(rng.integers(64, 192, (1, 8, 16, 1)), N, axis=0); err = under(rng, th)
    for a in range(N):
        for g in range(8):
            n = (C, C + 1, 0, 1, C - 1, M, C, C + 1)[(a + g) % 8]
            plant(rng, err[a, g], th[a, g], o[a, g, 0:2 * M:2], o[a, g, 1:2 * M:2], np.where(rng.permutation(M) < n, Q, Q - 1))
    return pack(err, p, sn, det, wt, th)
def setup_inputs_chain(rng):
    M = V // (2 * (IT + 3)); p, sn, o = meshes(rng, np.full((N, 8), M), True); det, wt = more(rng)
    th = np.repeat(rng.integers(64, 192, (1, 8, 16, 1)), N, axis=0); err = under(rng, th); far = np.array([0, 1, IT - 1, IT, IT, IT + 1, IT + 1])
    for a in range(N):
        for g in range(8):
            i = 2 * np.arange(M) + 2 * M * rng.permuted(np.resize(far, M))
            plant(rng, err[a, g], th[a, g], o[a, g, i], o[a, g, i + 1], np.where(rng.random(M) < 0.8, Q, Q - 1))
    return pack(err, p, sn, det, wt, th)
def setup_inputs_ties(rng):
    p, sn, o = meshes(rng, rng.integers(V // 8, V // 3 + 1, (N, 8))); det, wt = more(rng)
    th = np.clip(np.array([1, 2, 100, 128, 254, 255, 255, 30])[None, :, None, None] + rng.integers(-1, 2, (N, 8, 16, 1)), 1, 255); th[:, 6] = 255
    err = np.clip(th - 1 + (rng.random((N, 8, 16, V)) < 0.5 * rng.random((N, 8, 1, V))) * rng.integers(1, 3, (N, 8, 16, V)), 0, 255)
    err[:, 6] = np.minimum(err[:, 6], 254); err[:, 7] = 255
    det[:, 1] = 255; det[:, 2] = 0; wt[:, 0] = 0; wt[:, 1] = 255
    return pack(err, p, sn, det, wt, th)
def pools(rng):
    return [[int(z) for z in rng.permutation(V)] for a in range(N)], rng.permutation(S)[:8 * N].reshape(N, 2, 4)
def watch(x, leg, u, v, slot):
    x[leg, u] = P + slot; x[1 - leg, u] = v; x[2, u] = v; x[:, v] = u
def renamed(rng, x, sn, e):
    pool, kk = pools(rng)
    for a in range(N):
        for s in range(2):
            k, k2, kb, kb2 = [int(z) for z in kk[a, s]]; q, z = (a + 2 * s - 1) % N, (a - 2 * s + 1) % N
            t, b = pool[a].pop(), pool[a].pop()
            x[a, 2, t] = b; x[a, 2, b] = t; x[a, 0, t] = P + (1 - s) * S + k2; x[a, 1, t] = P + s * S + k; e[a, :, t] = 255
            sn[a, s * S + k] = t; sn[a, (1 - s) * S + k] = t
            u, v = pool[q].pop(), pool[q].pop(); sn[q, (1 - s) * S + k] = u; watch(x[q], s, u, v, (1 - s) * S + k)
            u, v = pool[z].pop(), pool[z].pop(); sn[z, s * S + k2] = u; watch(x[z], 1 - s, u, v, s * S + k)
            t, b = pool[a].pop(), pool[a].pop()
            x[a, 2, t] = b; x[a, 2, b] = t; x[a, 0, t] = P + s * S + kb2; e[a, :, t] = 255
            x[a, 1, t] = (P + s * S + kb) % (2 * S) + 2 * S * int(rng.integers(0, V // (2 * S))); sn[a, s * S + kb] = t
            u, v = pool[q].pop(), pool[q].pop(); sn[q, (1 - s) * S + kb2] = u; watch(x[q], s, u, v, (1 - s) * S + kb)
def allpairs(rng, x, e):
    for a in range(N):
        pr = np.sort(rng.permutation(V).reshape(-1, 2), axis=1); pr = pr[np.argsort(pr[:, 0])]
        x[a, 0, pr[0::2]] = pr[1::2]; x[a, 0, pr[1::2]] = pr[0::2]
        for i in (1, 2):
            x[a, i, pr[:, 0]] = pr[:, 1]; x[a, i, pr[:, 1]] = pr[:, 0]
        e[a][:, pr[len(pr) - C // 2:].reshape(-1)] = 255
def crowded(rng, x, sn, e):
    pool, kk = pools(rng)
    for a in range(N):
        for s in range(2):
            q = (a + 2 * s - 1) % N
            for i in range(2):
                k, kn = int(kk[a, s, 2 * i]), int(kk[a, s, 2 * i + 1]); many = [pool[a].pop() for z in range(V // 16)]
                x[a, 2, np.array(many)] = P + s * S + kn
                t = max(many) if i == 0 else min(many); e[a, :, t] = 255; sn[a, s * S + k] = t
                u, v = pool[q].pop(), pool[q].pop(); sn[q, (1 - s) * S + kn] = u; watch(x[q], 1 - i, u, v, (1 - s) * S + k)
def newbases(rng, x, sn, e, th):
    pool, kk = pools(rng)
    for a in range(N):
        pr = np.sort(np.array(pool[a][:2 * S]).reshape(S, 2), axis=1); pr = pr[np.argsort(pr[:, 0])]
        x[a, 2, pr[:, 0]] = pr[:, 1]; x[a, 2, pr[:, 1]] = pr[:, 0]
        plant(rng, e[a], th[a], pr[:, 0], pr[:, 1], rng.integers(Q, 17, S))
        for s in range(2):
            q = (a + 2 * s - 1) % N
            for i in range(2):
                k, kn = int(kk[a, s, 2 * i]), int(kk[a, s, 2 * i + 1]); j = (s * S + kn + P - V) % (2 * S)
                y = int(pr[j // 2, j % 2]); w = pool[a].pop()
                x[a, :, w] = y; x[a, 1, y] = w; e[a, :, w] = 255; sn[a, s * S + k] = w
                u, v = pool[q].pop(), pool[q].pop(); sn[q, (1 - s) * S + kn] = u; watch(x[q], i, u, v, (1 - s) * S + k)
def setup_inputs_free(rng):
    p = rng.choice(np.concatenate([np.arange(V), P + np.arange(2 * S)]), (N, 8, 3, V)); sn = rng.integers(0, V, (N, 8, 2 * S)); m = V // 4
    det, wt = more(rng); err = errors(rng); th = levels(rng)
    for a in range(N):
        for g in range(0, 8, 2):
            o = rng.permutation(V); x = p[a, g]; x[2, o[0:2 * m:2]] = o[1:2 * m:2]; x[2, o[1:2 * m:2]] = o[0:2 * m:2]
            v = o[2 * m:]; v = v[x[2, v] < V]; x[rng.integers(0, 2, len(v)), x[2, v]] = v
            x[0, o[:40]] = o[:40]; x[1, o[20:60]] = o[20:60]; x[0, o[100:140]] = x[1, o[100:140]]; x[1, o[200:240:2]] = o[201:240:2]
            j = rng.permutation(2 * S)[:S // 2]; x[1, sn[a, g, j]] = P + j
    for a in range(N):
        for g in range(0, 8, 2):
            for s in range(2):
                q = (a + 2 * s - 1) % N; k = rng.integers(0, S, 32); k2 = rng.integers(0, S, 32)
                p[q, g, 2, sn[q, g, (1 - s) * S + k]] = P + (1 - s) * S + k2
                p[a, g, rng.integers(0, 2, 32), sn[a, g, s * S + k2]] = P + s * S + k
    p[:, 0, 2, 0] = V - 1; p[:, 0, 2, V - 1] = 0; err[:, 0, :, 0] = 255; err[:, 0, :, V - 1] = 255
    n = 16; me = np.arange(V); two, lone = {}, {}
    for a in range(N):
        for g in range(0, 8, 2):
            x = p[a, g]
            b = np.minimum(x[2], V - 1); pair = (x[2] < V) & (x[2, b] == me) & (b != me)
            t = rng.permutation(np.flatnonzero(pair & (me < b) & (me > 0)))
            two[a, g] = rng.permuted(np.stack([t[:2 * n], b[t[:2 * n]]]), axis=0)
            lone[a, g] = rng.permutation(np.flatnonzero(~pair & (me > 0) & (me < V - 1)))[:2 * n]
            cut = t[C - 4 * n:]; x[2, cut] = P + rng.integers(0, 2 * S, len(cut))
    for g in range(0, 8, 2):
        k, k2 = rng.permutation(S)[:2 * n].reshape(2, n)
        for a in range(N):
            for s in range(2):
                q = (a + 2 * s - 1) % N; u, v = two[a, g][:, s * n:(s + 1) * n]; w = lone[q, g][(1 - s) * n:(2 - s) * n]
                sn[a, g, s * S + k2] = u; sn[q, g, (1 - s) * S + k] = w
                x = p[a, g]; x[0, u] = P + s * S + k; x[1, u] = v; x[0, v] = u; x[1, v] = u
                p[q, g, 2, w] = np.where(np.arange(n) < n // 2, P + s * S + k2, (P + k2) % S + S * rng.integers(0, V // S, n))
                e = err[a, g]; c = np.concatenate([u, v]); e[:, c] = np.minimum(e[:, c], th[a, g] - 1)
                plant(rng, err[q, g], th[a, g], w, w, rng.integers(Q, 17, n))
    th[:, 1::2] = rng.integers(20, 121, (N, 4, 16, 1)); err[:, 1::2] = under(rng, th)[:, 1::2]
    p[:, 1::2, 2] = P + rng.integers(0, 2 * S, (N, 4, V)); p[:, 5] = P + rng.integers(0, 2 * S, (N, 3, V))
    sn[:, 5] = rng.choice(np.array([0, V - 1, V // 2, 5]), (N, 2 * S))
    renamed(rng, p[:, 1], sn[:, 1], err[:, 1]); allpairs(rng, p[:, 3], err[:, 3])
    crowded(rng, p[:, 5], sn[:, 5], err[:, 5]); newbases(rng, p[:, 7], sn[:, 7], err[:, 7], th[:, 7])
    return pack(err, p, sn, det, wt, th)
def setup_inputs_spread(rng):
    p, sn, o = meshes(rng, rng.integers(V // 8, V // 3 + 1, (N, 8)))
    err = (np.exp2(8 * rng.random((N, 8, 1, V))) * rng.random((N, 8, 16, V))).astype(np.int64)
    det = (np.exp2(8 * rng.random((N, 8, 1, D))) * rng.random((N, 8, 16, D))).astype(np.int64)
    wt = np.minimum(np.exp2(8 * rng.random((N, 8, 16, 1))).astype(np.int64), 255)
    th = np.clip(np.exp2(3 + 5 * rng.random((N, 8, 1, 1)) + rng.random((N, 8, 16, 1)) - 0.5).astype(np.int64), 1, 255)
    return pack(np.minimum(err, 255), p, sn, np.minimum(det, 255), wt, th)
def check_inputs(d):
    bad = []
    for k in ("err", "det"):
        x = np.asarray(d[k]).astype(np.float32)
        if not np.all((x >= 0) & (x <= 255) & (x == np.floor(x))): bad.append("range of " + k)
    for k in ("lt", "rt", "bs"):
        x = d[k]
        if not np.all(((x >= 0) & (x < V)) | ((x >= P) & (x < P + 2 * S))): bad.append("range of " + k)
    for k, lo, hi in (("snd", 0, V - 1), ("wt", 0, 255), ("th", 1, 255)):
        if np.min(d[k]) < lo or np.max(d[k]) > hi: bad.append("range of " + k)
    return bad
def ghosts(x):
    return np.concatenate([np.roll(x[..., S:], 1, axis=0), np.roll(x[..., :S], -1, axis=0)], axis=-1)
def reference(err, lt, rt, bs, snd, det, wt, th):
    take = np.take_along_axis; me = np.arange(P)
    e = np.zeros((N, 8, 16, P), np.int32); e[..., :V] = err.astype(np.float32).astype(np.int32).reshape(N, 8, 16, V)
    dt = det.astype(np.float32).astype(np.int32).reshape(N, 8, 16, D); wq = wt.astype(np.int32).reshape(N, 8, 16, 1); tq = th.astype(np.int32).reshape(N, 8, 16, 1)
    p = np.zeros((N, 8, 3, P), np.int64) + me
    p[:, :, 0, :V] = lt; p[:, :, 1, :V] = rt; p[:, :, 2, :V] = bs
    sn = snd.astype(np.int64)
    lo = np.repeat(np.array([0, S]), S); off = np.repeat(np.array([-S, S]), S)
    for t in range(RO):
        L, R, B = p[:, :, 0], p[:, :, 1], p[:, :, 2]
        j = ghosts(take(B, sn, 2)) - P + off
        gb = np.where((j >= lo) & (j < lo + S), take(sn, np.clip(j, 0, 2 * S - 1), 2), -1)
        base = np.concatenate([B, gb], axis=2); gl = (take(base, L, 2) == me)[:, :, None]; gr = (take(base, R, 2) == me)[:, :, None]
        W = e
        for it in range(IT):
            A = np.concatenate([W, ghosts(take(W, sn[:, :, None], 3))], axis=3)
            W = np.maximum(W, np.maximum(np.where(gl, take(A, L[:, :, None], 3), 0), np.where(gr, take(A, R[:, :, None], 3), 0)))
        bo = np.minimum(B, P - 1); pair = (B < P) & (take(B, bo, 2) == me) & (me < B)
        rows = np.add.reduce((np.maximum(W, take(W, bo[:, :, None], 3)) >= tq).astype(np.int32), axis=2)
        go = (pair & (rows >= Q)).astype(np.int64); k = np.add.accumulate(go, axis=2) - go
        a, g, x = np.nonzero((go == 1) & (k < C)); y = B[a, g, x]
        new = np.zeros((N, 8, P), np.int64)
        new[a, g, x] = V + 2 * C * t + 2 * k[a, g, x]; new[a, g, y] = new[a, g, x] + 1
        nx = np.concatenate([new, np.zeros((N, 8, 2 * S), np.int64)], axis=2); rx = np.concatenate([R, np.full((N, 8, 2 * S), -1)], axis=2)
        pn = np.stack([np.where((take(nx, T, 2) > 0) & (take(rx, T, 2) == me), take(nx, T, 2), T) for T in (L, R, B)], axis=2)
        sn = np.where((take(new, sn, 2) > 0) & (take(R, sn, 2) == P + np.arange(2 * S)), take(new, sn, 2), sn)
        a = np.concatenate([a, a]); g = np.concatenate([g, g]); s = np.concatenate([x, y]); o = np.concatenate([y, x])
        n, m = new[a, g, s], new[a, g, o]; bl, br = pn[a, g, 0, s], pn[a, g, 1, s]
        pn[a, g, 0, s] = n; pn[a, g, 1, s] = m; pn[a, g, 2, s] = bl
        pn[a, g, 0, n] = o; pn[a, g, 1, n] = s; pn[a, g, 2, n] = br
        p = pn
        es = e[a, g, :, s]; h = np.add.reduce(wq * e, axis=2)[a, g, s]
        for place in (s, n):
            e[a, g, :, place] = (es >> 1) + (dt[a, g, :, (h + place) & (D - 1)] >> 1)
    return {"ye": e.reshape(N, 128, P).astype(np.float32).astype(BF), "yl": p[:, :, 0].astype(np.float32), "yr": p[:, :, 1].astype(np.float32), "yb": p[:, :, 2].astype(np.float32)}

@@ -1,0 +1,706 @@
+import numpy as np
+from concourse.mybir import dt, AluOpType, AxisListType, ActivationFunctionType
+
+OP = AluOpType
+AF = ActivationFunctionType
+NR = 4
+V0 = 1536
+GH = 2560
+OWN = 528
+
+SCRATCH = {}
+PK = {}
+
+
+def _pack(big, dtype, parts):
+    o = 0
+    for n, c in parts:
+        PK[n] = (big, o)
+        o += (c + 15) // 16 * 16
+    SCRATCH[big] = ("sbuf", [128, o], dtype)
+
+
+_pack("kf", "float32", (("pq", 16), ("meS", 160), ("slotc", 32), ("zer", 128), ("thf", 1), ("wtf", 1), ("ab", 2),
+                        ("st0", 352), ("st1", 448), ("ns0", 288), ("ns1", 384), ("ns2", 480), ("sn0", 32), ("sn1", 32),
+                        ("ixa", 320), ("ixb", 320), ("ulf", 320), ("mB", 128), ("mB2", 128), ("pe", 128), ("thr", 128),
+                        ("xo", 32), ("xz", 32), ("xo2", 32), ("sc", 128), ("ka", 128), ("kc", 128), ("kd", 128),
+                        ("pm2", 384), ("fl", 384), ("lff", 384), ("t32", 32), ("z", 512), ("pt", 384), ("q3", 384),
+                        ("q3u", 384), ("sp", 128), ("nsp", 128), ("ysn", 256), ("yss", 256), ("oa", 128), ("ob", 128),
+                        ("oc", 128), ("od", 128), ("tsw", 32), ("tab", 32), ("td", 32), ("zy", 32), ("yzy", 32), ("yt", 32),
+                        ("yu", 32), ("snv", 32), ("sna", 32), ("snb", 32), ("snc", 32), ("hq", 64), ("hm", 64), ("pres", 64)))
+_pack("ki", "int32", (("nraw", 288), ("nsn", 32), ("thi", 1), ("wti", 1), ("ik", 16), ("ik2", 16), ("pmi", 160), ("pmod", 160),
+                      ("c16", 160), ("hz", 64), ("hz2", 64)))
+_pack("ku", "uint16", (("li0", 352), ("li1", 448), ("snl0", 32), ("snl1", 32), ("gbo", 32), ("bo", 32), ("ul", 320), ("pl", 128),
+                       ("koff", 128), ("tl", 16), ("TL", 32), ("lf", 384), ("snf", 32), ("eo", 64)))
+_pack("kh", "float16", (("n16", 288), ("nsn16", 32), ("ra", 1536), ("rb", 1536), ("rc", 1536), ("bs16", 512), ("ls16", 1024),
+                        ("T16", 512), ("Y16", 512), ("x16", 384), ("sn16", 32), ("me16", 128)))
+_pack("kb", "bfloat16", (("ones", 128), ("eye", 128), ("blk", 128), ("blka", 128), ("tri", 128), ("ltg", 128), ("jq", 256),
+                         ("jrow", 512), ("go", 128), ("eT", 512), ("e2", 512), ("e2b", 512), ("cT", 512), ("vs", 512), ("vy", 512),
+                         ("sb0", 512), ("sb1", 512), ("sb2", 512), ("sb3", 512), ("sb4", 512)))
+for _n, _c, _d in (("brow", 3088, "float32"), ("lrow", 3088, "float32"), ("rrow", 3088, "float32"), ("mex", 2560, "float32"),
+                   ("snt", 544, "float32"), ("fr", 2048, "float32"), ("MDf", 2048, "float32"),
+                   ("MD", 2048, "bfloat16"), ("EQ", 2048, "bfloat16"), ("CQ", 2048, "bfloat16"), ("WQ", 2048, "bfloat16"),
+                   ("dtb", 2064, "bfloat16"), ("NT", 2576, "bfloat16"), ("vL", 2048, "bfloat16"), ("vR", 2560, "bfloat16"),
+                   ("vB", 2048, "bfloat16"), ("U0", OWN + 2560, "bfloat16"), ("U1", OWN + 2048, "bfloat16"),
+                   ("U2", OWN + 2048, "bfloat16"), ("U3", OWN + 2048, "bfloat16"), ("U4", OWN + 2048, "bfloat16"),
+                   ("u5", 2048, "bfloat16"), ("gr0", 2560, "bfloat16"), ("gr1", 2560, "bfloat16"), ("in0", 2048, "bfloat16"),
+                   ("in1", 2048, "bfloat16")):
+    SCRATCH[_n] = ("sbuf", [128, _c], _d)
+for _n in range(8):
+    SCRATCH["p%d" % _n] = ("psum", [128, 512], "float32")
+
+KINDS = ["b", "0", "1", "2", "3", "4"]
+SEMAPHORES = (["cv", "cs", "cp", "cg"] + ["d%d" % i for i in range(24)]
+              + ["r%s%d" % (k, s) for k in KINDS for s in range(2)] + ["l%s%d" % (k, s) for k in KINDS for s in range(2)])
+
+
+def _is_psum(n):
+    return len(n) == 2 and n[0] == "p" and n[1].isdigit()
+
+
+def rank_program(g, core, T, topo):
+    rank = T.rank_of(core)
+    if rank is None:
+        return
+    nb_core = [T.cores[(rank - 1) % NR], T.cores[(rank + 1) % NR]]
+    order = sorted(range(2), key=lambda s: nb_core[s] in topo.cores_of(core))
+
+    Q = {"V": g.vector, "S": g.scalar, "P": g.tensor, "G": g, "Y": g.sync}
+    SEM = {"V": "cv", "S": "cs", "P": "cp", "G": "cg"}
+    cnt = {}
+    known = {q: {} for q in Q}
+    snaps = {}
+    hist = {}
+
+    def wait_for(q, need):
+        for s in sorted(need):
+            v = need[s]
+            if known[q].get(s, 0) >= v:
+                continue
+            Q[q].wait_ge(T.sem[s], v)
+            known[q][s] = v
+            for s2, v2 in snaps.get((s, v), {}).items():
+                if known[q].get(s2, 0) < v2:
+                    known[q][s2] = v2
+
+    def needs(q, reads, writes):
+        need = {}
+        for regs, w in ((reads, 0), (writes, 1)):
+            for n, lo, hi in regs:
+                ps = _is_psum(n)
+                for e in hist.get(n, []):
+                    if not ps and (e[0] >= hi or lo >= e[1]):
+                        continue
+                    if ps:
+                        if e[5] == q and (q == "P" or not (w or e[2])):
+                            continue
+                    elif not (w or e[2]):
+                        continue
+                    if need.get(e[3], 0) < e[4]:
+                        need[e[3]] = e[4]
+        return need
+
+    def note(q, reads, writes, sem, val):
+        snaps[(sem, val)] = dict(known[q]) if q else {}
+        for regs, w in ((writes, 1), (reads, 0)):
+            for n, lo, hi in regs:
+                old = hist.get(n, [])
+                if w:
+                    old = [e for e in old if not (lo <= e[0] and e[1] <= hi)]
+                else:
+                    old = [e for e in old if not (e[2] == 0 and e[3] == sem and lo <= e[0] and e[1] <= hi)]
+                old.append((lo, hi, w, sem, val, q))
+                hist[n] = old
+
+    def op(q, fns, reads, writes):
+        wait_for(q, needs(q, reads, writes))
+        s = SEM[q]
+        for f in fns:
+            f().then_inc(T.sem[s], 1)
+            cnt[s] = cnt.get(s, 0) + 1
+        note(q, reads, writes, s, cnt[s])
+
+    ndma = [0]
+
+    def dma(q, out, in_):
+        wait_for(q, needs(q, in_[1], out[1]))
+        s = "d%d" % ndma[0]
+        ndma[0] += 1
+        Q[q].dma_start(out[0], in_[0]).then_inc(T.sem[s], 16)
+        cnt[s] = 16
+        note(q, in_[1], out[1], s, 16)
+
+    def X(n, lo, hi, st=1):
+        if n in PK:
+            t, o = T[PK[n][0]], PK[n][1]
+        else:
+            t, o = T[n], 0
+        return t[:, o + lo:o + hi] if st == 1 else t[:, o + lo:o + hi:st]
+
+    def A(n, lo, hi, st=1):
+        return (X(n, lo, hi, st), [(n, lo, hi)])
+
+    def ind(w, o):
+        return (w[0].indirect(o[0]), w[1] + o[1])
+
+    def tt(out, a, b, f):
+        op("V", [lambda: g.vector.tensor_tensor(out[0], a[0], b[0], f)], a[1] + b[1], out[1])
+
+    def ts(out, a, s1, f1, s2=None, f2=None):
+        r = list(a[1])
+        v1 = s1
+        if isinstance(s1, tuple):
+            r += s1[1]
+            v1 = s1[0]
+        if f2 is None:
+            op("V", [lambda: g.vector.tensor_scalar(out[0], a[0], v1, None, f1)], r, out[1])
+        else:
+            op("V", [lambda: g.vector.tensor_scalar(out[0], a[0], v1, s2, f1, f2)], r, out[1])
+
+    def cp(out, a):
+        op("V", [lambda: g.vector.tensor_copy(out[0], a[0])], a[1], out[1])
+
+    def scat(w, o, a):
+        op("V", [lambda: g.vector.tensor_copy(w[0].indirect(o[0]), a[0])], a[1] + o[1], w[1])
+
+    def ms(out, v):
+        op("V", [lambda: g.vector.memset(out[0], v)], [], out[1])
+
+    def act(out, a, f=AF.Copy, bias=0.0, scale=1.0):
+        r = list(a[1])
+        sc = scale
+        if isinstance(scale, tuple):
+            r += scale[1]
+            sc = scale[0]
+        bi = bias
+        if isinstance(bias, tuple):
+            r += bias[1]
+            bi = bias[0]
+        op("S", [lambda: g.scalar.activation(out[0], a[0], f, bias=bi, scale=sc)], r, out[1])
+
+    def iota(out, pattern, base, cm, small=True):
+        if small:
+            op("G", [lambda: g.iota(out[0], pattern, base, cm, allow_small_or_imprecise_dtypes=True)], [], out[1])
+        else:
+            op("G", [lambda: g.iota(out[0], pattern, base, cm)], [], out[1])
+
+    def sel(out, a, pattern, cmp, base, cm):
+        op("G", [lambda: g.affine_select(out[0], a[0], pattern, cmp, 0.0, base, cm)], a[1], out[1])
+
+    bank = [4]
+
+    def wb():
+        b = bank[0]
+        bank[0] = 4 + (b - 3) % 4
+        return "p%d" % b
+
+    def mm(b, jobs):
+        fns, rd = [], []
+        for o, l, r, s0, s1 in jobs:
+            fns.append(lambda o=o, l=l, r=r, s0=s0, s1=s1: g.tensor.matmul(o[0], l[0], r[0], s0, s1))
+            for x in (l, r):
+                if x[1][0] not in rd:
+                    rd.append(x[1][0])
+        op("P", fns, rd, [(b, 0, 512)])
+
+    def conv(b, jobs):
+        js = []
+        for lo, hi, st, m, rh in jobs:
+            for q in range(16):
+                js.append((A(b, lo, hi, st), A(m, 128 * q, 128 * q + 128), rh(q), q == 0, q == 15))
+        mm(b, js)
+
+    def rS(n, lo, hi):
+        return lambda q: (X(n, lo + q, hi, 16), [(n, lo, hi)])
+
+    def chosen(src, dst):
+        return topo.engines(src, dst)[-8:]
+
+    def send(s, kind, src, dst, lo, hi):
+        d = nb_core[s]
+        wait_for("G", needs("G", src[1], []))
+        rid, pid = topo.addr(d, core)
+        es = chosen(core, d)
+        ls = "l%s%d" % (kind, s)
+        g.remote_dma(X(dst, lo, hi), src[0], T.sem["r%s%d" % (kind, 1 - s)], T.sem[ls], pid, rid, sum(1 << e for e in es))
+        cnt[ls] = cnt.get(ls, 0) + len(es)
+        note("G", src[1], [], ls, cnt[ls])
+
+    def recv(s, kind, dst, lo, hi):
+        rs = "r%s%d" % (kind, s)
+        cnt[rs] = cnt.get(rs, 0) + len(chosen(nb_core[s], core))
+        note(None, [], [(dst, lo, hi)], rs, cnt[rs])
+
+    def HB(n):
+        return T[n][:]
+
+    PP, NW, LW = (V0, 2048), (96, 128), (128, 160)
+
+    dma("Y", A("nsn", 0, 32), (HB("snd"), []))
+    dma("S", A("nraw", 192, 288), (HB("bs"), []))
+    dma("Y", A("nraw", 96, 192), (HB("rt"), []))
+    dma("S", A("nraw", 0, 96), (HB("lt"), []))
+    dma("Y", A("U0", OWN, OWN + V0), (HB("err"), []))
+    dma("S", A("thi", 0, 1), (HB("th"), []))
+    dma("S", A("wti", 0, 1), (HB("wt"), []))
+    dma("Y", A("dtb", 0, 2048), (HB("det"), []))
+
+    ms(A("ones", 0, 128), 1.0)
+    iota(A("ik", 0, 16), [[-1, 16]], 16, 1, False)
+    sel(A("blka", 0, 128), A("ones", 0, 128), [[-16, 8], [0, 16]], OP.is_ge, 0, 1)
+    sel(A("blk", 0, 128), A("blka", 0, 128), [[16, 8], [0, 16]], OP.is_ge, 15, -1)
+    sel(A("eye", 0, 128), A("ones", 0, 128), [[-1, 128]], OP.is_equal, 0, 1)
+    iota(A("pmi", 0, 160), [[0, 160]], 0, 1, False)
+    iota(A("c16", 0, 160), [[16, 160]], 0, 0, False)
+    iota(A("brow", V0, GH), [[2, 512], [-1, 2]], V0 + 1, 0)
+    iota(A("mex", 512, 2560), [[1, 2048]], 0, 0)
+    ts(A("ik2", 0, 16), A("ik", 0, 16), 15, OP.bitwise_and)
+    ts(A("pq", 0, 16), A("ik2", 0, 16), 0, OP.is_equal)
+    for q in range(16):
+        ts(A("EQ", 128 * q, 128 * q + 128), A("blk", 0, 128), A("pq", q, q + 1), OP.mult)
+        act(A("MD", 128 * q, 128 * q + 128), A("eye", 0, 128), AF.Copy, scale=A("pq", q, q + 1))
+    ts(A("nsn16", 0, 32), A("nsn", 0, 32), -1536, OP.add)
+    ts(A("n16", 192, 288), A("nraw", 192, 288), -1536, OP.add)
+    ts(A("n16", 0, 192), A("nraw", 0, 192), -1536, OP.add)
+
+    def nrow(x, lo, row, r16):
+        for i in range(4):
+            b = wb()
+            k = min(5, 16 - 5 * i)
+            mm(b, [(A(b, 96 * j, 96 * j + 96), A("EQ", 128 * (5 * i + j), 128 * (5 * i + j) + 128), A(x, lo, lo + 96), True, True)
+                   for j in range(k)])
+            act(A(row, 480 * i, 480 * i + 96 * k), A(b, 0, 96 * k), AF.Identity, bias=1536.0)
+            cp(A(r16, 480 * i, 480 * i + 96 * k), A(b, 0, 96 * k))
+
+    b = wb()
+    mm(b, [(A(b, 32 * q, 32 * q + 32), A("EQ", 128 * q, 128 * q + 128), A("nsn16", 0, 32), True, True) for q in range(16)])
+    cp(A("bs16", 0, 512), A(b, 0, 512))
+    sb = b
+    b = wb()
+    conv(b, [(0, 32, 1, "MD", rS("bs16", 0, 512))])
+    ts(A("snl0", 0, 32), A(b, 0, 32), 1536, OP.add)
+    ts(A("sn0", 0, 32), A(b, 0, 32), 1536, OP.add)
+    act(A("mex", 0, 512), A(sb, 0, 512), AF.Identity, bias=1536.0)
+
+    def sndtab():
+        for s in range(2):
+            act(A("snt", 272 * s, 272 * s + 256), A("mex", 256 * s, 256 * s + 256))
+
+    nrow("n16", 192, "brow", "ra")
+    nrow("n16", 96, "rrow", "rb")
+    nrow("n16", 0, "lrow", "rc")
+    sndtab()
+    ms(A("snt", 256, 272), -1.0)
+    ms(A("snt", 528, 544), -1.0)
+    for i in range(5):
+        ms(A("U%d" % i, 0, 16), 0.0)
+
+    def base_send(t, P):
+        ts(A("bs16", 0, 512), ind(A("brow", 0, P), A("snl%d" % t, 0, 32)), -1536, OP.add)
+        b = wb()
+        conv(b, [(0, 32, 1, "MD", rS("bs16", 0, 512))])
+        for s in range(2):
+            ts(A("xo", 16 * s, 16 * s + 16), A(b, 16 * s, 16 * s + 16), -1024 - 256 * s, OP.add)
+        ts(A("xz", 0, 32), A("xo", 0, 32), 0, OP.is_lt, 8192, OP.mult)
+        tt(A("xo2", 0, 32), A("xo", 0, 32), A("xz", 0, 32), OP.add)
+        ts(A("bo", 0, 32), A("xo2", 0, 32), 256, OP.min)
+        for s in order:
+            send(s, "b", A("bo", 16 * s, 16 * s + 16), "gbo", 16 * (1 - s), 16 * (1 - s) + 16)
+
+    def ghost0(t, P):
+        for i, s in enumerate(order):
+            o = A("sb0", 256 * s, 256 * s + 256)
+            x = ind(A("U0", OWN, OWN + P), A("snl%d" % t, 16 * s, 16 * s + 16))
+            if i == 0:
+                cp(o, x)
+            else:
+                act(o, x)
+        for s in order:
+            send(s, "0", A("sb0", 256 * s, 256 * s + 256), "U0", 16 + 256 * (1 - s), 16 + 256 * (1 - s) + 256)
+
+    def stlist(lo, t, leg, src):
+        nw, lw = NW[t], LW[t]
+        o = leg * lw + (32 if leg < 2 else 0)
+        for n in ("li%d" % t, "st%d" % t):
+            ts(A(n, o, o + nw), A(src, lo, lo + nw), 1536, OP.add)
+
+    base_send(0, V0)
+    cp(A("thf", 0, 1), A("thi", 0, 1))
+    cp(A("wtf", 0, 1), A("wti", 0, 1))
+    b = wb()
+    conv(b, [(192, 288, 1, "MD", rS("ra", 0, V0)), (96, 192, 1, "MD", rS("rb", 0, V0)), (0, 96, 1, "MD", rS("rc", 0, V0))])
+    ghost0(0, V0)
+    ts(A("pmod", 0, 160), A("pmi", 0, 160), 15, OP.bitwise_and)
+    tt(A("meS", 0, 160), A("pmod", 0, 160), A("c16", 0, 160), OP.add)
+    ts(A("slotc", 0, 32), A("meS", 0, 32), GH, OP.add)
+    for leg in (2, 1, 0):
+        stlist(96 * leg, 0, leg, b)
+    cb = (A("ab", 0, 1), A("ab", 1, 2))
+    ms(cb[0], -0.5)
+    ms(cb[1], 0.5)
+
+    def prep(t):
+        P, nw, lw = PP[t], NW[t], LW[t]
+        st, li = "st%d" % t, "li%d" % t
+        B0 = 2 * lw
+        ts(A("pl", 0, nw), A(st, B0, B0 + nw), P - 1, OP.min)
+        act(A("fr", 0, P), ind(A("brow", 0, P), A("pl", 0, nw)))
+        if t == 0:
+            masks2()
+        h = lw // 2 + 16
+
+        def valid(b, i, c0, c1):
+            nm = "gr%d" % i
+            tt(A(nm, 16 * c0, 16 * c1), ind(A("brow", 0, 3072), A(li, i * lw + c0, i * lw + c1)), A("mex", 16 * c0, 16 * c1), OP.is_equal)
+            conv(b, [(i * lw + c0, i * lw + c1, 1, "MD", rS(nm, 16 * c0, 16 * c1))])
+        b, bl, b1 = wb(), wb(), wb()
+        valid(b, 1, 32, lw)
+        for i, nm in ((1, "rrow"), (0, "lrow")):
+            ts(A("ls16", 512 * i, 512 * i + 512), ind(A(nm, 0, P), A("snl%d" % t, 0, 32)), -1536, OP.add)
+            conv(bl, [(32 * i, 32 * i + 32, 1, "MD", rS("ls16", 512 * i, 512 * i + 512))])
+        valid(b, 0, 32, h)
+        for k in (1, 0):
+            ts(A(li, k * lw, k * lw + 32), A(bl, 32 * k, 32 * k + 32), 1536, OP.add)
+            ts(A(st, k * lw, k * lw + 32), A(bl, 32 * k, 32 * k + 32), 1536, OP.add)
+        ts(A("ixa", 0, 2 * lw), A(st, 0, 2 * lw), GH, OP.is_ge, -3072, OP.mult)
+        tt(A("ixb", 0, 2 * lw), A("ixa", 0, 2 * lw), A(st, 0, 2 * lw), OP.add)
+        ts(A("ixa", 0, 2 * lw), A("ixb", 0, 2 * lw), OWN, OP.add)
+        valid(b, 1, 0, 32)
+        valid(b, 0, 0, 32)
+        valid(b1, 0, h, lw)
+        legs(b, lw, 2 * lw)
+        legs(b, 0, h)
+        legs(b1, h, lw)
+
+    def ghost_bases():
+        for s in range(2):
+            recv(s, "b", "gbo", 16 * s, 16 * s + 16)
+        for s in range(2):
+            act(A("brow", GH + 256 * s, GH + 256 * s + 256),
+                ind(A("snt", 272 * s, 272 * s + 272), A("gbo", 16 * s, 16 * s + 16)))
+
+    def legs(b, lo, hi):
+        tt(A("ulf", lo, hi), A(b, lo, hi), A("ixa", lo, hi), OP.mult)
+        cp(A("ul", lo, hi), A("ulf", lo, hi))
+
+    held = {}
+
+    def turn(t):
+        P, nw = PP[t], NW[t]
+        b = wb()
+        conv(b, [(0, nw, 1, "MDf", rS("fr", 0, P))])
+        held["b"] = b
+
+    def pairs(t):
+        nw, lw = NW[t], LW[t]
+        st, B0 = "st%d" % t, 2 * LW[t]
+        b = held["b"]
+        ts(A("mB", 0, nw), A(st, B0, B0 + nw), GH, OP.is_lt, -88, OP.mult)
+        tt(A("mB2", 0, nw), A("meS", 0, nw), A(st, B0, B0 + nw), OP.is_lt)
+        tt(A("pe", 0, nw), A(b, 0, nw), A("meS", 0, nw), OP.is_equal)
+        tt(A("mB2", 0, nw), A("mB2", 0, nw), A("mB", 0, nw), OP.mult)
+        tt(A("mB", 0, nw), A("mB2", 0, nw), A("pe", 0, nw), OP.mult)
+        ts(A("thr", 0, nw), A("mB", 0, nw), 99, OP.add)
+
+    def flags_row(t, i):
+        P, nw, lw = PP[t], NW[t], LW[t]
+        o = i * lw + (32 if i < 2 else 0)
+        act(A("fr", 0, P), ind(A("rrow", 0, 3072), A("li%d" % t, o, o + nw)))
+        turn(t)
+
+    def flags_col(t, i):
+        nw, lw = NW[t], LW[t]
+        o = i * lw + (32 if i < 2 else 0)
+        b = held["b"]
+        tt(A("fl", nw * i, nw * i + nw), A(b, 0, nw), A("meS", 0, nw), OP.is_equal)
+        ts(A("pm2", nw * i, nw * i + nw), A("st%d" % t, o, o + nw), -GH, OP.add)
+
+    def flags_list(t):
+        nw, lw = NW[t], LW[t]
+        tt(A("lff", 0, 3 * nw), A("fl", 0, 3 * nw), A("pm2", 0, 3 * nw), OP.mult)
+        ts(A("lf", 0, 3 * nw), A("lff", 0, 3 * nw), GH, OP.add)
+        if t == 0:
+            tt(A("sna", 0, 32), A("st0", lw, lw + 32), A("slotc", 0, 32), OP.is_equal)
+            ts(A("snb", 0, 32), A("sn0", 0, 32), -GH, OP.add)
+            tt(A("snc", 0, 32), A("sna", 0, 32), A("snb", 0, 32), OP.mult)
+            ts(A("snf", 0, 32), A("snc", 0, 32), GH, OP.add)
+
+    def marks(u, lo, P, n):
+        nm = "in%d" % (n % 2)
+        for i in range(P // 512):
+            ts(A(nm, 512 * i, 512 * i + 512), A(u, lo + 512 * i, lo + 512 * i + 512), A("thf", 0, 1), OP.is_ge)
+            mm("p%d" % i, [(A("p%d" % i, 0, 512), A("eye", 0, 128), A(nm, 512 * i, 512 * i + 512), n == 0, n == 5)])
+
+    def depths(t, slack):
+        P, nw, lw = PP[t], NW[t], LW[t]
+        for n in range(5):
+            u = "U%d" % n
+            gr = "gr%d" % (n % 2)
+            win = A(u, 0, OWN + P)
+            marks(u, OWN, P, n)
+            for s in range(2):
+                recv(s, str(n), u, 16 + 256 * s, 16 + 256 * s + 256)
+            if n < 4:
+                for s in order:
+                    c = lw + 16 * s
+                    act(A(gr, 256 * s, 256 * s + 256), ind(win, A("ul", c, c + 16)))
+                for s in order:
+                    o = A("sb%d" % (n + 1), 256 * s, 256 * s + 256)
+                    tt(o, ind(win, A("ul", 16 * s, 16 * s + 16)), A(gr, 256 * s, 256 * s + 256), OP.max)
+                    send(s, str(n + 1), o, "U%d" % (n + 1), 16 + 256 * (1 - s), 16 + 256 * (1 - s) + 256)
+            H = P // 2
+            h16 = H // 16
+            for h in range(2):
+                c = lw + 32 + h16 * h
+                act(A(gr, 512 + H * h, 512 + H * h + H), ind(win, A("ul", c, c + h16)))
+            for h in range(2):
+                o = A("U%d" % (n + 1), OWN + H * h, OWN + H * h + H) if n < 4 else A("u5", H * h, H * h + H)
+                c = 32 + h16 * h
+                tt(o, ind(win, A("ul", c, c + h16)), A(gr, 512 + H * h, 512 + H * h + H), OP.max)
+            for f in slack.get(n, []):
+                f()
+        marks("u5", 0, P, 5)
+
+    def splits(t):
+        P, nw, nb = PP[t], NW[t], PP[t]
+        for k in range(2):
+            for i in range(P // 512):
+                o, x = A("in%d" % k, 512 * i, 512 * i + 512), A("p%d" % i, 0, 512)
+                if (i + k) % 2 == 0:
+                    act(o, x, AF.Sign)
+                else:
+                    ts(o, x, 0, OP.is_gt)
+        b = wb()
+        for c0, c1 in ((0, nw // 2), (nw // 2, nw)):
+            tt(A("gr1", 16 * c0, 16 * c1), ind(A("in0", 0, P), A("pl", c0, c1)), A("in1", 16 * c0, 16 * c1), OP.max)
+            conv(b, [(c0, c1, 1, "CQ", rS("gr1", 16 * c0, 16 * c1))])
+        tt(A("go", 0, nw), A(b, 0, nw), A("thr", 0, nw), OP.is_ge)
+        b = wb()
+        mm(b, [(A(b, nw, 2 * nw), A("blk", 0, 128), A("go", 0, nw), True, True),
+               (A(b, 0, nw), A("ltg", 0, 128), A("go", 0, nw), True, False),
+               (A(b, 0, nw), A("eye", 0, 128), A("me16", 0, nw), False, True)])
+        op("V", [lambda: g.vector.tensor_tensor_scan(X("sc", 0, nw), X(b, nw, 2 * nw), X("zer", 0, nw), 2048.0, OP.add, OP.add)],
+           [(b, 0, 512), ("zer", 0, nw)], [("sc", 0, nw)])
+        tt(A("ka", 0, nw), A("sc", 0, nw), A(b, 0, nw), OP.add)
+        tt(A("kc", 0, nw), A("ka", 0, nw), A("go", 0, nw), OP.mult)
+        tt(A("kd", 0, nw), A("kc", 0, nw), A("meS", 0, nw), OP.add)
+        cp(A("koff", 0, nw), A("kd", 0, nw))
+        scat(A("lrow", 0, 3072), A("koff", 0, nw), A("mex", 512, 512 + P))
+        ts((X("T16", 0, 512, 2), [("T16", 0, 512)]), A("lrow", 2048, 2304), -1536, OP.add)
+        b = wb()
+        conv(b, [(0, 16, 1, "MD", lambda q: (X("T16", 2 * q, 512, 32), [("T16", 0, 512)]))])
+        ts(A("tl", 0, 16), A(b, 0, 16), 1536, OP.add)
+        ts((X("T16", 1, 512, 2), [("T16", 0, 512)]), ind(A("brow", 0, nb + 512), A("tl", 0, 16)), -1536, OP.add)
+        b = wb()
+        conv(b, [(0, 32, 1, "MD", rS("T16", 0, 512))])
+        ts(A("TL", 0, 32), A(b, 0, 32), 1536, OP.add)
+        act(A("t32", 0, 32), A(b, 0, 32), AF.Identity, bias=1536.0)
+
+    def renames(t):
+        P, nw, nb = PP[t], NW[t], PP[t]
+        scat(A("NT", 0, nb + 512), A("TL", 0, 32), A("jrow", 0, 512))
+        act(A("eT", 0, 512), ind(A("U0", OWN, OWN + nb + 512), A("TL", 0, 32)))
+        win = A("NT", 0, 2576)
+        H = P // 2
+        act(A("vR", 0, P), ind(win, A("lf", nw, 2 * nw)))
+        act(A("vL", H, P), ind(win, A("lf", nw // 2, nw)))
+        act(A("e2", 0, 512), A("eT", 0, 512), AF.Identity, bias=128.75, scale=0.5)
+        act(A("e2b", 0, 512), A("e2", 0, 512), AF.Identity, bias=-258.0)
+        act(A("vy", 0, 512), ind(A("vR", 0, nb + 512), A("TL", 0, 32)))
+        cp(A("vB", 0, P), ind(win, A("lf", 2 * nw, 3 * nw)))
+        cp(A("vL", 0, H), ind(win, A("lf", 0, nw // 2)))
+        if t == 0:
+            cp(A("vs", 0, 512), ind(win, A("snf", 0, 32)))
+        ts(A("Y16", 0, 512), ind(A("rrow", 0, nb + 512), A("TL", 0, 32)), -1536, OP.add)
+
+    def update(t, lay):
+        P, nw, nb = PP[t], NW[t], PP[t]
+        k0 = nb - 1.5
+        if lay == "S":
+            a, c, ic = "st%d" % t, "st%d" % (t + 1), LW[t + 1]
+            src = (32, LW[t] + 32, 2 * LW[t])
+            dst = (32, ic + 32, 2 * ic)
+        else:
+            a, c, ic = "ns%d" % t, "ns%d" % (t + 1), nw + 32
+            src = (0, nw, 2 * nw)
+            dst = (0, ic, 2 * ic)
+
+        def places(n, lo):
+            if lay == "S":
+                return [(lo, lo + nw, 1, "MD", rS(n, 0, P))]
+            r = [(lo, lo + 96, 1, "MD", lambda q: (X(n, 96 * q, 96 * q + 96), [(n, 0, P)]))]
+            if P > V0:
+                r.append((lo + 96, lo + 128, 1, "MD", lambda q: (X(n, V0 + 32 * q, V0 + 32 * q + 32), [(n, 0, P)])))
+            return r
+
+        def new(n, lo, swap):
+            if lay == "S":
+                return [(lo, lo + 32, 1, "MD", lambda q: (X(n, q ^ swap, 512, 16), [(n, 0, 512)]))]
+            if not swap:
+                return [(lo, lo + 32, 1, "MD", lambda q: (X(n, 32 * q, 32 * q + 32), [(n, 0, 512)]))]
+            return [(lo + e, lo + 32, 2, "MD", lambda q, e=e: (X(n, 32 * q + 1 - e, 32 * q + 32, 2), [(n, 0, 512)])) for e in range(2)]
+        for i in range(3):
+            act(A("pt", nw * i, nw * i + nw), A(a, src[i], src[i] + nw), AF.Identity, bias=-k0)
+        b = wb()
+        for n, lo in (("NT", 3 * nw), ("vB", 2 * nw), ("vR", nw), ("vL", 0)):
+            conv(b, places(n, lo))
+        b3, b2 = wb(), wb()
+        conv(b2, new("T16", 0, 0) + new("T16", 32, 1) + new("Y16", 64, 0) + new("vy", 96, 0))
+        yield
+        act(A(b3, 0, 4 * nw), A(b, 0, 4 * nw), AF.Abs, bias=cb[0], scale=2.0)
+        ts(A("z", 0, 4 * nw), A(b, 0, 4 * nw), 0, OP.is_equal, -8192, OP.mult)
+        tt(A("q3", 0, 3 * nw), A(b3, 0, 3 * nw), A("z", 0, 3 * nw), OP.add)
+        ts(A("ysn", 0, nw), A(b3, 3 * nw, 4 * nw), k0, OP.add)
+        act(A(b3, 0, nw), A(b, 3 * nw, 4 * nw), AF.Abs, bias=cb[1], scale=2.0)
+        tt(A("q3", 0, 3 * nw), A("q3", 0, 3 * nw), A("pt", 0, 3 * nw), OP.max)
+        ts(A("q3u", 0, 3 * nw), A("q3", 0, 3 * nw), k0, OP.add)
+        yield
+        ts(A("sp", 0, nw), A("z", 3 * nw, 4 * nw), 0, OP.is_equal)
+        ts(A("nsp", 0, nw), A("z", 3 * nw, 4 * nw), 0, OP.is_lt)
+        ts(A("ysn", nw, 2 * nw), A(b3, 0, nw), k0, OP.add)
+        for i in range(2):
+            tt(A("yss", nw * i, nw * i + nw), A("ysn", nw * i, nw * i + nw), A("sp", 0, nw), OP.mult)
+        tt(A("oc", 0, nw), A("q3u", 2 * nw, 3 * nw), A("nsp", 0, nw), OP.mult)
+        tt(A("od", 0, nw), A("q3u", 0, nw), A("sp", 0, nw), OP.mult)
+        tt(A(c, dst[2], dst[2] + nw), A("oc", 0, nw), A("od", 0, nw), OP.add)
+        o = nw
+        act(A(b3, 256, 288), A(b2, 96, 128), AF.Abs, bias=cb[0], scale=2.0)
+        act(A("yt", 0, 32), A(b2, 64, 96), AF.Identity, bias=1536 - k0)
+        act(A(c, dst[1] + o, dst[1] + o + 32), A(b2, 0, 32), AF.Identity, bias=1536.0)
+        act(A("tsw", 0, 32), A(b2, 32, 64), AF.Identity, bias=1536.0)
+        ts(A("zy", 0, 32), A(b2, 96, 128), 0, OP.is_equal, -8192, OP.mult)
+        tt(A("yzy", 0, 32), A(b3, 256, 288), A("zy", 0, 32), OP.add)
+        tt(A("td", 0, 32), A("yzy", 0, 32), A("yt", 0, 32), OP.max)
+        ts(A(c, dst[2] + o, dst[2] + o + 32), A("td", 0, 32), k0, OP.add)
+        yield
+        tt(A("oa", 0, nw), A("q3u", 0, nw), A("nsp", 0, nw), OP.mult)
+        tt(A(c, dst[0], dst[0] + nw), A("oa", 0, nw), A("yss", 0, nw), OP.add)
+        tt(A("ob", 0, nw), A("q3u", nw, 2 * nw), A("nsp", 0, nw), OP.mult)
+        tt(A(c, dst[1], dst[1] + nw), A("ob", 0, nw), A("yss", nw, 2 * nw), OP.add)
+        tr = A(c, dst[1] + o, dst[1] + o + 32)
+        ts(A("tab", 0, 32), tr, nb, OP.is_ge)
+        tt(A("td", 0, 32), tr, A("tsw", 0, 32), OP.subtract)
+        tt(A("yu", 0, 32), A("td", 0, 32), A("tab", 0, 32), OP.mult)
+        tt(A(c, dst[0] + o, dst[0] + o + 32), A("tsw", 0, 32), A("yu", 0, 32), OP.add)
+        yield
+
+    def srow(x, lo, ncol, row, both):
+        for i in range(ncol // 32):
+            b = wb()
+            mm(b, [(A(b, q, 512, 16), A("EQ", 128 * q, 128 * q + 128), A(x, lo + 32 * i, lo + 32 * i + 32), True, True) for q in range(16)])
+            o = A(row, 512 * i, 512 * i + 512)
+            if both and i % 2:
+                ts(o, A(b, 0, 512), 1536, OP.add)
+            else:
+                act(o, A(b, 0, 512), AF.Identity, bias=1536.0)
+
+    def new_snd():
+        b = wb()
+        conv(b, [(0, 32, 1, "MD", rS("vs", 0, 512))])
+        act(A("sna", 0, 32), A(b, 0, 32), AF.Abs, bias=cb[0], scale=2.0)
+        ts(A("snv", 0, 32), A(b, 0, 32), 0, OP.is_equal, -8192, OP.mult)
+        tt(A("snb", 0, 32), A("sna", 0, 32), A("snv", 0, 32), OP.add)
+        ts(A("snc", 0, 32), A("snb", 0, 32), V0 - 1.5, OP.add)
+        tt(A("sn1", 0, 32), A("snc", 0, 32), A("sn0", 0, 32), OP.max)
+        cp(A("snl1", 0, 32), A("sn1", 0, 32))
+        ts(A("sn16", 0, 32), A("sn1", 0, 32), -1536, OP.add)
+
+    def weigh(t):
+        nb = PP[t]
+        b = wb()
+        conv(b, [(0, 32, 1, "WQ", rS("eT", 0, 512))])
+        tt(A("hz", 0, 32), A(b, 0, 32), A("t32", 0, 32), OP.add)
+        tt(A("hz", 32, 64), A(b, 0, 32), A("meS", nb // 16, nb // 16 + 32), OP.add)
+
+    def children(t):
+        nb = PP[t]
+        ts(A("hz2", 0, 64), A("hz", 0, 64), 2047, OP.bitwise_and)
+        ts(A("hq", 0, 64), A("hz2", 0, 64), -2048, OP.add)
+        for i in range(2):
+            ts(A("pres", 32 * i, 32 * i + 32), A("t32", 0, 32), nb, OP.is_lt)
+        tt(A("hm", 0, 64), A("hq", 0, 64), A("pres", 0, 64), OP.mult)
+        ts(A("eo", 0, 64), A("hm", 0, 64), 2048, OP.add)
+        tt(A("cT", 0, 512), ind(A("dtb", 0, 2064), A("eo", 0, 32)), A("e2b", 0, 512), OP.add)
+        scat(A("U0", OWN, OWN + nb + 512), A("TL", 0, 32), A("cT", 0, 512))
+        tt(A("U0", OWN + nb, OWN + nb + 512), ind(A("dtb", 0, 2064), A("eo", 32, 64)), A("e2b", 0, 512), OP.add)
+
+    ms(A("rrow", GH, 3088), -1.0)
+    iota(A("rrow", V0, GH), [[1, 1024]], V0, 0)
+    iota(A("jq", 0, 256), [[1, 256]], 1, 0)
+    sel(A("tri", 0, 128), A("blk", 0, 128), [[-1, 128]], OP.is_ge, 0, 1)
+    iota(A("U0", OWN + V0, OWN + GH), [[0, 1024]], 0, 0)
+
+    def sentinels(t):
+        iota(A("lrow", 2048, 2304), [[2, 256]], PP[t], 0)
+
+    def late0():
+        for q in range(16):
+            act(A("MDf", 128 * q, 128 * q + 128), A("eye", 0, 128), AF.Copy, scale=A("pq", q, q + 1))
+        ts(A("ltg", 0, 128), A("tri", 0, 128), -1, OP.mult)
+        ts(A("me16", 0, 128), A("meS", 0, 128), -1, OP.mult)
+        ms(A("zer", 0, 128), 0.0)
+        cp((X("jrow", 0, 512, 2), [("jrow", 0, 512)]), A("jq", 0, 256))
+        ts((X("jrow", 1, 512, 2), [("jrow", 0, 512)]), A("jq", 0, 256), -1, OP.mult)
+
+    def masks2():
+        for i in range(4):
+            b = wb()
+            mm(b, [(A(b, 0, 512), A("blk", 0, 128), A("MD", 512 * i, 512 * i + 512), True, True)])
+            act(A("CQ", 512 * i, 512 * i + 512), A(b, 0, 512))
+            act(A("WQ", 512 * i, 512 * i + 512), A(b, 0, 512), AF.Copy, scale=A("wtf", 0, 1))
+
+    def late1():
+        act(A("dtb", 0, 2048), A("dtb", 0, 2048), AF.Identity, bias=128.75, scale=0.5)
+        ms(A("dtb", 2048, 2064), 129.0)
+        cp(A("ns0", 0, 288), A("nraw", 0, 288))
+
+    def late2(t):
+        iota(A("NT", 0, 2576), [[0, 2576]], 0, 0)
+        iota(A("vR", PP[t], PP[t] + 512), [[0, 512]], 0, 0)
+
+    ghost_bases()
+    prep(0)
+    depths(0, {0: [late0, lambda: turn(0), lambda: sentinels(0)], 1: [lambda: pairs(0), lambda: flags_row(0, 0)],
+               2: [lambda: flags_col(0, 0), lambda: flags_row(0, 1)],
+               3: [lambda: flags_col(0, 1), lambda: flags_row(0, 2), lambda: late2(0)],
+               4: [late1, lambda: flags_col(0, 2), lambda: flags_list(0)]})
+    splits(0)
+    renames(0)
+    for _ in update(0, "S"):
+        pass
+    new_snd()
+    lw, nw = LW[1], NW[1]
+    ts(A("x16", 256, 384), A("st1", 2 * lw, 2 * lw + nw), -1536, OP.add)
+    srow("x16", 256, 128, "brow", True)
+    srow("sn16", 0, 32, "mex", False)
+    sndtab()
+    base_send(1, 2048)
+    for i in (1, 0):
+        ts(A("x16", 128 * i, 128 * i + 128), A("st1", lw * i + 32, lw * i + 32 + nw), -1536, OP.add)
+    weigh(0)
+    srow("x16", 128, 128, "rrow", False)
+    ghost_bases()
+    srow("x16", 0, 128, "lrow", False)
+    children(0)
+    ghost0(1, 2048)
+    for i in range(3):
+        o = lw * i + (32 if i < 2 else 0)
+        cp(A("li1", o, o + nw), A("st1", o, o + nw))
+    prep(1)
+    un = update(0, "N")
+    next(un)
+    depths(1, {0: [lambda: turn(1), lambda: sentinels(1), lambda: next(un)], 1: [lambda: pairs(1), lambda: flags_row(1, 0)],
+               2: [lambda: flags_col(1, 0), lambda: next(un), lambda: flags_row(1, 1)],
+               3: [lambda: flags_col(1, 1), lambda: next(un), lambda: flags_row(1, 2), lambda: late2(1)],
+               4: [lambda: flags_col(1, 2), lambda: flags_list(1)]})
+    splits(1)
+    renames(1)
+    weigh(1)
+    children(1)
+    dma("Y", (HB("ye"), []), A("U0", OWN, OWN + GH))
+    for _ in update(1, "N"):
+        pass
+    for i, n in ((2, "yb"), (0, "yl"), (1, "yr")):
+        for j, (lo, hi, c0, c1) in enumerate(((0, 1536, 0, 96), (1536, 2048, 96, 128), (2048, 2560, 128, 160))):
+            dma("SYS"[j], (T[n][:, lo:hi], []), A("ns2", 160 * i + c0, 160 * i + c1))
+    wait_for("Y", {s: v for s, v in cnt.items()})

@@ -6,7 +6,8 @@ AF = ActivationFunctionType
 NR = 4
 V0 = 1536
 GH = 2560
-OWN = 528
+US = 3088
+BIG = 4096.0
 
 SCRATCH = {}
 PK = {}
@@ -20,29 +21,27 @@ def _pack(big, dtype, parts):
     SCRATCH[big] = ("sbuf", [128, o], dtype)
 
 
-_pack("kf", "float32", (("pq", 16), ("meS", 160), ("slotc", 32), ("zer", 128), ("thf", 1), ("wtf", 1), ("ab", 2),
-                        ("st0", 352), ("st1", 448), ("ns0", 288), ("ns1", 384), ("ns2", 480), ("sn0", 32), ("sn1", 32),
-                        ("ixa", 320), ("ixb", 320), ("ulf", 320), ("mB", 128), ("mB2", 128), ("pe", 128), ("thr", 128),
-                        ("xo", 32), ("xz", 32), ("xo2", 32), ("sc", 128), ("ka", 128), ("kc", 128), ("kd", 128),
-                        ("pm2", 384), ("fl", 384), ("lff", 384), ("t32", 32), ("z", 512), ("pt", 384), ("q3", 384),
-                        ("q3u", 384), ("sp", 128), ("nsp", 128), ("ysn", 256), ("yss", 256), ("oa", 128), ("ob", 128),
-                        ("oc", 128), ("od", 128), ("tsw", 32), ("tab", 32), ("td", 32), ("zy", 32), ("yzy", 32), ("yt", 32),
-                        ("yu", 32), ("snv", 32), ("sna", 32), ("snb", 32), ("snc", 32), ("hq", 64), ("hm", 64), ("pres", 64)))
-_pack("ki", "int32", (("nraw", 288), ("nsn", 32), ("thi", 1), ("wti", 1), ("ik", 16), ("ik2", 16), ("pmi", 160), ("pmod", 160),
-                      ("c16", 160), ("hz", 64), ("hz2", 64)))
-_pack("ku", "uint16", (("li0", 352), ("li1", 448), ("snl0", 32), ("snl1", 32), ("gbo", 32), ("bo", 32), ("ul", 320), ("pl", 128),
-                       ("koff", 128), ("tl", 16), ("TL", 32), ("lf", 384), ("snf", 32), ("eo", 64)))
-_pack("kh", "float16", (("n16", 288), ("nsn16", 32), ("ra", 1536), ("rb", 1536), ("rc", 1536), ("bs16", 512), ("ls16", 1024),
-                        ("T16", 512), ("Y16", 512), ("x16", 384), ("sn16", 32), ("me16", 128)))
-_pack("kb", "bfloat16", (("ones", 128), ("eye", 128), ("blk", 128), ("blka", 128), ("tri", 128), ("ltg", 128), ("jq", 256),
-                         ("jrow", 512), ("go", 128), ("eT", 512), ("e2", 512), ("e2b", 512), ("cT", 512), ("vs", 512), ("vy", 512),
+MASKS = ("zl", "zr", "zb", "zm", "s0", "s1", "s2", "s3", "za", "cq")
+_pack("km", "bfloat16", [(n, 144) for n in MASKS])
+_pack("kf", "float32", (("pq", 16), ("qf", 1), ("qn", 1), ("meS", 160), ("zer", 128), ("thf", 1), ("thb", 1), ("wtf", 1), ("bq", 2), ("jb", 4),
+                        ("n3", 1), ("f1", 144), ("f2", 144), ("f3", 144), ("sn0", 32), ("sn1", 32), ("old", 480), ("val", 256), ("m4k", 256),
+                        ("sc", 512), ("t32", 32), ("lrb", 480), ("nsp", 320), ("ua", 320), ("ub", 160), ("uc", 160), ("new", 480),
+                        ("big", 32), ("hb", 32), ("gf", 512), ("c160", 160), ("c16", 160), ("snt", 560)))
+_pack("ki", "int32", (("thi", 1), ("wti", 1), ("ik", 16), ("ik2", 16), ("pi", 1), ("qi", 1), ("mi", 16), ("mi2", 16), ("ti", 32), ("ti2", 32),
+                      ("hz", 64), ("hz2", 64)))
+_pack("ku", "uint16", (("li", 448), ("snl", 32), ("gbo", 32), ("bo", 32), ("ul", 320), ("pl", 128), ("off", 8), ("TL", 32), ("lf", 384),
+                       ("snf", 32), ("eo", 64)))
+_pack("kh", "float16", (("meN", 160), ("sn16", 512), ("gs", 512), ("st", 448), ("snS", 32), ("slc", 32), ("me16", 128), ("d16", 8),
+                        ("inc", 144), ("y16", 512), ("n16", 384)))
+_pack("kb", "bfloat16", (("ones", 128), ("eye", 128), ("blk", 128), ("blka", 128), ("tri", 128), ("lt", 128), ("n64", 128), ("n4k", 128),
+                         ("ts0", 128), ("tsel", 128), ("s1k", 144), ("s2k", 144), ("wn", 144), ("wq", 144), ("ncq", 144), ("mem", 384),
+                         ("kq", 256), ("jr", 512), ("go", 128), ("pen", 384), ("ee", 8), ("eT", 512), ("e2", 512), ("e2b", 512),
+                         ("cT", 512), ("vs", 512), ("vy", 512), ("fs", 1024),
                          ("sb0", 512), ("sb1", 512), ("sb2", 512), ("sb3", 512), ("sb4", 512)))
-for _n, _c, _d in (("brow", 3088, "float32"), ("lrow", 3088, "float32"), ("rrow", 3088, "float32"), ("mex", 2560, "float32"),
-                   ("snt", 544, "float32"), ("fr", 2048, "float32"), ("MDf", 2048, "float32"),
-                   ("MD", 2048, "bfloat16"), ("EQ", 2048, "bfloat16"), ("CQ", 2048, "bfloat16"), ("WQ", 2048, "bfloat16"),
-                   ("dtb", 2064, "bfloat16"), ("NT", 2576, "bfloat16"), ("vL", 2048, "bfloat16"), ("vR", 2560, "bfloat16"),
-                   ("vB", 2048, "bfloat16"), ("U0", OWN + 2560, "bfloat16"), ("U1", OWN + 2048, "bfloat16"),
-                   ("U2", OWN + 2048, "bfloat16"), ("U3", OWN + 2048, "bfloat16"), ("U4", OWN + 2048, "bfloat16"),
+for _n, _c, _d in (("raw", V0, "int32"), ("rsn", 512, "int32"), ("r16", 2560, "float16"), ("TB", 3072, "float32"),
+                   ("Z0", 3072, "float32"), ("Z1", 3072, "float32"), ("UU", 5 * US + 16, "bfloat16"),
+                   ("dtb", 2064, "bfloat16"), ("NT", 2592, "bfloat16"), ("vL", 2048, "bfloat16"), ("vR", 2560, "bfloat16"),
+                   ("vB", 2048, "bfloat16"), ("dL", 2048, "bfloat16"), ("dR", 2048, "bfloat16"), ("dB", 2048, "bfloat16"),
                    ("u5", 2048, "bfloat16"), ("gr0", 2560, "bfloat16"), ("gr1", 2560, "bfloat16"), ("in0", 2048, "bfloat16"),
                    ("in1", 2048, "bfloat16")):
     SCRATCH[_n] = ("sbuf", [128, _c], _d)
@@ -50,7 +49,7 @@ for _n in range(8):
     SCRATCH["p%d" % _n] = ("psum", [128, 512], "float32")
 
 KINDS = ["b", "0", "1", "2", "3", "4"]
-SEMAPHORES = (["cv", "cs", "cp", "cg"] + ["d%d" % i for i in range(24)]
+SEMAPHORES = (["cv", "cs", "cp", "cg"] + ["d%d" % i for i in range(32)]
               + ["r%s%d" % (k, s) for k in KINDS for s in range(2)] + ["l%s%d" % (k, s) for k in KINDS for s in range(2)])
 
 
@@ -130,15 +129,21 @@ def rank_program(g, core, T, topo):
         cnt[s] = 16
         note(q, in_[1], out[1], s, 16)
 
-    def X(n, lo, hi, st=1):
+    def X(n, lo, hi, st=1, p0=0, p1=128):
         if n in PK:
             t, o = T[PK[n][0]], PK[n][1]
         else:
             t, o = T[n], 0
-        return t[:, o + lo:o + hi] if st == 1 else t[:, o + lo:o + hi:st]
+        return t[p0:p1, o + lo:o + hi] if st == 1 else t[p0:p1, o + lo:o + hi:st]
 
     def A(n, lo, hi, st=1):
         return (X(n, lo, hi, st), [(n, lo, hi)])
+
+    def R(n, k0, k1, lo, hi, st=1):
+        return (X(n, lo, hi, st, 8 * k0, 8 * k1), [("%s:%d" % (n, k), lo, hi) for k in range(k0, k1)])
+
+    def U(n, lo, hi):
+        return A("UU", US * n + lo, US * n + hi)
 
     def ind(w, o):
         return (w[0].indirect(o[0]), w[1] + o[1])
@@ -148,20 +153,25 @@ def rank_program(g, core, T, topo):
 
     def ts(out, a, s1, f1, s2=None, f2=None):
         r = list(a[1])
-        v1 = s1
-        if isinstance(s1, tuple):
-            r += s1[1]
-            v1 = s1[0]
+        v = []
+        for s in (s1, s2):
+            if isinstance(s, tuple):
+                r += s[1]
+                s = s[0]
+            v.append(s)
         if f2 is None:
-            op("V", [lambda: g.vector.tensor_scalar(out[0], a[0], v1, None, f1)], r, out[1])
+            op("V", [lambda: g.vector.tensor_scalar(out[0], a[0], v[0], None, f1)], r, out[1])
         else:
-            op("V", [lambda: g.vector.tensor_scalar(out[0], a[0], v1, s2, f1, f2)], r, out[1])
+            op("V", [lambda: g.vector.tensor_scalar(out[0], a[0], v[0], v[1], f1, f2)], r, out[1])
 
     def cp(out, a):
         op("V", [lambda: g.vector.tensor_copy(out[0], a[0])], a[1], out[1])
 
     def scat(w, o, a):
         op("V", [lambda: g.vector.tensor_copy(w[0].indirect(o[0]), a[0])], a[1] + o[1], w[1])
+
+    def scan(out, a, b, f0, f1):
+        op("V", [lambda: g.vector.tensor_tensor_scan(out[0], a[0], b[0], 0.0, f0, f1)], a[1] + b[1], out[1])
 
     def ms(out, v):
         op("V", [lambda: g.vector.memset(out[0], v)], [], out[1])
@@ -178,529 +188,502 @@ def rank_program(g, core, T, topo):
             bi = bias[0]
         op("S", [lambda: g.scalar.activation(out[0], a[0], f, bias=bi, scale=sc)], r, out[1])
 
+    def add(q, out, a, v):
+        if q == "S":
+            act(out, a, AF.Identity, bias=float(v))
+        else:
+            ts(out, a, v, OP.add)
+
     def iota(out, pattern, base, cm, small=True):
         if small:
             op("G", [lambda: g.iota(out[0], pattern, base, cm, allow_small_or_imprecise_dtypes=True)], [], out[1])
         else:
             op("G", [lambda: g.iota(out[0], pattern, base, cm)], [], out[1])
 
+    def fill(n, lo, hi, v=0):
+        iota(A(n, lo, hi), [[0, hi - lo]], v, 0)
+
     def sel(out, a, pattern, cmp, base, cm):
         op("G", [lambda: g.affine_select(out[0], a[0], pattern, cmp, 0.0, base, cm)], a[1], out[1])
-
-    bank = [4]
-
-    def wb():
-        b = bank[0]
-        bank[0] = 4 + (b - 3) % 4
-        return "p%d" % b
 
     def mm(b, jobs):
         fns, rd = [], []
         for o, l, r, s0, s1 in jobs:
             fns.append(lambda o=o, l=l, r=r, s0=s0, s1=s1: g.tensor.matmul(o[0], l[0], r[0], s0, s1))
-            for x in (l, r):
-                if x[1][0] not in rd:
-                    rd.append(x[1][0])
+            for x in l[1] + r[1]:
+                if x not in rd:
+                    rd.append(x)
         op("P", fns, rd, [(b, 0, 512)])
 
-    def conv(b, jobs):
+    def M(m, q, k=128):
+        return (X(m, 16 - q, 144 - q, 1, 0, k), [(m, 0, 144)])
+
+    def one(b, lo, hi, m, x, s0=True, s1=True):
+        mm(b, [(A(b, lo, hi), A(m, 0, 128), x, s0, s1)])
+
+    def toS(b, lo, m, n, c0, c1, s0=True, s1=True, k=None):
         js = []
-        for lo, hi, st, m, rh in jobs:
-            for q in range(16):
-                js.append((A(b, lo, hi, st), A(m, 128 * q, 128 * q + 128), rh(q), q == 0, q == 15))
+        for q in range(16):
+            x = (X(n, c0 + q, c1, 16), [(n, c0, c1)]) if k is None else R(n, 0, k, c0 + q, c1, 16)
+            js.append((A(b, lo, lo + (c1 - c0) // 16), M(m, q, 128 if k is None else 8 * k), x, s0 and q == 0, s1 and q == 15))
         mm(b, js)
 
-    def rS(n, lo, hi):
-        return lambda q: (X(n, lo + q, hi, 16), [(n, lo, hi)])
+    def toN(b, lo, w, m, n, c0, x0, x1, s0=True, s1=True, k=None):
+        ps = [(q, max(x0, w * q), min(x1, w * q + w)) for q in range(16)]
+        ps = sorted([p for p in ps if p[1] < p[2]], key=lambda p: p[1] - p[2])
+        js = []
+        for i, (q, a, z) in enumerate(ps):
+            x = A(n, c0 + a - x0, c0 + z - x0) if k is None else R(n, 0, k, c0 + a - x0, c0 + z - x0)
+            js.append((A(b, lo + a - w * q, lo + z - w * q), M(m, q, 128 if k is None else 8 * k), x, s0 and i == 0, s1 and i == len(ps) - 1))
+        mm(b, js)
 
     def chosen(src, dst):
         return topo.engines(src, dst)[-8:]
 
-    def send(s, kind, src, dst, lo, hi):
+    def send(s, kind, src, dst):
         d = nb_core[s]
         wait_for("G", needs("G", src[1], []))
         rid, pid = topo.addr(d, core)
         es = chosen(core, d)
         ls = "l%s%d" % (kind, s)
-        g.remote_dma(X(dst, lo, hi), src[0], T.sem["r%s%d" % (kind, 1 - s)], T.sem[ls], pid, rid, sum(1 << e for e in es))
+        g.remote_dma(dst[0], src[0], T.sem["r%s%d" % (kind, 1 - s)], T.sem[ls], pid, rid, sum(1 << e for e in es))
         cnt[ls] = cnt.get(ls, 0) + len(es)
         note("G", src[1], [], ls, cnt[ls])
 
-    def recv(s, kind, dst, lo, hi):
+    def recv(s, kind, dst):
         rs = "r%s%d" % (kind, s)
         cnt[rs] = cnt.get(rs, 0) + len(chosen(nb_core[s], core))
-        note(None, [], [(dst, lo, hi)], rs, cnt[rs])
+        note(None, [], dst[1], rs, cnt[rs])
+
+    def ghosts(n, s):
+        return U(n, 16 + GH + 256 * s, 16 + GH + 256 * s + 256)
 
     def HB(n):
-        return T[n][:]
+        return (T[n][:], [])
 
-    PP, NW, LW = (V0, 2048), (96, 128), (128, 160)
+    PP, NW, WN = (V0, 2048), (96, 128), (128, 160)
 
-    dma("Y", A("nsn", 0, 32), (HB("snd"), []))
-    dma("S", A("nraw", 192, 288), (HB("bs"), []))
-    dma("Y", A("nraw", 96, 192), (HB("rt"), []))
-    dma("S", A("nraw", 0, 96), (HB("lt"), []))
-    dma("Y", A("U0", OWN, OWN + V0), (HB("err"), []))
-    dma("S", A("thi", 0, 1), (HB("th"), []))
-    dma("S", A("wti", 0, 1), (HB("wt"), []))
-    dma("Y", A("dtb", 0, 2048), (HB("det"), []))
+    def L(t, i):
+        return i * (NW[t] + 32) + (32 if i < 2 else 0)
+
+    dma("Y", R("rsn", 0, 1, 0, 512), HB("snd"))
+    for i, (q, n) in enumerate((("S", "lt"), ("Y", "rt"), ("S", "bs"))):
+        dma(q, R("raw", i, i + 1, 0, V0), HB(n))
+    dma("Y", U(0, 16, 16 + V0), HB("err"))
+    dma("S", A("thi", 0, 1), HB("th"))
+    dma("S", A("wti", 0, 1), HB("wt"))
 
     ms(A("ones", 0, 128), 1.0)
-    iota(A("ik", 0, 16), [[-1, 16]], 16, 1, False)
-    sel(A("blka", 0, 128), A("ones", 0, 128), [[-16, 8], [0, 16]], OP.is_ge, 0, 1)
-    sel(A("blk", 0, 128), A("blka", 0, 128), [[16, 8], [0, 16]], OP.is_ge, 15, -1)
+    op("V", [lambda: g.vector.memset(T["km"][:], 0.0)], [], [(n, 0, 144) for n in MASKS])
+    iota(A("pi", 0, 1), [[0, 1]], 0, 1, False)
+    iota(A("c160", 0, 160), [[1, 160]], 0, 0)
+    for a, n in enumerate(("zl", "zr", "zb", "zm")):
+        sel((X(n, 0, 144, 16), [(n, 0, 144)]), A("ones", 0, 9), [[-1, 9]], OP.is_equal, 1 - 8 * a, 1)
+    ts(A("qi", 0, 1), A("pi", 0, 1), 15, OP.bitwise_and)
+    cp(A("qf", 0, 1), A("qi", 0, 1))
+    ts(A("qn", 0, 1), A("qi", 0, 1), 160, OP.mult, -1536, OP.add)
+    ts(A("meN", 0, 160), A("c160", 0, 160), A("qn", 0, 1), OP.add)
+    dma("Y", R("r16", 3, 4, 0, 2560), A("meN", 0, 160))
+    dma("Y", A("dtb", 0, 2048), HB("det"))
+    for a in (2, 0, 1, 3):
+        n = "s%d" % a
+        sel((X(n, 16, 144, 16), [(n, 0, 144)]), A("ones", 0, 8), [[-16, 8]], OP.is_equal, -a, 1)
     sel(A("eye", 0, 128), A("ones", 0, 128), [[-1, 128]], OP.is_equal, 0, 1)
-    iota(A("pmi", 0, 160), [[0, 160]], 0, 1, False)
-    iota(A("c16", 0, 160), [[16, 160]], 0, 0, False)
-    iota(A("brow", V0, GH), [[2, 512], [-1, 2]], V0 + 1, 0)
-    iota(A("mex", 512, 2560), [[1, 2048]], 0, 0)
-    ts(A("ik2", 0, 16), A("ik", 0, 16), 15, OP.bitwise_and)
-    ts(A("pq", 0, 16), A("ik2", 0, 16), 0, OP.is_equal)
-    for q in range(16):
-        ts(A("EQ", 128 * q, 128 * q + 128), A("blk", 0, 128), A("pq", q, q + 1), OP.mult)
-        act(A("MD", 128 * q, 128 * q + 128), A("eye", 0, 128), AF.Copy, scale=A("pq", q, q + 1))
-    ts(A("nsn16", 0, 32), A("nsn", 0, 32), -1536, OP.add)
-    ts(A("n16", 192, 288), A("nraw", 192, 288), -1536, OP.add)
-    ts(A("n16", 0, 192), A("nraw", 0, 192), -1536, OP.add)
+    tt(A("ts0", 0, 128), A("zl", 16, 144), A("zr", 15, 143), OP.add)
+    tt(A("tsel", 0, 128), A("zb", 14, 142), A("zm", 13, 141), OP.add)
+    tt(A("tsel", 0, 128), A("tsel", 0, 128), A("ts0", 0, 128), OP.add)
+    for n in range(6):
+        ms(A("UU", US * n, US * n + 16), 0.0)
+    for lo in (0, 272, 544):
+        ms(A("snt", lo, lo + 16), -1.0)
+    ts(A("meS", 0, 160), A("c160", 0, 160), 16, OP.mult, A("qf", 0, 1), OP.add)
+    ms(U(0, 16 + V0, 16 + GH), 0.0)
 
-    def nrow(x, lo, row, r16):
-        for i in range(4):
-            b = wb()
-            k = min(5, 16 - 5 * i)
-            mm(b, [(A(b, 96 * j, 96 * j + 96), A("EQ", 128 * (5 * i + j), 128 * (5 * i + j) + 128), A(x, lo, lo + 96), True, True)
-                   for j in range(k)])
-            act(A(row, 480 * i, 480 * i + 96 * k), A(b, 0, 96 * k), AF.Identity, bias=1536.0)
-            cp(A(r16, 480 * i, 480 * i + 96 * k), A(b, 0, 96 * k))
+    ts(R("sn16", 0, 1, 0, 512), R("rsn", 0, 1, 0, 512), -1536, OP.add)
+    toS("p4", 0, "zl", "sn16", 0, 512, k=1)
+    mm("p5", [(A("p5", 0, 512), M("zl", 2, 8), R("sn16", 0, 1, 0, 512), True, True)])
+    ts(A("snl", 0, 32), A("p4", 0, 32), 1536, OP.add)
 
-    b = wb()
-    mm(b, [(A(b, 32 * q, 32 * q + 32), A("EQ", 128 * q, 128 * q + 128), A("nsn16", 0, 32), True, True) for q in range(16)])
-    cp(A("bs16", 0, 512), A(b, 0, 512))
-    sb = b
-    b = wb()
-    conv(b, [(0, 32, 1, "MD", rS("bs16", 0, 512))])
-    ts(A("snl0", 0, 32), A(b, 0, 32), 1536, OP.add)
-    ts(A("sn0", 0, 32), A(b, 0, 32), 1536, OP.add)
-    act(A("mex", 0, 512), A(sb, 0, 512), AF.Identity, bias=1536.0)
+    def ghost0(qs):
+        for q, s in zip(qs, order):
+            add(q, A("sb0", 256 * s, 256 * s + 256), ind(U(0, 16, 16 + GH), A("snl", 16 * s, 16 * s + 16)), 0)
+            send(s, "0", A("sb0", 256 * s, 256 * s + 256), ghosts(0, 1 - s))
 
-    def sndtab():
-        for s in range(2):
-            act(A("snt", 272 * s, 272 * s + 256), A("mex", 256 * s, 256 * s + 256))
+    def table(t, qs):
+        for i, q in enumerate(qs):
+            b = "p%d" % i
+            mm(b, [(A(b, 0, 512), (X("tsel", 0, 128, 1, 0, 32), [("tsel", 0, 128)]), R("r16", 0, 4, 512 * i, 512 * i + 512), True, True)])
+            add(q, A("TB", 512 * i, 512 * i + 512), A(b, 0, 512), 1536)
 
-    nrow("n16", 192, "brow", "ra")
-    nrow("n16", 96, "rrow", "rb")
-    nrow("n16", 0, "lrow", "rc")
-    sndtab()
-    ms(A("snt", 256, 272), -1.0)
-    ms(A("snt", 528, 544), -1.0)
-    for i in range(5):
-        ms(A("U%d" % i, 0, 16), 0.0)
-
-    def base_send(t, P):
-        ts(A("bs16", 0, 512), ind(A("brow", 0, P), A("snl%d" % t, 0, 32)), -1536, OP.add)
-        b = wb()
-        conv(b, [(0, 32, 1, "MD", rS("bs16", 0, 512))])
-        for s in range(2):
-            ts(A("xo", 16 * s, 16 * s + 16), A(b, 16 * s, 16 * s + 16), -1024 - 256 * s, OP.add)
-        ts(A("xz", 0, 32), A("xo", 0, 32), 0, OP.is_lt, 8192, OP.mult)
-        tt(A("xo2", 0, 32), A("xo", 0, 32), A("xz", 0, 32), OP.add)
-        ts(A("bo", 0, 32), A("xo2", 0, 32), 256, OP.min)
+    def base_send(t):
+        P, nw = PP[t], NW[t]
+        toS("p6", nw, "zr", "r16", 0, P, k=3)
+        ts(A("gs", 0, 512), ind(A("TB", 0, P), A("snl", 0, 32)), -1536, OP.add)
+        toS("p4", 0, "s2", "gs", 0, 512)
         for s in order:
-            send(s, "b", A("bo", 16 * s, 16 * s + 16), "gbo", 16 * (1 - s), 16 * (1 - s) + 16)
+            ts(A("bo", 16 * s, 16 * s + 16), A("p4", 16 * s, 16 * s + 16), 16 - 1024 - 256 * s, OP.add, 272, OP.min)
+            send(s, "b", A("bo", 16 * s, 16 * s + 16), A("gbo", 16 * (1 - s), 16 * (1 - s) + 16))
+        toS("p6", 0, "zl", "r16", 0, P, k=3)
+        toS("p7", 0, "s0", "gs", 0, 512)
+        toS("p7", 32, "s1", "gs", 0, 512)
+        toS("p6", 2 * nw, "zb", "r16", 0, P, k=3)
 
-    def ghost0(t, P):
-        for i, s in enumerate(order):
-            o = A("sb0", 256 * s, 256 * s + 256)
-            x = ind(A("U0", OWN, OWN + P), A("snl%d" % t, 16 * s, 16 * s + 16))
-            if i == 0:
-                cp(o, x)
-            else:
-                act(o, x)
-        for s in order:
-            send(s, "0", A("sb0", 256 * s, 256 * s + 256), "U0", 16 + 256 * (1 - s), 16 + 256 * (1 - s) + 256)
+    def lists(t):
+        P, nw = PP[t], NW[t]
+        for i in range(2):
+            cp(A("st", L(t, i) - 32, L(t, i)), A("p7", 32 * i, 32 * i + 32))
+        for i in range(3):
+            cp(A("st", L(t, i), L(t, i) + nw), A("p6", nw * i, nw * i + nw))
+        n = L(t, 2) + nw
+        ts(A("li", 0, n), A("st", 0, n), 1536, OP.add)
+        ts(A("pl", 0, nw), A("st", L(t, 2), n), 1536, OP.add, P - 1, OP.min)
 
-    def stlist(lo, t, leg, src):
-        nw, lw = NW[t], LW[t]
-        o = leg * lw + (32 if leg < 2 else 0)
-        for n in ("li%d" % t, "st%d" % t):
-            ts(A(n, o, o + nw), A(src, lo, lo + nw), 1536, OP.add)
+    ghost0("SS")
+    for i in range(3):
+        ts(R("r16", 0, 3, 512 * i, 512 * i + 512), R("raw", 0, 3, 512 * i, 512 * i + 512), -1536, OP.add)
+    table(0, "SSV")
+    base_send(0)
+    for s in range(2):
+        act(A("snt", 16 + 272 * s, 272 + 272 * s), A("p5", 256 * s, 256 * s + 256), AF.Identity, bias=1536.0)
+    act(A("dtb", 0, 2048), A("dtb", 0, 2048), AF.Identity, bias=128.75, scale=0.5)
+    for n in range(1, 5):
+        dma("Y", U(n, 16 + V0, 16 + GH), U(0, 16 + V0, 16 + GH))
+    iota(A("TB", V0, GH), [[1, 1024]], V0, 0)
 
-    base_send(0, V0)
     cp(A("thf", 0, 1), A("thi", 0, 1))
+    ts(A("thb", 0, 1), A("thi", 0, 1), -1, OP.mult, 0.5, OP.add)
     cp(A("wtf", 0, 1), A("wti", 0, 1))
-    b = wb()
-    conv(b, [(192, 288, 1, "MD", rS("ra", 0, V0)), (96, 192, 1, "MD", rS("rb", 0, V0)), (0, 96, 1, "MD", rS("rc", 0, V0))])
-    ghost0(0, V0)
-    ts(A("pmod", 0, 160), A("pmi", 0, 160), 15, OP.bitwise_and)
-    tt(A("meS", 0, 160), A("pmod", 0, 160), A("c16", 0, 160), OP.add)
-    ts(A("slotc", 0, 32), A("meS", 0, 32), GH, OP.add)
-    for leg in (2, 1, 0):
-        stlist(96 * leg, 0, leg, b)
-    cb = (A("ab", 0, 1), A("ab", 1, 2))
-    ms(cb[0], -0.5)
-    ms(cb[1], 0.5)
+    ts(A("n4k", 0, 128), A("eye", 0, 128), -BIG, OP.mult)
+    ts(A("s2k", 0, 144), A("s2", 0, 144), BIG, OP.mult)
+    ts(A("s1k", 0, 144), A("s1", 0, 144), BIG, OP.mult)
+    cp(A("mem", 0, 16), A("meS", 0, 16))
+    for a, z in ((16, 32), (32, 64), (64, 128), (128, 256), (256, 384)):
+        cp(A("mem", a, z), A("mem", 0, z - a))
+    lists(0)
+
+    def marks(t, n, c, q):
+        nm, b = "in%d" % (n % 2), "p%d" % c
+        x = U(n, 16 + 512 * c, 16 + 512 * c + 512) if n < 5 else A("u5", 512 * c, 512 * c + 512)
+        o = A(nm, 512 * c, 512 * c + 512)
+        if q == "V":
+            ts(o, x, A("thf", 0, 1), OP.is_ge)
+        else:
+            act(o, x, AF.Sign, bias=A("thb", 0, 1))
+        one(b, 0, 512, "eye", o, n == 0, n == 5)
+
+    MK = (("VVV", "VVV", "VVV", "VVS", "VVS", "VSV"), ("VVVV", "VVVV", "VVVV", "VVVS", "VVVS", "VSVS"))
+
+    def diff(q, n, i, t, c):
+        o = L(t, i) + 16 * c
+        add(q, A(n, 256 * c, 256 * c + 256), ind(A("TB", 0, 3072), A("li", o, o + 16)), -256 * c)
+
+    def keep(b, lo, t, i, c0, c1, s1=False):
+        mm(b, [(A(b, lo, lo + c1 - c0), A("eye", 0, 128), A("st", L(t, i) + c0, L(t, i) + c1), False, s1)])
 
     def prep(t):
-        P, nw, lw = PP[t], NW[t], LW[t]
-        st, li = "st%d" % t, "li%d" % t
-        B0 = 2 * lw
-        ts(A("pl", 0, nw), A(st, B0, B0 + nw), P - 1, OP.min)
-        act(A("fr", 0, P), ind(A("brow", 0, P), A("pl", 0, nw)))
-        if t == 0:
-            masks2()
-        h = lw // 2 + 16
-
-        def valid(b, i, c0, c1):
-            nm = "gr%d" % i
-            tt(A(nm, 16 * c0, 16 * c1), ind(A("brow", 0, 3072), A(li, i * lw + c0, i * lw + c1)), A("mex", 16 * c0, 16 * c1), OP.is_equal)
-            conv(b, [(i * lw + c0, i * lw + c1, 1, "MD", rS(nm, 16 * c0, 16 * c1))])
-        b, bl, b1 = wb(), wb(), wb()
-        valid(b, 1, 32, lw)
-        for i, nm in ((1, "rrow"), (0, "lrow")):
-            ts(A("ls16", 512 * i, 512 * i + 512), ind(A(nm, 0, P), A("snl%d" % t, 0, 32)), -1536, OP.add)
-            conv(bl, [(32 * i, 32 * i + 32, 1, "MD", rS("ls16", 512 * i, 512 * i + 512))])
-        valid(b, 0, 32, h)
-        for k in (1, 0):
-            ts(A(li, k * lw, k * lw + 32), A(bl, 32 * k, 32 * k + 32), 1536, OP.add)
-            ts(A(st, k * lw, k * lw + 32), A(bl, 32 * k, 32 * k + 32), 1536, OP.add)
-        ts(A("ixa", 0, 2 * lw), A(st, 0, 2 * lw), GH, OP.is_ge, -3072, OP.mult)
-        tt(A("ixb", 0, 2 * lw), A("ixa", 0, 2 * lw), A(st, 0, 2 * lw), OP.add)
-        ts(A("ixa", 0, 2 * lw), A("ixb", 0, 2 * lw), OWN, OP.add)
-        valid(b, 1, 0, 32)
-        valid(b, 0, 0, 32)
-        valid(b1, 0, h, lw)
-        legs(b, lw, 2 * lw)
-        legs(b, 0, h)
-        legs(b1, h, lw)
-
-    def ghost_bases():
-        for s in range(2):
-            recv(s, "b", "gbo", 16 * s, 16 * s + 16)
-        for s in range(2):
-            act(A("brow", GH + 256 * s, GH + 256 * s + 256),
-                ind(A("snt", 272 * s, 272 * s + 272), A("gbo", 16 * s, 16 * s + 16)))
-
-    def legs(b, lo, hi):
-        tt(A("ulf", lo, hi), A(b, lo, hi), A("ixa", lo, hi), OP.mult)
-        cp(A("ul", lo, hi), A("ulf", lo, hi))
-
-    held = {}
-
-    def turn(t):
         P, nw = PP[t], NW[t]
-        b = wb()
-        conv(b, [(0, nw, 1, "MDf", rS("fr", 0, P))])
-        held["b"] = b
-
-    def pairs(t):
-        nw, lw = NW[t], LW[t]
-        st, B0 = "st%d" % t, 2 * LW[t]
-        b = held["b"]
-        ts(A("mB", 0, nw), A(st, B0, B0 + nw), GH, OP.is_lt, -88, OP.mult)
-        tt(A("mB2", 0, nw), A("meS", 0, nw), A(st, B0, B0 + nw), OP.is_lt)
-        tt(A("pe", 0, nw), A(b, 0, nw), A("meS", 0, nw), OP.is_equal)
-        tt(A("mB2", 0, nw), A("mB2", 0, nw), A("mB", 0, nw), OP.mult)
-        tt(A("mB", 0, nw), A("mB2", 0, nw), A("pe", 0, nw), OP.mult)
-        ts(A("thr", 0, nw), A("mB", 0, nw), 99, OP.add)
-
-    def flags_row(t, i):
-        P, nw, lw = PP[t], NW[t], LW[t]
-        o = i * lw + (32 if i < 2 else 0)
-        act(A("fr", 0, P), ind(A("rrow", 0, 3072), A("li%d" % t, o, o + nw)))
-        turn(t)
-
-    def flags_col(t, i):
-        nw, lw = NW[t], LW[t]
-        o = i * lw + (32 if i < 2 else 0)
-        b = held["b"]
-        tt(A("fl", nw * i, nw * i + nw), A(b, 0, nw), A("meS", 0, nw), OP.is_equal)
-        ts(A("pm2", nw * i, nw * i + nw), A("st%d" % t, o, o + nw), -GH, OP.add)
-
-    def flags_list(t):
-        nw, lw = NW[t], LW[t]
-        tt(A("lff", 0, 3 * nw), A("fl", 0, 3 * nw), A("pm2", 0, 3 * nw), OP.mult)
-        ts(A("lf", 0, 3 * nw), A("lff", 0, 3 * nw), GH, OP.add)
-        if t == 0:
-            tt(A("sna", 0, 32), A("st0", lw, lw + 32), A("slotc", 0, 32), OP.is_equal)
-            ts(A("snb", 0, 32), A("sn0", 0, 32), -GH, OP.add)
-            tt(A("snc", 0, 32), A("sna", 0, 32), A("snb", 0, 32), OP.mult)
-            ts(A("snf", 0, 32), A("snc", 0, 32), GH, OP.add)
-
-    def marks(u, lo, P, n):
-        nm = "in%d" % (n % 2)
-        for i in range(P // 512):
-            ts(A(nm, 512 * i, 512 * i + 512), A(u, lo + 512 * i, lo + 512 * i + 512), A("thf", 0, 1), OP.is_ge)
-            mm("p%d" % i, [(A("p%d" % i, 0, 512), A("eye", 0, 128), A(nm, 512 * i, 512 * i + 512), n == 0, n == 5)])
+        h, nc = nw // 2, P // 256
+        one("p4", 0, 64, "n4k", A("ones", 0, 64), True, False)
+        for i in range(2):
+            keep("p4", 32 * i, t, i, -32, 0)
+        for k in range(2):
+            b = "p%d" % (5 + k)
+            one(b, 0, nw, "n4k", A("mem", 0, nw), True, False)
+            for i in range(2):
+                keep(b, h * i, t, i, h * k, h * k + h)
+        for q, s in zip("VS", order[::-1]):
+            recv(s, "b", A("gbo", 16 * s, 16 * s + 16))
+            add(q, A("TB", GH + 256 * s, GH + 256 * s + 256), ind(A("snt", 272 * s, 272 * s + 288), A("gbo", 16 * s, 16 * s + 16)), 0)
+        for c in range(nc // 2):
+            diff("S", "dL", 0, t, c)
+        for i in range(2):
+            for s in range(2):
+                o = L(t, i) - 32 + 16 * s
+                tt(A("fs", 512 * i + 256 * s, 512 * i + 256 * s + 256), ind(A("TB", 0, 3072), A("li", o, o + 16)),
+                   A("snt", 16 + 272 * s, 272 + 272 * s), OP.is_equal)
+            toS("p4", 32 * i, "s2k", "fs", 512 * i, 512 * i + 512, False, i == 1)
+        toS("p5", 0, "s2k", "dL", 0, P // 2, False, False)
+        for c in range(nc // 2, nc):
+            diff("S", "dL", 0, t, c)
+        for c in range(nc // 2):
+            diff("V", "dR", 1, t, c)
+        toS("p5", h, "s2k", "dR", 0, P // 2, False, True)
+        toS("p6", 0, "s2k", "dL", P // 2, P, False, False)
+        for c in range(nc // 2, nc):
+            diff("V" if c < nc - 2 else "S", "dR", 1, t, c)
+        toS("p6", h, "s2k", "dR", P // 2, P, False, True)
+        ts(A("ul", 0, 64), A("p4", 0, 64), 1552, OP.add, US, OP.min)
+        ts(A("ul", 64, 64 + nw), A("p5", 0, nw), 1552, OP.add, US, OP.min)
 
     def depths(t, slack):
-        P, nw, lw = PP[t], NW[t], LW[t]
+        P, nw = PP[t], NW[t]
+        H, h = P // 2, nw // 2
         for n in range(5):
-            u = "U%d" % n
             gr = "gr%d" % (n % 2)
-            win = A(u, 0, OWN + P)
-            marks(u, OWN, P, n)
+            win = U(n, 0, US + 16)
             for s in range(2):
-                recv(s, str(n), u, 16 + 256 * s, 16 + 256 * s + 256)
+                recv(s, str(n), ghosts(n, s))
             if n < 4:
                 for s in order:
-                    c = lw + 16 * s
-                    act(A(gr, 256 * s, 256 * s + 256), ind(win, A("ul", c, c + 16)))
+                    act(A(gr, 256 * s, 256 * s + 256), ind(win, A("ul", 32 + 16 * s, 48 + 16 * s)))
                 for s in order:
                     o = A("sb%d" % (n + 1), 256 * s, 256 * s + 256)
                     tt(o, ind(win, A("ul", 16 * s, 16 * s + 16)), A(gr, 256 * s, 256 * s + 256), OP.max)
-                    send(s, str(n + 1), o, "U%d" % (n + 1), 16 + 256 * (1 - s), 16 + 256 * (1 - s) + 256)
-            H = P // 2
-            h16 = H // 16
-            for h in range(2):
-                c = lw + 32 + h16 * h
-                act(A(gr, 512 + H * h, 512 + H * h + H), ind(win, A("ul", c, c + h16)))
-            for h in range(2):
-                o = A("U%d" % (n + 1), OWN + H * h, OWN + H * h + H) if n < 4 else A("u5", H * h, H * h + H)
-                c = 32 + h16 * h
-                tt(o, ind(win, A("ul", c, c + h16)), A(gr, 512 + H * h, 512 + H * h + H), OP.max)
+                    send(s, str(n + 1), o, ghosts(n + 1, 1 - s))
+            if n == 0:
+                ts(A("ul", 64 + nw, 64 + 2 * nw), A("p6", 0, nw), 1552, OP.add, US, OP.min)
+            for k in range(2):
+                c = 64 + nw * k + h
+                act(A(gr, 512 + H * k, 512 + H * k + H), ind(win, A("ul", c, c + h)))
+            for k in range(2):
+                o = U(n + 1, 16 + H * k, 16 + H * k + H) if n < 4 else A("u5", H * k, H * k + H)
+                c = 64 + nw * k
+                tt(o, ind(win, A("ul", c, c + h)), A(gr, 512 + H * k, 512 + H * k + H), OP.max)
             for f in slack.get(n, []):
                 f()
-        marks("u5", 0, P, 5)
+            for c, q in enumerate(MK[t][n + 1]):
+                marks(t, n + 1, c, q)
+
+    def flags0(t):
+        P, nw = PP[t], NW[t]
+        one("p7", 0, 3 * nw, "n4k", A("mem", 0, 3 * nw), True, False)
+        for i in range(3):
+            keep("p7", nw * i, t, i, 0, nw)
+        toS("p7", 0, "s1k", "dL", 0, P, False, False)
+        toS("p7", nw, "s1k", "dR", 0, P, False, False)
+
+    def bases(t, c0, c1):
+        for c in range(c0, c1):
+            diff("S", "dB", 2, t, c)
+
+    def flags1(t):
+        P, nw = PP[t], NW[t]
+        one("p5", 0, nw, "n4k", A("mem", 0, nw), True, False)
+        toS("p5", 0, "s2k", "dB", 0, P, False, True)
+        toS("p7", 2 * nw, "s1k", "dB", 0, P, False, True)
+        b = A("st", L(t, 2), L(t, 2) + nw)
+        ts(A("pen", nw, 2 * nw), b, GH - 1536, OP.is_ge)
+        tt(A("pen", 2 * nw, 3 * nw), A("me16", 0, nw), b, OP.is_ge)
+
+    def flags2(t):
+        nw = NW[t]
+        ts(A("pen", 0, nw), A("p5", 0, nw), 0, OP.not_equal)
+        ts(A("lf", 0, 3 * nw), A("p7", 0, 3 * nw), 1552, OP.add, 16 + GH, OP.min)
+
+    def olds(t):
+        P, w = PP[t], WN[t]
+        for i, m in enumerate(("zl", "zr", "zb")):
+            toN("p6", w * i, w, m, "r16", 0, 0, P, k=3)
+        for i in range(3):
+            act(A("old", w * i, w * i + 128), A("p6", w * i, w * i + 128), AF.Identity, bias=A("bq", t, t + 1))
+            if w > 128:
+                act(A("old", w * i + 128, w * i + w), A("p6", w * i + 128, w * i + w), AF.Identity, bias=A("bq", 0, 1))
+
+    def codes(t):
+        ts(A("jb", 0, 1), A("pq", 0, 1), PP[t], OP.mult, A("pq", 3, 4), OP.add)
+        ts(A("jb", 1, 2), A("pq", 0, 1), PP[t], OP.mult, A("jb", 2, 3), OP.add)
+        for e in range(2):
+            ts((X("jr", e, 512, 2), [("jr", 0, 512)]), A("kq", 0, 256), A("pq", 1, 2), OP.mult, A("jb", e, e + 1), OP.add)
 
     def splits(t):
-        P, nw, nb = PP[t], NW[t], PP[t]
-        for k in range(2):
-            for i in range(P // 512):
-                o, x = A("in%d" % k, 512 * i, 512 * i + 512), A("p%d" % i, 0, 512)
-                if (i + k) % 2 == 0:
-                    act(o, x, AF.Sign)
-                else:
-                    ts(o, x, 0, OP.is_gt)
-        b = wb()
-        for c0, c1 in ((0, nw // 2), (nw // 2, nw)):
-            tt(A("gr1", 16 * c0, 16 * c1), ind(A("in0", 0, P), A("pl", c0, c1)), A("in1", 16 * c0, 16 * c1), OP.max)
-            conv(b, [(c0, c1, 1, "CQ", rS("gr1", 16 * c0, 16 * c1))])
-        tt(A("go", 0, nw), A(b, 0, nw), A("thr", 0, nw), OP.is_ge)
-        b = wb()
-        mm(b, [(A(b, nw, 2 * nw), A("blk", 0, 128), A("go", 0, nw), True, True),
-               (A(b, 0, nw), A("ltg", 0, 128), A("go", 0, nw), True, False),
-               (A(b, 0, nw), A("eye", 0, 128), A("me16", 0, nw), False, True)])
-        op("V", [lambda: g.vector.tensor_tensor_scan(X("sc", 0, nw), X(b, nw, 2 * nw), X("zer", 0, nw), 2048.0, OP.add, OP.add)],
-           [(b, 0, 512), ("zer", 0, nw)], [("sc", 0, nw)])
-        tt(A("ka", 0, nw), A("sc", 0, nw), A(b, 0, nw), OP.add)
-        tt(A("kc", 0, nw), A("ka", 0, nw), A("go", 0, nw), OP.mult)
-        tt(A("kd", 0, nw), A("kc", 0, nw), A("meS", 0, nw), OP.add)
-        cp(A("koff", 0, nw), A("kd", 0, nw))
-        scat(A("lrow", 0, 3072), A("koff", 0, nw), A("mex", 512, 512 + P))
-        ts((X("T16", 0, 512, 2), [("T16", 0, 512)]), A("lrow", 2048, 2304), -1536, OP.add)
-        b = wb()
-        conv(b, [(0, 16, 1, "MD", lambda q: (X("T16", 2 * q, 512, 32), [("T16", 0, 512)]))])
-        ts(A("tl", 0, 16), A(b, 0, 16), 1536, OP.add)
-        ts((X("T16", 1, 512, 2), [("T16", 0, 512)]), ind(A("brow", 0, nb + 512), A("tl", 0, 16)), -1536, OP.add)
-        b = wb()
-        conv(b, [(0, 32, 1, "MD", rS("T16", 0, 512))])
-        ts(A("TL", 0, 32), A(b, 0, 32), 1536, OP.add)
-        act(A("t32", 0, 32), A(b, 0, 32), AF.Identity, bias=1536.0)
-
-    def renames(t):
-        P, nw, nb = PP[t], NW[t], PP[t]
-        scat(A("NT", 0, nb + 512), A("TL", 0, 32), A("jrow", 0, 512))
-        act(A("eT", 0, 512), ind(A("U0", OWN, OWN + nb + 512), A("TL", 0, 32)))
-        win = A("NT", 0, 2576)
-        H = P // 2
-        act(A("vR", 0, P), ind(win, A("lf", nw, 2 * nw)))
-        act(A("vL", H, P), ind(win, A("lf", nw // 2, nw)))
-        act(A("e2", 0, 512), A("eT", 0, 512), AF.Identity, bias=128.75, scale=0.5)
-        act(A("e2b", 0, 512), A("e2", 0, 512), AF.Identity, bias=-258.0)
-        act(A("vy", 0, 512), ind(A("vR", 0, nb + 512), A("TL", 0, 32)))
-        cp(A("vB", 0, P), ind(win, A("lf", 2 * nw, 3 * nw)))
-        cp(A("vL", 0, H), ind(win, A("lf", 0, nw // 2)))
-        if t == 0:
-            cp(A("vs", 0, 512), ind(win, A("snf", 0, 32)))
-        ts(A("Y16", 0, 512), ind(A("rrow", 0, nb + 512), A("TL", 0, 32)), -1536, OP.add)
-
-    def update(t, lay):
-        P, nw, nb = PP[t], NW[t], PP[t]
-        k0 = nb - 1.5
-        if lay == "S":
-            a, c, ic = "st%d" % t, "st%d" % (t + 1), LW[t + 1]
-            src = (32, LW[t] + 32, 2 * LW[t])
-            dst = (32, ic + 32, 2 * ic)
-        else:
-            a, c, ic = "ns%d" % t, "ns%d" % (t + 1), nw + 32
-            src = (0, nw, 2 * nw)
-            dst = (0, ic, 2 * ic)
-
-        def places(n, lo):
-            if lay == "S":
-                return [(lo, lo + nw, 1, "MD", rS(n, 0, P))]
-            r = [(lo, lo + 96, 1, "MD", lambda q: (X(n, 96 * q, 96 * q + 96), [(n, 0, P)]))]
-            if P > V0:
-                r.append((lo + 96, lo + 128, 1, "MD", lambda q: (X(n, V0 + 32 * q, V0 + 32 * q + 32), [(n, 0, P)])))
-            return r
-
-        def new(n, lo, swap):
-            if lay == "S":
-                return [(lo, lo + 32, 1, "MD", lambda q: (X(n, q ^ swap, 512, 16), [(n, 0, 512)]))]
-            if not swap:
-                return [(lo, lo + 32, 1, "MD", lambda q: (X(n, 32 * q, 32 * q + 32), [(n, 0, 512)]))]
-            return [(lo + e, lo + 32, 2, "MD", lambda q, e=e: (X(n, 32 * q + 1 - e, 32 * q + 32, 2), [(n, 0, 512)])) for e in range(2)]
-        for i in range(3):
-            act(A("pt", nw * i, nw * i + nw), A(a, src[i], src[i] + nw), AF.Identity, bias=-k0)
-        b = wb()
-        for n, lo in (("NT", 3 * nw), ("vB", 2 * nw), ("vR", nw), ("vL", 0)):
-            conv(b, places(n, lo))
-        b3, b2 = wb(), wb()
-        conv(b2, new("T16", 0, 0) + new("T16", 32, 1) + new("Y16", 64, 0) + new("vy", 96, 0))
-        yield
-        act(A(b3, 0, 4 * nw), A(b, 0, 4 * nw), AF.Abs, bias=cb[0], scale=2.0)
-        ts(A("z", 0, 4 * nw), A(b, 0, 4 * nw), 0, OP.is_equal, -8192, OP.mult)
-        tt(A("q3", 0, 3 * nw), A(b3, 0, 3 * nw), A("z", 0, 3 * nw), OP.add)
-        ts(A("ysn", 0, nw), A(b3, 3 * nw, 4 * nw), k0, OP.add)
-        act(A(b3, 0, nw), A(b, 3 * nw, 4 * nw), AF.Abs, bias=cb[1], scale=2.0)
-        tt(A("q3", 0, 3 * nw), A("q3", 0, 3 * nw), A("pt", 0, 3 * nw), OP.max)
-        ts(A("q3u", 0, 3 * nw), A("q3", 0, 3 * nw), k0, OP.add)
-        yield
-        ts(A("sp", 0, nw), A("z", 3 * nw, 4 * nw), 0, OP.is_equal)
-        ts(A("nsp", 0, nw), A("z", 3 * nw, 4 * nw), 0, OP.is_lt)
-        ts(A("ysn", nw, 2 * nw), A(b3, 0, nw), k0, OP.add)
-        for i in range(2):
-            tt(A("yss", nw * i, nw * i + nw), A("ysn", nw * i, nw * i + nw), A("sp", 0, nw), OP.mult)
-        tt(A("oc", 0, nw), A("q3u", 2 * nw, 3 * nw), A("nsp", 0, nw), OP.mult)
-        tt(A("od", 0, nw), A("q3u", 0, nw), A("sp", 0, nw), OP.mult)
-        tt(A(c, dst[2], dst[2] + nw), A("oc", 0, nw), A("od", 0, nw), OP.add)
-        o = nw
-        act(A(b3, 256, 288), A(b2, 96, 128), AF.Abs, bias=cb[0], scale=2.0)
-        act(A("yt", 0, 32), A(b2, 64, 96), AF.Identity, bias=1536 - k0)
-        act(A(c, dst[1] + o, dst[1] + o + 32), A(b2, 0, 32), AF.Identity, bias=1536.0)
-        act(A("tsw", 0, 32), A(b2, 32, 64), AF.Identity, bias=1536.0)
-        ts(A("zy", 0, 32), A(b2, 96, 128), 0, OP.is_equal, -8192, OP.mult)
-        tt(A("yzy", 0, 32), A(b3, 256, 288), A("zy", 0, 32), OP.add)
-        tt(A("td", 0, 32), A("yzy", 0, 32), A("yt", 0, 32), OP.max)
-        ts(A(c, dst[2] + o, dst[2] + o + 32), A("td", 0, 32), k0, OP.add)
-        yield
-        tt(A("oa", 0, nw), A("q3u", 0, nw), A("nsp", 0, nw), OP.mult)
-        tt(A(c, dst[0], dst[0] + nw), A("oa", 0, nw), A("yss", 0, nw), OP.add)
-        tt(A("ob", 0, nw), A("q3u", nw, 2 * nw), A("nsp", 0, nw), OP.mult)
-        tt(A(c, dst[1], dst[1] + nw), A("ob", 0, nw), A("yss", nw, 2 * nw), OP.add)
-        tr = A(c, dst[1] + o, dst[1] + o + 32)
-        ts(A("tab", 0, 32), tr, nb, OP.is_ge)
-        tt(A("td", 0, 32), tr, A("tsw", 0, 32), OP.subtract)
-        tt(A("yu", 0, 32), A("td", 0, 32), A("tab", 0, 32), OP.mult)
-        tt(A(c, dst[0] + o, dst[0] + o + 32), A("tsw", 0, 32), A("yu", 0, 32), OP.add)
-        yield
-
-    def srow(x, lo, ncol, row, both):
-        for i in range(ncol // 32):
-            b = wb()
-            mm(b, [(A(b, q, 512, 16), A("EQ", 128 * q, 128 * q + 128), A(x, lo + 32 * i, lo + 32 * i + 32), True, True) for q in range(16)])
-            o = A(row, 512 * i, 512 * i + 512)
-            if both and i % 2:
-                ts(o, A(b, 0, 512), 1536, OP.add)
+        P, nw = PP[t], NW[t]
+        nc, k = P // 512, nw // 16
+        who = ["VS"[c % 2] for c in range(nc)]
+        for c in range(nc):
+            lift = sum(MK[t][n][c] == "S" for n in range(6))
+            if nc == 3 and c == 2:
+                for e in range(2):
+                    add("VS"[e], A("in0", 1024 + 256 * e, 1280 + 256 * e), A("p2", 256 * e, 256 * e + 256), lift)
             else:
-                act(o, A(b, 0, 512), AF.Identity, bias=1536.0)
-
-    def new_snd():
-        b = wb()
-        conv(b, [(0, 32, 1, "MD", rS("vs", 0, 512))])
-        act(A("sna", 0, 32), A(b, 0, 32), AF.Abs, bias=cb[0], scale=2.0)
-        ts(A("snv", 0, 32), A(b, 0, 32), 0, OP.is_equal, -8192, OP.mult)
-        tt(A("snb", 0, 32), A("sna", 0, 32), A("snv", 0, 32), OP.add)
-        ts(A("snc", 0, 32), A("snb", 0, 32), V0 - 1.5, OP.add)
-        tt(A("sn1", 0, 32), A("snc", 0, 32), A("sn0", 0, 32), OP.max)
-        cp(A("snl1", 0, 32), A("sn1", 0, 32))
-        ts(A("sn16", 0, 32), A("sn1", 0, 32), -1536, OP.add)
+                add(who[c], A("in0", 512 * c, 512 * c + 512), A("p%d" % c, 0, 512), lift)
+        one("p4", 0, nw, "n64", A("pen", 0, nw), True, False)
+        for i in (1, 2):
+            one("p4", 0, nw, "n64", A("pen", nw * i, nw * i + nw), False, False)
+        parts = [(q, 256 * c, 256 * c + 256) for c, q in enumerate("VS" * nc)]
+        for q, lo, hi in parts:
+            add(q, A("gr0", lo, hi), ind(A("in0", 0, P), A("pl", lo // 16, hi // 16)), 0)
+        for c in range(nc):
+            b = "p%d" % c
+            mm(b, [(A(b, 0, 512), A("eye", 0, 128), A(n, 512 * c, 512 * c + 512), n == "in0", n == "gr0") for n in ("in0", "gr0")])
+        for c in range(nc):
+            b, o = A("p%d" % c, 0, 512), A("in1", 512 * c, 512 * c + 512)
+            if who[c] == "S":
+                act(o, b, AF.Sign)
+            else:
+                ts(o, b, 0, OP.is_gt)
+        cut = 1024
+        toS("p4", 0, "cq", "in1", 0, cut, False, False)
+        toS("p4", cut // 16, "cq", "in1", cut, P, False, True)
+        go = A("go", 0, nw)
+        ts(go, A("p4", 0, nw), 11, OP.is_ge)
+        one("p5", 0, nw, "blk", go)
+        one("p6", 0, k, "eye", A("d16", 0, k), True, False)
+        toS("p6", 0, "ncq", "go", 0, nw, False, True)
+        for e, x in enumerate((A("me16", 0, nw), A("st", L(t, 2), L(t, 2) + nw))):
+            mm("p7", [(A("p7", nw * e, nw * e + nw), A("eye", 0, 128), x, True, False), (A("p7", nw * e, nw * e + nw), A("lt", 0, 128), go, False, True)])
+        scan(A("inc", 1, nw + 1), A("p5", 0, nw), A("zer", 0, nw), OP.add, OP.add)
+        act(A("ee", 0, k), A("p6", 0, k), AF.Relu)
+        act(A("val", 0, 2 * nw), A("p7", 0, 2 * nw), AF.Identity, bias=1537.0 - 32 * BIG)
+        toS("p4", 0, "s0", "inc", 0, nw, True, False)
+        one("p4", 0, k, "eye", A("ee", 0, k), False, True)
+        cp(A("off", 0, k), A("p4", 0, k))
+        for e in range(2):
+            scat(A("Z%d" % e, 0, 3072), A("off", 0, k), A("val", nw * e, nw * e + nw))
+        for e in range(2):
+            scan(A("sc", 256 * e, 256 * e + 256), A("m4k", 0, 256), A("Z%d" % e, 0, 256), OP.add, OP.max)
+        ts(A("y16", 0, 512), A("sc", 0, 512), 0, OP.max, BIG, OP.min)
+        mm("p5", [(A("p5", 0, 32), M("cq", q), (X("y16", 256 * (q % 2) + q // 2, 256 * (q % 2) + 256, 8), [("y16", 0, 512)]), q == 0, q == 15)
+                  for q in range(16)])
+        ts(A("ti", 0, 32), A("p5", 0, 32), -1, OP.add)
+        ts(A("ti2", 0, 32), A("ti", 0, 32), 4095, OP.bitwise_and)
+        tt(A("t32", 0, 32), A("ti2", 0, 32), A("meS", nw, nw + 32), OP.min)
+        cp(A("TL", 0, 32), A("t32", 0, 32))
 
     def weigh(t):
-        nb = PP[t]
-        b = wb()
-        conv(b, [(0, 32, 1, "WQ", rS("eT", 0, 512))])
-        tt(A("hz", 0, 32), A(b, 0, 32), A("t32", 0, 32), OP.add)
-        tt(A("hz", 32, 64), A(b, 0, 32), A("meS", nb // 16, nb // 16 + 32), OP.add)
+        nw = NW[t]
+        tt(A("hz", 0, 32), A("p3", 0, 32), A("t32", 0, 32), OP.add)
+        tt(A("hz", 32, 64), A("p3", 0, 32), A("meS", nw, nw + 32), OP.add)
+        ts(A("big", 0, 32), A("t32", 0, 32), PP[t], OP.is_ge, BIG, OP.mult)
+        ts(A("hz2", 0, 64), A("hz", 0, 64), 2047, OP.bitwise_and)
+        tt(A("hb", 0, 32), A("hz2", 32, 64), A("big", 0, 32), OP.add)
+        cp(A("eo", 0, 32), A("hz2", 0, 32))
+        ts(A("eo", 32, 64), A("hb", 0, 32), 2048, OP.min)
 
     def children(t):
-        nb = PP[t]
-        ts(A("hz2", 0, 64), A("hz", 0, 64), 2047, OP.bitwise_and)
-        ts(A("hq", 0, 64), A("hz2", 0, 64), -2048, OP.add)
-        for i in range(2):
-            ts(A("pres", 32 * i, 32 * i + 32), A("t32", 0, 32), nb, OP.is_lt)
-        tt(A("hm", 0, 64), A("hq", 0, 64), A("pres", 0, 64), OP.mult)
-        ts(A("eo", 0, 64), A("hm", 0, 64), 2048, OP.add)
+        P = PP[t]
         tt(A("cT", 0, 512), ind(A("dtb", 0, 2064), A("eo", 0, 32)), A("e2b", 0, 512), OP.add)
-        scat(A("U0", OWN, OWN + nb + 512), A("TL", 0, 32), A("cT", 0, 512))
-        tt(A("U0", OWN + nb, OWN + nb + 512), ind(A("dtb", 0, 2064), A("eo", 32, 64)), A("e2b", 0, 512), OP.add)
+        scat(U(0, 16, 16 + P + 512), A("TL", 0, 32), A("cT", 0, 512))
+        tt(U(0, 16 + P, 16 + P + 512), ind(A("dtb", 0, 2064), A("eo", 32, 64)), A("e2b", 0, 512), OP.add)
 
-    ms(A("rrow", GH, 3088), -1.0)
-    iota(A("rrow", V0, GH), [[1, 1024]], V0, 0)
-    iota(A("jq", 0, 256), [[1, 256]], 1, 0)
-    sel(A("tri", 0, 128), A("blk", 0, 128), [[-1, 128]], OP.is_ge, 0, 1)
-    iota(A("U0", OWN + V0, OWN + GH), [[0, 1024]], 0, 0)
+    def update(t, cut):
+        P, nw, w = PP[t], NW[t], WN[t]
+        tl = A("TL", 0, 32)
+        scat(A("NT", 16, 16 + P + 512), tl, A("jr", 0, 512))
+        act(A("gf", 0, 512), ind(A("TB", 0, P + 512), tl))
+        act(A("eT", 0, 512), ind(U(0, 16, 16 + P + 512), tl))
+        win = A("NT", 0, 2592)
+        if t == 0:
+            act(A("vs", 0, 512), ind(win, A("snf", 0, 32)))
+        act(A("vR", 0, P), ind(win, A("lf", nw, 2 * nw)))
+        cp(A("vL", 0, P), ind(win, A("lf", 0, nw)))
+        toN("p0", 0, w, "f1", "gf", 0, P, P + 512)
+        one("p1", 0, 3 * w, "za", A("jr", 0, 3 * w), True, False)
+        toN("p1", 0, w, "f2", "gf", 0, P, P + 512, False, False)
+        toN("p1", w, w, "f3", "gf", 0, P, P + 512, False, False)
+        toS("p3", 0, "wq", "eT", 0, 512)
+        toN("p2", 0, w, "wn", "NT", 16, 0, P)
+        toN("p2", w, w, "cq", "NT", 16, 0, P)
+        if t == 0:
+            toS("p4", 0, "wn", "vs", 0, 512)
+            mm("p5", [(A("p5", 0, 512), M("wn", 2), A("vs", 0, 512), True, True)])
+        act(A("vy", 0, 512), ind(A("vR", 0, P + 512), tl))
+        if cut < nw:
+            act(A("vB", 16 * cut, P), ind(win, A("lf", 2 * nw + cut, 3 * nw)))
+        cp(A("vB", 0, 16 * cut), ind(win, A("lf", 2 * nw, 2 * nw + cut)))
+        act(A("e2", 0, 512), A("eT", 0, 512), AF.Identity, bias=128.75, scale=0.5)
+        act(A("e2b", 0, 512), A("e2", 0, 512), AF.Identity, bias=-258.0)
+        toN("p1", w, w, "wn", "vR", 0, 0, P, False, False)
+        toN("p1", 0, w, "wn", "vL", 0, 0, P, False, False)
+        toN("p1", 2 * w, w, "wn", "vy", 0, P, P + 512, False, False)
+        toN("p1", 2 * w, w, "wn", "vB", 0, 0, P, False, True)
+        tt(A("old", 2 * w, 3 * w), A("old", 2 * w, 3 * w), A("p0", 0, w), OP.add)
+        ts(A("nsp", 0, 2 * w), A("p2", 0, 2 * w), 0, OP.is_equal)
+        yield
+        tt(A("lrb", 0, 3 * w), A("old", 0, 3 * w), A("p1", 0, 3 * w), OP.max)
+        tt(A("ub", 0, w), A("lrb", 2 * w, 3 * w), A("lrb", 0, w), OP.subtract)
+        tt(A("ua", 0, 2 * w), A("lrb", 0, 2 * w), A("nsp", 0, 2 * w), OP.mult)
+        tt(A("uc", 0, w), A("ub", 0, w), A("nsp", 0, w), OP.mult)
+        tt(A("new", 0, 2 * w), A("ua", 0, 2 * w), A("p2", 0, 2 * w), OP.add)
+        tt(A("new", 2 * w, 3 * w), A("uc", 0, w), A("lrb", 0, w), OP.add)
+        yield
 
-    def sentinels(t):
-        iota(A("lrow", 2048, 2304), [[2, 256]], PP[t], 0)
+    iota(A("ik", 0, 16), [[-1, 16]], 16, 1, False)
+    sel((X("za", 16, 144, 16), [("za", 0, 144)]), A("ones", 0, 8), [[-16, 8]], OP.is_ge, 0, 1)
+    sel((X("cq", 16, 144, 16), [("cq", 0, 144)]), (X("za", 16, 144, 16), [("za", 0, 144)]), [[16, 8]], OP.is_ge, 15, -1)
+    sel(A("blka", 0, 128), A("ones", 0, 128), [[-16, 8], [0, 16]], OP.is_ge, 0, 1)
+    sel(A("blk", 0, 128), A("blka", 0, 128), [[16, 8], [0, 16]], OP.is_ge, 15, -1)
+    sel(A("tri", 0, 128), A("blk", 0, 128), [[1, 128]], OP.is_gt, 0, -1)
+    iota(A("kq", 0, 256), [[2, 256]], 0, 0)
+    fill("za", 0, 144)
+    fill("dtb", 2048, 2064, 129)
+    fill("zer", 0, 128)
+    fill("m4k", 0, 256, -4096)
+    cp(A("snS", 0, 32), A("snl", 0, 32))
+    ts(A("slc", 0, 32), A("meS", 0, 32), GH - 1536, OP.add)
+    cp(A("sn0", 0, 32), A("snl", 0, 32))
+    one("p3", 0, 32, "eye", A("snS", 0, 32), True, False)
+    one("p3", 0, 32, "n4k", A("slc", 0, 32), False, False)
+    toS("p3", 0, "s1k", "gs", 0, 512, False, True)
+    ts(A("snf", 0, 32), A("p3", 0, 32), 16, OP.add, 16 + GH, OP.min)
+    for c, q in enumerate(MK[0][0]):
+        marks(0, 0, c, q)
+    prep(0)
 
     def late0():
-        for q in range(16):
-            act(A("MDf", 128 * q, 128 * q + 128), A("eye", 0, 128), AF.Copy, scale=A("pq", q, q + 1))
-        ts(A("ltg", 0, 128), A("tri", 0, 128), -1, OP.mult)
-        ts(A("me16", 0, 128), A("meS", 0, 128), -1, OP.mult)
-        ms(A("zer", 0, 128), 0.0)
-        cp((X("jrow", 0, 512, 2), [("jrow", 0, 512)]), A("jq", 0, 256))
-        ts((X("jrow", 1, 512, 2), [("jrow", 0, 512)]), A("jq", 0, 256), -1, OP.mult)
-
-    def masks2():
-        for i in range(4):
-            b = wb()
-            mm(b, [(A(b, 0, 512), A("blk", 0, 128), A("MD", 512 * i, 512 * i + 512), True, True)])
-            act(A("CQ", 512 * i, 512 * i + 512), A(b, 0, 512))
-            act(A("WQ", 512 * i, 512 * i + 512), A(b, 0, 512), AF.Copy, scale=A("wtf", 0, 1))
+        ts(A("me16", 0, 128), A("meS", 0, 128), -1536, OP.add)
+        ts(A("d16", 0, 8), A("meS", 0, 8), 8, OP.mult, 1024, OP.add)
+        ts(A("ik2", 0, 16), A("ik", 0, 16), 15, OP.bitwise_and)
+        ts(A("inc", 0, 1), A("zer", 0, 1), 0, OP.add)
+        ts(A("pq", 0, 16), A("ik2", 0, 16), 0, OP.is_equal)
+        for t in range(2):
+            ts(A("bq", t, t + 1), A("qf", 0, 1), 12 + t, OP.is_lt, 1536, OP.mult)
+        ts(A("n3", 0, 1), A("qf", 0, 1), 3, OP.not_equal)
+        tt(A("jb", 2, 3), A("pq", 2, 3), A("pq", 3, 4), OP.subtract)
 
     def late1():
-        act(A("dtb", 0, 2048), A("dtb", 0, 2048), AF.Identity, bias=128.75, scale=0.5)
-        ms(A("dtb", 2048, 2064), 129.0)
-        cp(A("ns0", 0, 288), A("nraw", 0, 288))
+        for a in (1, 2, 3):
+            act(A("f%d" % a, 0, 144), A("s%d" % a, 0, 144))
+        act(A("wn", 0, 144), A("cq", 0, 144), scale=A("n3", 0, 1))
+        act(A("wq", 0, 144), A("cq", 0, 144), scale=A("wtf", 0, 1))
+        act(A("ncq", 0, 144), A("cq", 0, 144), scale=-BIG)
+        act(A("n64", 0, 128), A("eye", 0, 128), scale=-64.0)
+        act(A("blka", 0, 128), A("eye", 0, 128), scale=32 * BIG)
+        act(A("tri", 0, 128), A("tri", 0, 128), scale=BIG)
+        tt(A("lt", 0, 128), A("tri", 0, 128), A("blka", 0, 128), OP.add)
 
-    def late2(t):
-        iota(A("NT", 0, 2576), [[0, 2576]], 0, 0)
-        iota(A("vR", PP[t], PP[t] + 512), [[0, 512]], 0, 0)
+    def zs():
+        for e in range(2):
+            fill("Z%d" % e, 0, 256)
 
-    ghost_bases()
-    prep(0)
-    depths(0, {0: [late0, lambda: turn(0), lambda: sentinels(0)], 1: [lambda: pairs(0), lambda: flags_row(0, 0)],
-               2: [lambda: flags_col(0, 0), lambda: flags_row(0, 1)],
-               3: [lambda: flags_col(0, 1), lambda: flags_row(0, 2), lambda: late2(0)],
-               4: [late1, lambda: flags_col(0, 2), lambda: flags_list(0)]})
+    nc = 6
+    depths(0, {0: [late0, lambda: flags0(0), lambda: bases(0, 0, 2), lambda: fill("NT", 0, 1024)],
+               1: [lambda: bases(0, 2, 4), lambda: fill("NT", 1024, 2048), lambda: codes(0)],
+               2: [lambda: bases(0, 4, 6), lambda: flags1(0), lambda: fill("NT", 2048, 2592), zs],
+               3: [late1, lambda: flags2(0), lambda: fill("vR", V0, GH)],
+               4: [lambda: olds(0)]})
     splits(0)
-    renames(0)
-    for _ in update(0, "S"):
-        pass
-    new_snd()
-    lw, nw = LW[1], NW[1]
-    ts(A("x16", 256, 384), A("st1", 2 * lw, 2 * lw + nw), -1536, OP.add)
-    srow("x16", 256, 128, "brow", True)
-    srow("sn16", 0, 32, "mex", False)
-    sndtab()
-    base_send(1, 2048)
-    for i in (1, 0):
-        ts(A("x16", 128 * i, 128 * i + 128), A("st1", lw * i + 32, lw * i + 32 + nw), -1536, OP.add)
-    weigh(0)
-    srow("x16", 128, 128, "rrow", False)
-    ghost_bases()
-    srow("x16", 0, 128, "lrow", False)
-    children(0)
-    ghost0(1, 2048)
-    for i in range(3):
-        o = lw * i + (32 if i < 2 else 0)
-        cp(A("li1", o, o + nw), A("st1", o, o + nw))
-    prep(1)
-    un = update(0, "N")
+    un = update(0, 40)
     next(un)
-    depths(1, {0: [lambda: turn(1), lambda: sentinels(1), lambda: next(un)], 1: [lambda: pairs(1), lambda: flags_row(1, 0)],
-               2: [lambda: flags_col(1, 0), lambda: next(un), lambda: flags_row(1, 1)],
-               3: [lambda: flags_col(1, 1), lambda: next(un), lambda: flags_row(1, 2), lambda: late2(1)],
-               4: [lambda: flags_col(1, 2), lambda: flags_list(1)]})
+    tt(A("sn1", 0, 32), A("sn0", 0, 32), A("p4", 0, 32), OP.max)
+    cp(A("snl", 0, 32), A("sn1", 0, 32))
+    next(un)
+    ts(A("n16", 0, 384), A("new", 0, 384), -1536, OP.add)
+    for i in range(3):
+        dma("Y", R("r16", i, i + 1, 0, 2048), A("n16", 128 * i, 128 * i + 128))
+    for s in range(2):
+        x = A("snt", 16 + 272 * s, 272 + 272 * s)
+        tt(x, x, A("p5", 256 * s, 256 * s + 256), OP.max)
+    weigh(0)
+    children(0)
+    table(1, "SSSV")
+    base_send(1)
+    ghost0("SS")
+    lists(1)
+    for c, q in enumerate(MK[1][0]):
+        marks(1, 0, c, q)
+    prep(1)
+    depths(1, {0: [lambda: flags0(1), lambda: bases(1, 0, 3), lambda: fill("NT", 16, 1040)],
+               1: [lambda: bases(1, 3, 6), lambda: fill("NT", 1040, 2064), lambda: codes(1)],
+               2: [lambda: bases(1, 6, 8), lambda: flags1(1), zs],
+               3: [lambda: flags2(1)],
+               4: [lambda: olds(1)]})
     splits(1)
-    renames(1)
+    un = update(1, 32)
+    next(un)
     weigh(1)
     children(1)
-    dma("Y", (HB("ye"), []), A("U0", OWN, OWN + GH))
-    for _ in update(1, "N"):
-        pass
-    for i, n in ((2, "yb"), (0, "yl"), (1, "yr")):
-        for j, (lo, hi, c0, c1) in enumerate(((0, 1536, 0, 96), (1536, 2048, 96, 128), (2048, 2560, 128, 160))):
-            dma("SYS"[j], (T[n][:, lo:hi], []), A("ns2", 160 * i + c0, 160 * i + c1))
+    dma("Y", HB("ye"), U(0, 16, 16 + GH))
+    next(un)
+    for i, n in ((0, "yl"), (1, "yr"), (2, "yb")):
+        dma("YSY"[i], HB(n), A("new", 160 * i, 160 * i + 160))
     wait_for("Y", {s: v for s, v in cnt.items()})

@@ -21,28 +21,28 @@ def _pack(big, dtype, parts):
     SCRATCH[big] = ("sbuf", [128, o], dtype)
 
 
-MASKS = ("zl", "zr", "zb", "zm", "s0", "s1", "s2", "s3", "za", "cq")
+MASKS = ("zl", "zr", "zb", "s0", "s1", "s2", "s3", "za", "cq")
 _pack("km", "bfloat16", [(n, 144) for n in MASKS])
-_pack("kf", "float32", (("pq", 16), ("qf", 1), ("qn", 1), ("meS", 160), ("zer", 128), ("thf", 1), ("thb", 1), ("wtf", 1), ("bq", 2), ("jb", 4),
-                        ("n3", 1), ("f1", 144), ("f2", 144), ("f3", 144), ("sn0", 32), ("sn1", 32), ("old", 480), ("val", 256), ("m4k", 256),
-                        ("sc", 512), ("t32", 32), ("lrb", 480), ("nsp", 320), ("ua", 320), ("ub", 160), ("uc", 160), ("new", 480),
-                        ("big", 32), ("hb", 32), ("gf", 512), ("c160", 160), ("c16", 160), ("snt", 560)))
-_pack("ki", "int32", (("thi", 1), ("wti", 1), ("ik", 16), ("ik2", 16), ("pi", 1), ("qi", 1), ("mi", 16), ("mi2", 16), ("ti", 32), ("ti2", 32),
+_pack("kf", "float32", (("pq", 16), ("qf", 1), ("qn", 1), ("meS", 160), ("zer", 128), ("thf", 1), ("thb", 1), ("wtf", 1), ("jb", 4),
+                        ("n3", 1), ("meN", 96), ("sn0", 32), ("sn1", 32), ("old", 480), ("val", 256), ("m4k", 256),
+                        ("sc", 512), ("t32", 32), ("lrb", 480), ("nsp", 480), ("ua", 480), ("new", 480),
+                        ("big", 32), ("hb", 32), ("c160", 160), ("snt", 560), ("b0", 32), ("dl", 64), ("sp", 64), ("bx", 64)))
+_pack("ki", "int32", (("thi", 1), ("wti", 1), ("ik", 16), ("ik2", 16), ("pi", 1), ("qi", 1), ("ti", 32), ("ti2", 32),
                       ("hz", 64), ("hz2", 64)))
 _pack("ku", "uint16", (("li", 448), ("snl", 32), ("gbo", 32), ("bo", 32), ("ul", 320), ("pl", 128), ("off", 8), ("TL", 32), ("lf", 384),
                        ("snf", 32), ("eo", 64)))
-_pack("kh", "float16", (("meN", 160), ("sn16", 512), ("gs", 512), ("st", 448), ("snS", 32), ("slc", 32), ("me16", 128), ("d16", 8),
-                        ("inc", 144), ("y16", 512), ("n16", 384)))
+_pack("kh", "float16", (("sn16", 512), ("gs", 512), ("st", 448), ("snS", 32), ("slc", 32), ("me16", 128), ("d16", 128),
+                        ("inc", 144), ("ofr", 128), ("y16", 512), ("n16", 384), ("gf", 512)))
 _pack("kb", "bfloat16", (("ones", 128), ("eye", 128), ("blk", 128), ("blka", 128), ("tri", 128), ("lt", 128), ("n64", 128), ("n4k", 128),
-                         ("ts0", 128), ("tsel", 128), ("s1k", 144), ("s2k", 144), ("wn", 144), ("wq", 144), ("ncq", 144), ("mem", 384),
-                         ("kq", 256), ("jr", 512), ("go", 128), ("pen", 384), ("ee", 8), ("eT", 512), ("e2", 512), ("e2b", 512),
-                         ("cT", 512), ("vs", 512), ("vy", 512), ("fs", 1024),
+                         ("ts0", 128), ("tsel", 128), ("s1k", 144), ("s2k", 144), ("wn", 144), ("wq", 144), ("nblk", 128), ("mem", 384),
+                         ("mem0", 384), ("kq", 256), ("jr", 512), ("go", 128), ("pen", 384), ("eT", 512), ("e2", 512), ("e2b", 512),
+                         ("cT", 512), ("vs", 1024), ("vy", 512), ("fs", 1024),
                          ("sb0", 512), ("sb1", 512), ("sb2", 512), ("sb3", 512), ("sb4", 512)))
-for _n, _c, _d in (("raw", V0, "int32"), ("rsn", 512, "int32"), ("r16", 2560, "float16"), ("TB", 3072, "float32"),
-                   ("Z0", 3072, "float32"), ("Z1", 3072, "float32"), ("UU", 5 * US + 16, "bfloat16"),
+for _n, _c, _d in (("raw", V0, "int32"), ("rsn", 512, "int32"), ("r16", 2048, "float16"), ("TB", 3072, "float32"),
+                   ("Z0", 1152, "float32"), ("Z1", 1152, "float32"), ("UU", 5 * US + 16, "bfloat16"),
                    ("dtb", 2064, "bfloat16"), ("NT", 2592, "bfloat16"), ("vL", 2048, "bfloat16"), ("vR", 2560, "bfloat16"),
                    ("vB", 2048, "bfloat16"), ("dL", 2048, "bfloat16"), ("dR", 2048, "bfloat16"), ("dB", 2048, "bfloat16"),
-                   ("u5", 2048, "bfloat16"), ("gr0", 2560, "bfloat16"), ("gr1", 2560, "bfloat16"), ("in0", 2048, "bfloat16"),
+                   ("gr0", 2560, "bfloat16"), ("gr1", 2560, "bfloat16"), ("in0", 2048, "bfloat16"),
                    ("in1", 2048, "bfloat16")):
     SCRATCH[_n] = ("sbuf", [128, _c], _d)
 for _n in range(8):
@@ -121,13 +121,25 @@ def rank_program(g, core, T, topo):
 
     ndma = [0]
 
+    def dmas(jobs, done=None, more=False):
+        done = [] if done is None else done
+        for q, out, in_ in jobs:
+            wait_for(q, needs(q, in_[1], out[1]))
+            s = "d%d" % ndma[0]
+            ndma[0] += 1
+            Q[q].dma_start(out[0], in_[0]).then_inc(T.sem[s], 16)
+            cnt[s] = 16
+            snaps[(s, 16)] = dict(known[q])
+            done.append((q, out, in_, s))
+        if more:
+            return done
+        for q, out, in_, s in done:
+            for regs, w in ((out[1], 1), (in_[1], 0)):
+                for n, lo, hi in regs:
+                    hist.setdefault(n, []).append((lo, hi, w, s, 16, q))
+
     def dma(q, out, in_):
-        wait_for(q, needs(q, in_[1], out[1]))
-        s = "d%d" % ndma[0]
-        ndma[0] += 1
-        Q[q].dma_start(out[0], in_[0]).then_inc(T.sem[s], 16)
-        cnt[s] = 16
-        note(q, in_[1], out[1], s, 16)
+        dmas([(q, out, in_)])
 
     def X(n, lo, hi, st=1, p0=0, p1=128):
         if n in PK:
@@ -224,8 +236,8 @@ def rank_program(g, core, T, topo):
     def toS(b, lo, m, n, c0, c1, s0=True, s1=True, k=None):
         js = []
         for q in range(16):
-            x = (X(n, c0 + q, c1, 16), [(n, c0, c1)]) if k is None else R(n, 0, k, c0 + q, c1, 16)
-            js.append((A(b, lo, lo + (c1 - c0) // 16), M(m, q, 128 if k is None else 8 * k), x, s0 and q == 0, s1 and q == 15))
+            x = (X(n, c0 + q, c1, 16), [(n, c0, c1)]) if k is None else R(n, k[0], k[1], c0 + q, c1, 16)
+            js.append((A(b, lo, lo + (c1 - c0) // 16), M(m, q, 128 if k is None else 8 * k[1]), x, s0 and q == 0, s1 and q == 15))
         mm(b, js)
 
     def toN(b, lo, w, m, n, c0, x0, x1, s0=True, s1=True, k=None):
@@ -233,8 +245,8 @@ def rank_program(g, core, T, topo):
         ps = sorted([p for p in ps if p[1] < p[2]], key=lambda p: p[1] - p[2])
         js = []
         for i, (q, a, z) in enumerate(ps):
-            x = A(n, c0 + a - x0, c0 + z - x0) if k is None else R(n, 0, k, c0 + a - x0, c0 + z - x0)
-            js.append((A(b, lo + a - w * q, lo + z - w * q), M(m, q, 128 if k is None else 8 * k), x, s0 and i == 0, s1 and i == len(ps) - 1))
+            x = A(n, c0 + a - x0, c0 + z - x0) if k is None else R(n, k[0], k[1], c0 + a - x0, c0 + z - x0)
+            js.append((A(b, lo + a - w * q, lo + z - w * q), M(m, q, 128 if k is None else 8 * k[1]), x, s0 and i == 0, s1 and i == len(ps) - 1))
         mm(b, js)
 
     def chosen(src, dst):
@@ -262,6 +274,7 @@ def rank_program(g, core, T, topo):
         return (T[n][:], [])
 
     PP, NW, WN = (V0, 2048), (96, 128), (128, 160)
+    KZ = ("zl", "zr", "zb")
 
     def L(t, i):
         return i * (NW[t] + 32) + (32 if i < 2 else 0)
@@ -269,109 +282,83 @@ def rank_program(g, core, T, topo):
     dma("Y", R("rsn", 0, 1, 0, 512), HB("snd"))
     for i, (q, n) in enumerate((("S", "lt"), ("Y", "rt"), ("S", "bs"))):
         dma(q, R("raw", i, i + 1, 0, V0), HB(n))
-    dma("Y", U(0, 16, 16 + V0), HB("err"))
-    dma("S", A("thi", 0, 1), HB("th"))
-    dma("S", A("wti", 0, 1), HB("wt"))
+    dma("S", U(0, 16, 16 + V0), HB("err"))
 
-    ms(A("ones", 0, 128), 1.0)
-    op("V", [lambda: g.vector.memset(T["km"][:], 0.0)], [], [(n, 0, 144) for n in MASKS])
+    def clear(a, z):
+        op("V", [lambda: g.vector.memset(T["km"][:, 144 * a:144 * z], 0.0)], [], [(n, 0, 144) for n in MASKS[a:z]])
     iota(A("pi", 0, 1), [[0, 1]], 0, 1, False)
-    iota(A("c160", 0, 160), [[1, 160]], 0, 0)
-    for a, n in enumerate(("zl", "zr", "zb", "zm")):
+    ms(A("ones", 0, 128), 1.0)
+    clear(0, 3)
+    for a, n in enumerate(KZ):
         sel((X(n, 0, 144, 16), [(n, 0, 144)]), A("ones", 0, 9), [[-1, 9]], OP.is_equal, 1 - 8 * a, 1)
-    ts(A("qi", 0, 1), A("pi", 0, 1), 15, OP.bitwise_and)
-    cp(A("qf", 0, 1), A("qi", 0, 1))
-    ts(A("qn", 0, 1), A("qi", 0, 1), 160, OP.mult, -1536, OP.add)
-    ts(A("meN", 0, 160), A("c160", 0, 160), A("qn", 0, 1), OP.add)
-    dma("Y", R("r16", 3, 4, 0, 2560), A("meN", 0, 160))
+    dma("Y", A("thi", 0, 1), HB("th"))
+    dma("Y", A("wti", 0, 1), HB("wt"))
     dma("Y", A("dtb", 0, 2048), HB("det"))
+    clear(3, 9)
     for a in (2, 0, 1, 3):
         n = "s%d" % a
         sel((X(n, 16, 144, 16), [(n, 0, 144)]), A("ones", 0, 8), [[-16, 8]], OP.is_equal, -a, 1)
     sel(A("eye", 0, 128), A("ones", 0, 128), [[-1, 128]], OP.is_equal, 0, 1)
+    iota(A("c160", 0, 160), [[1, 160]], 0, 0)
+    iota(A("mem0", 0, 384), [[0, 24], [16, 16]], 0, 0)
+    ts(A("qi", 0, 1), A("pi", 0, 1), 15, OP.bitwise_and)
     tt(A("ts0", 0, 128), A("zl", 16, 144), A("zr", 15, 143), OP.add)
-    tt(A("tsel", 0, 128), A("zb", 14, 142), A("zm", 13, 141), OP.add)
-    tt(A("tsel", 0, 128), A("tsel", 0, 128), A("ts0", 0, 128), OP.add)
-    for n in range(6):
-        ms(A("UU", US * n, US * n + 16), 0.0)
+    cp(A("qf", 0, 1), A("qi", 0, 1))
+    tt(A("tsel", 0, 128), A("zb", 14, 142), A("ts0", 0, 128), OP.add)
     for lo in (0, 272, 544):
         ms(A("snt", lo, lo + 16), -1.0)
-    ts(A("meS", 0, 160), A("c160", 0, 160), 16, OP.mult, A("qf", 0, 1), OP.add)
-    ms(U(0, 16 + V0, 16 + GH), 0.0)
 
     ts(R("sn16", 0, 1, 0, 512), R("rsn", 0, 1, 0, 512), -1536, OP.add)
-    toS("p4", 0, "zl", "sn16", 0, 512, k=1)
+    toS("p4", 0, "zl", "sn16", 0, 512, k=(0, 1))
     mm("p5", [(A("p5", 0, 512), M("zl", 2, 8), R("sn16", 0, 1, 0, 512), True, True)])
-    ts(A("snl", 0, 32), A("p4", 0, 32), 1536, OP.add)
 
-    def ghost0(qs):
+    def ghost0(t, qs):
         for q, s in zip(qs, order):
-            add(q, A("sb0", 256 * s, 256 * s + 256), ind(U(0, 16, 16 + GH), A("snl", 16 * s, 16 * s + 16)), 0)
+            add(q, A("sb0", 256 * s, 256 * s + 256), ind(U(0, 16, 16 + PP[t]), A("snl", 16 * s, 16 * s + 16)), 0)
             send(s, "0", A("sb0", 256 * s, 256 * s + 256), ghosts(0, 1 - s))
 
-    def table(t, qs):
-        for i, q in enumerate(qs):
-            b = "p%d" % i
-            mm(b, [(A(b, 0, 512), (X("tsel", 0, 128, 1, 0, 32), [("tsel", 0, 128)]), R("r16", 0, 4, 512 * i, 512 * i + 512), True, True)])
-            add(q, A("TB", 512 * i, 512 * i + 512), A(b, 0, 512), 1536)
-
-    def base_send(t):
-        P, nw = PP[t], NW[t]
-        toS("p6", nw, "zr", "r16", 0, P, k=3)
-        ts(A("gs", 0, 512), ind(A("TB", 0, P), A("snl", 0, 32)), -1536, OP.add)
-        toS("p4", 0, "s2", "gs", 0, 512)
+    def base_send(x):
         for s in order:
-            ts(A("bo", 16 * s, 16 * s + 16), A("p4", 16 * s, 16 * s + 16), 16 - 1024 - 256 * s, OP.add, 272, OP.min)
+            ts(A("bo", 16 * s, 16 * s + 16), A(x, 16 * s, 16 * s + 16), 16 - 1024 - 256 * s, OP.add, 272, OP.min)
             send(s, "b", A("bo", 16 * s, 16 * s + 16), A("gbo", 16 * (1 - s), 16 * (1 - s) + 16))
-        toS("p6", 0, "zl", "r16", 0, P, k=3)
-        toS("p7", 0, "s0", "gs", 0, 512)
-        toS("p7", 32, "s1", "gs", 0, 512)
-        toS("p6", 2 * nw, "zb", "r16", 0, P, k=3)
 
-    def lists(t):
-        P, nw = PP[t], NW[t]
+    def ghost_bases(qs):
+        for q, s in zip(qs, order[::-1]):
+            recv(s, "b", A("gbo", 16 * s, 16 * s + 16))
+            add(q, A("TB", GH + 256 * s, GH + 256 * s + 256), ind(A("snt", 272 * s, 272 * s + 288), A("gbo", 16 * s, 16 * s + 16)), 0)
+
+    def turn(t, i):
+        toS("p%d" % i, 0, KZ[i], "r16", 0, PP[t], k=(0, i + 1))
+
+    def wrapped(t, i):
+        nw = NW[t]
+        o = L(t, i)
+        ts(A("li", o, o + nw), A("p%d" % i, 0, nw), 1536, OP.add)
+        cp(A("st", o, o + nw), A("p%d" % i, 0, nw))
+
+    def slots(t):
+        ts(A("gs", 0, 512), ind(A("TB", 0, PP[t]), A("snl", 0, 32)), -1536, OP.add)
+
+    def slot_legs(t):
         for i in range(2):
-            cp(A("st", L(t, i) - 32, L(t, i)), A("p7", 32 * i, 32 * i + 32))
-        for i in range(3):
-            cp(A("st", L(t, i), L(t, i) + nw), A("p6", nw * i, nw * i + nw))
-        n = L(t, 2) + nw
-        ts(A("li", 0, n), A("st", 0, n), 1536, OP.add)
-        ts(A("pl", 0, nw), A("st", L(t, 2), n), 1536, OP.add, P - 1, OP.min)
+            toS("p7", 32 * i, "s%d" % i, "gs", 0, 512)
 
-    ghost0("SS")
-    for i in range(3):
-        ts(R("r16", 0, 3, 512 * i, 512 * i + 512), R("raw", 0, 3, 512 * i, 512 * i + 512), -1536, OP.add)
-    table(0, "SSV")
-    base_send(0)
-    for s in range(2):
-        act(A("snt", 16 + 272 * s, 272 + 272 * s), A("p5", 256 * s, 256 * s + 256), AF.Identity, bias=1536.0)
-    act(A("dtb", 0, 2048), A("dtb", 0, 2048), AF.Identity, bias=128.75, scale=0.5)
-    for n in range(1, 5):
-        dma("Y", U(n, 16 + V0, 16 + GH), U(0, 16 + V0, 16 + GH))
-    iota(A("TB", V0, GH), [[1, 1024]], V0, 0)
+    def slot_lists(t):
+        for i in range(2):
+            o = L(t, i) - 32
+            ts(A("li", o, o + 32), A("p7", 32 * i, 32 * i + 32), 1536, OP.add)
+            cp(A("st", o, o + 32), A("p7", 32 * i, 32 * i + 32))
 
-    cp(A("thf", 0, 1), A("thi", 0, 1))
-    ts(A("thb", 0, 1), A("thi", 0, 1), -1, OP.mult, 0.5, OP.add)
-    cp(A("wtf", 0, 1), A("wti", 0, 1))
-    ts(A("n4k", 0, 128), A("eye", 0, 128), -BIG, OP.mult)
-    ts(A("s2k", 0, 144), A("s2", 0, 144), BIG, OP.mult)
-    ts(A("s1k", 0, 144), A("s1", 0, 144), BIG, OP.mult)
-    cp(A("mem", 0, 16), A("meS", 0, 16))
-    for a, z in ((16, 32), (32, 64), (64, 128), (128, 256), (256, 384)):
-        cp(A("mem", a, z), A("mem", 0, z - a))
-    lists(0)
-
-    def marks(t, n, c, q):
-        nm, b = "in%d" % (n % 2), "p%d" % c
-        x = U(n, 16 + 512 * c, 16 + 512 * c + 512) if n < 5 else A("u5", 512 * c, 512 * c + 512)
-        o = A(nm, 512 * c, 512 * c + 512)
+    def marks(n, c, q, last=False):
+        o = A("in%d" % (n % 2), 512 * c, 512 * c + 512)
+        x = U(n, 16 + 512 * c, 16 + 512 * c + 512)
         if q == "V":
             ts(o, x, A("thf", 0, 1), OP.is_ge)
         else:
             act(o, x, AF.Sign, bias=A("thb", 0, 1))
-        one(b, 0, 512, "eye", o, n == 0, n == 5)
+        one("p%d" % c, 0, 512, "eye", o, n == 0, False)
 
-    MK = (("VVV", "VVV", "VVV", "VVS", "VVS", "VSV"), ("VVVV", "VVVV", "VVVV", "VVVS", "VVVS", "VSVS"))
+    MK = (("VVV", "VVV", "VVV", "VVV", "VVS"), ("VVVV", "VVVV", "VVVV", "VVVV", "VVVS"))
 
     def diff(q, n, i, t, c):
         o = L(t, i) + 16 * c
@@ -380,44 +367,53 @@ def rank_program(g, core, T, topo):
     def keep(b, lo, t, i, c0, c1, s1=False):
         mm(b, [(A(b, lo, lo + c1 - c0), A("eye", 0, 128), A("st", L(t, i) + c0, L(t, i) + c1), False, s1)])
 
-    def prep(t):
+    def UL(t, i, c0, c1):
+        nw = NW[t]
+        o = 32 * i + 32 + c0 if c0 < 0 else 64 + 64 * i + c0 if c0 < 64 else 192 + (nw - 64) * i + c0 - 64
+        return A("ul", o, o + c1 - c0)
+
+    def prep(t, first, mine):
         P, nw = PP[t], NW[t]
-        h, nc = nw // 2, P // 256
-        one("p4", 0, 64, "n4k", A("ones", 0, 64), True, False)
-        for i in range(2):
-            keep("p4", 32 * i, t, i, -32, 0)
-        for k in range(2):
-            b = "p%d" % (5 + k)
-            one(b, 0, nw, "n4k", A("mem", 0, nw), True, False)
+        nc, h = P // 256, nw - 64
+
+        def slot_flags():
+            one("p4", 0, 64, "n4k", A("ones", 0, 64), True, False)
             for i in range(2):
-                keep(b, h * i, t, i, h * k, h * k + h)
-        for q, s in zip("VS", order[::-1]):
-            recv(s, "b", A("gbo", 16 * s, 16 * s + 16))
-            add(q, A("TB", GH + 256 * s, GH + 256 * s + 256), ind(A("snt", 272 * s, 272 * s + 288), A("gbo", 16 * s, 16 * s + 16)), 0)
-        for c in range(nc // 2):
+                keep("p4", 32 * i, t, i, -32, 0)
+            for i in range(2):
+                for s in range(2):
+                    o = L(t, i) - 32 + 16 * s
+                    tt(A("fs", 512 * i + 256 * s, 512 * i + 256 * s + 256), ind(A("TB", 0, 3072), A("li", o, o + 16)),
+                       A("snt", 16 + 272 * s, 272 + 272 * s), OP.is_equal)
+                toS("p4", 32 * i, "s2k", "fs", 512 * i, 512 * i + 512, False, i == 1)
+        for c in range(nc):
             diff("S", "dL", 0, t, c)
-        for i in range(2):
-            for s in range(2):
-                o = L(t, i) - 32 + 16 * s
-                tt(A("fs", 512 * i + 256 * s, 512 * i + 256 * s + 256), ind(A("TB", 0, 3072), A("li", o, o + 16)),
-                   A("snt", 16 + 272 * s, 272 + 272 * s), OP.is_equal)
-            toS("p4", 32 * i, "s2k", "fs", 512 * i, 512 * i + 512, False, i == 1)
-        toS("p5", 0, "s2k", "dL", 0, P // 2, False, False)
-        for c in range(nc // 2, nc):
-            diff("S", "dL", 0, t, c)
-        for c in range(nc // 2):
+        for c in range(mine, nc):
+            diff("S", "dR", 1, t, c)
+        for b, c0, c1 in (("p5", 0, 64), ("p6", 64, nw)):
+            one(b, 0, 2 * (c1 - c0), "n4k", A("mem", 0, 2 * (c1 - c0)), True, False)
+            for i in range(2):
+                keep(b, (c1 - c0) * i, t, i, c0, c1)
+        if first:
+            slot_flags()
+        for c in range(4):
             diff("V", "dR", 1, t, c)
-        toS("p5", h, "s2k", "dR", 0, P // 2, False, True)
-        toS("p6", 0, "s2k", "dL", P // 2, P, False, False)
-        for c in range(nc // 2, nc):
-            diff("V" if c < nc - 2 else "S", "dR", 1, t, c)
-        toS("p6", h, "s2k", "dR", P // 2, P, False, True)
+        toS("p5", 0, "s2k", "dL", 0, 1024, False, False)
+        toS("p5", 64, "s2k", "dR", 0, 1024, False, True)
+        if not first:
+            yield
+            slot_flags()
+        for c in range(4, mine):
+            diff("V", "dR", 1, t, c)
+        toS("p6", 0, "s2k", "dL", 1024, P, False, False)
+        toS("p6", h, "s2k", "dR", 1024, P, False, True)
+        ts(A("ul", 64, 192), A("p5", 0, 128), 1552, OP.add, US, OP.min)
         ts(A("ul", 0, 64), A("p4", 0, 64), 1552, OP.add, US, OP.min)
-        ts(A("ul", 64, 64 + nw), A("p5", 0, nw), 1552, OP.add, US, OP.min)
+        yield
 
     def depths(t, slack):
         P, nw = PP[t], NW[t]
-        H, h = P // 2, nw // 2
+        nc = P // 512
         for n in range(5):
             gr = "gr%d" % (n % 2)
             win = U(n, 0, US + 16)
@@ -425,24 +421,39 @@ def rank_program(g, core, T, topo):
                 recv(s, str(n), ghosts(n, s))
             if n < 4:
                 for s in order:
-                    act(A(gr, 256 * s, 256 * s + 256), ind(win, A("ul", 32 + 16 * s, 48 + 16 * s)))
+                    act(A(gr, 256 * s, 256 * s + 256), ind(win, UL(t, 1, 16 * s - 32, 16 * s - 16)))
+            for c, q in enumerate(MK[t][n]):
+                if q == "V":
+                    marks(n, c, q)
+            if n < 4:
                 for s in order:
                     o = A("sb%d" % (n + 1), 256 * s, 256 * s + 256)
-                    tt(o, ind(win, A("ul", 16 * s, 16 * s + 16)), A(gr, 256 * s, 256 * s + 256), OP.max)
+                    tt(o, ind(win, UL(t, 0, 16 * s - 32, 16 * s - 16)), A(gr, 256 * s, 256 * s + 256), OP.max)
                     send(s, str(n + 1), o, ghosts(n + 1, 1 - s))
             if n == 0:
-                ts(A("ul", 64 + nw, 64 + 2 * nw), A("p6", 0, nw), 1552, OP.add, US, OP.min)
-            for k in range(2):
-                c = 64 + nw * k + h
-                act(A(gr, 512 + H * k, 512 + H * k + H), ind(win, A("ul", c, c + h)))
-            for k in range(2):
-                o = U(n + 1, 16 + H * k, 16 + H * k + H) if n < 4 else A("u5", H * k, H * k + H)
-                c = 64 + nw * k
-                tt(o, ind(win, A("ul", c, c + h)), A(gr, 512 + H * k, 512 + H * k + H), OP.max)
+                ts(A("ul", 192, 64 + 2 * nw), A("p6", 0, 2 * nw - 128), 1552, OP.add, US, OP.min)
+            if n == 4:
+                for c, q in enumerate(MK[t][n]):
+                    if q == "S":
+                        marks(n, c, q)
+            for c in range(nc):
+                r, x = A(gr, 512 + 512 * c, 1024 + 512 * c), ind(win, UL(t, 1, 32 * c, 32 * c + 32))
+                y = ind(win, UL(t, 0, 32 * c, 32 * c + 32))
+                if n < 4:
+                    act(r, x)
+                    tt(U(n + 1, 16 + 512 * c, 16 + 512 * c + 512), y, r, OP.max)
+                else:
+                    o = A("in1", 512 * c, 512 * c + 512)
+                    act(r, x, AF.Sign, bias=A("thb", 0, 1))
+                    ts(o, y, A("thf", 0, 1), OP.is_ge)
+                    one("p%d" % c, 0, 512, "eye", r, False, False)
+                    one("p%d" % c, 0, 512, "eye", o, False, True)
+            if n < 4:
+                for c, q in enumerate(MK[t][n]):
+                    if q == "S":
+                        marks(n, c, q)
             for f in slack.get(n, []):
                 f()
-            for c, q in enumerate(MK[t][n + 1]):
-                marks(t, n + 1, c, q)
 
     def flags0(t):
         P, nw = PP[t], NW[t]
@@ -456,28 +467,32 @@ def rank_program(g, core, T, topo):
         for c in range(c0, c1):
             diff("S", "dB", 2, t, c)
 
+    def pens(t):
+        P, nw = PP[t], NW[t]
+        b = A("st", L(t, 2), L(t, 2) + nw)
+        ts(A("pl", 0, nw), b, 1536, OP.add, P - 1, OP.min)
+        ts(A("pen", nw, 2 * nw), b, GH - 1536, OP.is_ge)
+        tt(A("pen", 2 * nw, 3 * nw), A("me16", 0, nw), b, OP.is_ge)
+
     def flags1(t):
         P, nw = PP[t], NW[t]
         one("p5", 0, nw, "n4k", A("mem", 0, nw), True, False)
         toS("p5", 0, "s2k", "dB", 0, P, False, True)
         toS("p7", 2 * nw, "s1k", "dB", 0, P, False, True)
-        b = A("st", L(t, 2), L(t, 2) + nw)
-        ts(A("pen", nw, 2 * nw), b, GH - 1536, OP.is_ge)
-        tt(A("pen", 2 * nw, 3 * nw), A("me16", 0, nw), b, OP.is_ge)
 
     def flags2(t):
         nw = NW[t]
         ts(A("pen", 0, nw), A("p5", 0, nw), 0, OP.not_equal)
         ts(A("lf", 0, 3 * nw), A("p7", 0, 3 * nw), 1552, OP.add, 16 + GH, OP.min)
+        one("p4", 0, nw, "n64", A("pen", 0, nw), True, False)
+        for i in (1, 2):
+            one("p4", 0, nw, "n64", A("pen", nw * i, nw * i + nw), False, False)
 
     def olds(t):
         P, w = PP[t], WN[t]
-        for i, m in enumerate(("zl", "zr", "zb")):
-            toN("p6", w * i, w, m, "r16", 0, 0, P, k=3)
-        for i in range(3):
-            act(A("old", w * i, w * i + 128), A("p6", w * i, w * i + 128), AF.Identity, bias=A("bq", t, t + 1))
-            if w > 128:
-                act(A("old", w * i + 128, w * i + w), A("p6", w * i + 128, w * i + w), AF.Identity, bias=A("bq", 0, 1))
+        one("p6", 0, 3 * w, "za", A("dtb", 0, 3 * w), True, False)
+        for i, m in enumerate(KZ):
+            toN("p6", w * i, w, m, "r16", 0, 0, P, False, False, k=(0, i + 1))
 
     def codes(t):
         ts(A("jb", 0, 1), A("pq", 0, 1), PP[t], OP.mult, A("pq", 3, 4), OP.add)
@@ -488,47 +503,37 @@ def rank_program(g, core, T, topo):
     def splits(t):
         P, nw = PP[t], NW[t]
         nc, k = P // 512, nw // 16
-        who = ["VS"[c % 2] for c in range(nc)]
-        for c in range(nc):
-            lift = sum(MK[t][n][c] == "S" for n in range(6))
-            if nc == 3 and c == 2:
-                for e in range(2):
-                    add("VS"[e], A("in0", 1024 + 256 * e, 1280 + 256 * e), A("p2", 256 * e, 256 * e + 256), lift)
-            else:
-                add(who[c], A("in0", 512 * c, 512 * c + 512), A("p%d" % c, 0, 512), lift)
-        one("p4", 0, nw, "n64", A("pen", 0, nw), True, False)
-        for i in (1, 2):
-            one("p4", 0, nw, "n64", A("pen", nw * i, nw * i + nw), False, False)
-        parts = [(q, 256 * c, 256 * c + 256) for c, q in enumerate("VS" * nc)]
-        for q, lo, hi in parts:
-            add(q, A("gr0", lo, hi), ind(A("in0", 0, P), A("pl", lo // 16, hi // 16)), 0)
+        halves = [("VS"[c % 2], c, 0, 512) for c in range(nc)] if nc % 2 == 0 else [("V", 0, 0, 512), ("S", 1, 0, 512), ("V", 2, 0, 256), ("S", 2, 256, 512)]
+        for q, c, lo, hi in halves:
+            lift = 1 + sum(MK[t][n][c] == "S" for n in range(5))
+            add(q, A("in0", 512 * c + lo, 512 * c + hi), A("p%d" % c, lo, hi), lift)
+        for c, q in enumerate("VS" * nc):
+            add(q, A("gr1", 256 * c, 256 * c + 256), ind(A("in0", 0, P), A("pl", 16 * c, 16 * c + 16)), 0)
         for c in range(nc):
             b = "p%d" % c
-            mm(b, [(A(b, 0, 512), A("eye", 0, 128), A(n, 512 * c, 512 * c + 512), n == "in0", n == "gr0") for n in ("in0", "gr0")])
-        for c in range(nc):
-            b, o = A("p%d" % c, 0, 512), A("in1", 512 * c, 512 * c + 512)
-            if who[c] == "S":
+            mm(b, [(A(b, 0, 512), A("eye", 0, 128), A(n, 512 * c, 512 * c + 512), n == "in0", n == "gr1") for n in ("in0", "gr1")])
+        for q, c, lo, hi in halves:
+            b, o = A("p%d" % c, lo, hi), A("in1", 512 * c + lo, 512 * c + hi)
+            if q == "S":
                 act(o, b, AF.Sign)
             else:
                 ts(o, b, 0, OP.is_gt)
-        cut = 1024
-        toS("p4", 0, "cq", "in1", 0, cut, False, False)
-        toS("p4", cut // 16, "cq", "in1", cut, P, False, True)
+        toS("p4", 0, "cq", "in1", 0, 1024, False, False)
+        toS("p4", 64, "cq", "in1", 1024, P, False, True)
         go = A("go", 0, nw)
         ts(go, A("p4", 0, nw), 11, OP.is_ge)
         one("p5", 0, nw, "blk", go)
-        one("p6", 0, k, "eye", A("d16", 0, k), True, False)
-        toS("p6", 0, "ncq", "go", 0, nw, False, True)
+        one("p5", nw, 2 * nw, "eye", A("d16", 0, nw), True, False)
+        one("p5", nw, 2 * nw, "nblk", go, False, True)
         for e, x in enumerate((A("me16", 0, nw), A("st", L(t, 2), L(t, 2) + nw))):
             mm("p7", [(A("p7", nw * e, nw * e + nw), A("eye", 0, 128), x, True, False), (A("p7", nw * e, nw * e + nw), A("lt", 0, 128), go, False, True)])
         scan(A("inc", 1, nw + 1), A("p5", 0, nw), A("zer", 0, nw), OP.add, OP.add)
-        act(A("ee", 0, k), A("p6", 0, k), AF.Relu)
+        tt(A("ofr", 0, nw), A("inc", 0, nw), A("p5", nw, 2 * nw), OP.max)
         act(A("val", 0, 2 * nw), A("p7", 0, 2 * nw), AF.Identity, bias=1537.0 - 32 * BIG)
-        toS("p4", 0, "s0", "inc", 0, nw, True, False)
-        one("p4", 0, k, "eye", A("ee", 0, k), False, True)
+        toS("p4", 0, "s0", "ofr", 0, nw)
         cp(A("off", 0, k), A("p4", 0, k))
         for e in range(2):
-            scat(A("Z%d" % e, 0, 3072), A("off", 0, k), A("val", nw * e, nw * e + nw))
+            scat(A("Z%d" % e, 0, 1152), A("off", 0, k), A("val", nw * e, nw * e + nw))
         for e in range(2):
             scan(A("sc", 256 * e, 256 * e + 256), A("m4k", 0, 256), A("Z%d" % e, 0, 256), OP.add, OP.max)
         ts(A("y16", 0, 512), A("sc", 0, 512), 0, OP.max, BIG, OP.min)
@@ -549,55 +554,117 @@ def rank_program(g, core, T, topo):
         cp(A("eo", 0, 32), A("hz2", 0, 32))
         ts(A("eo", 32, 64), A("hb", 0, 32), 2048, OP.min)
 
-    def children(t):
+    def children(t, qs):
         P = PP[t]
-        tt(A("cT", 0, 512), ind(A("dtb", 0, 2064), A("eo", 0, 32)), A("e2b", 0, 512), OP.add)
+        def child(q, i, out):
+            x = ind(A("dtb", 0, 2064), A("eo", 32 * i, 32 * i + 32))
+            if q == "V":
+                tt(out, x, A("e2b", 0, 512), OP.add)
+            else:
+                y, b = A("vs", 512 * i, 512 * i + 512), "p%d" % (3 * i)
+                act(y, x)
+                one(b, 0, 512, "eye", A("e2", 0, 512), True, False)
+                one(b, 0, 512, "eye", y, False, True)
+                act(out, A(b, 0, 512), AF.Identity, bias=-258.0)
+        child(qs[0], 0, A("cT", 0, 512))
+        yield
         scat(U(0, 16, 16 + P + 512), A("TL", 0, 32), A("cT", 0, 512))
-        tt(U(0, 16 + P, 16 + P + 512), ind(A("dtb", 0, 2064), A("eo", 32, 64)), A("e2b", 0, 512), OP.add)
+        yield
+        child(qs[1], 1, U(0, 16 + P, 16 + P + 512))
+        yield
 
-    def update(t, cut):
-        P, nw, w = PP[t], NW[t], WN[t]
+    NTW = A("NT", 0, 2592)
+
+    def rename(q, t, n, i, c0, c1):
+        add(q, A(n, 16 * c0, 16 * c1), ind(NTW, A("lf", NW[t] * i + c0, NW[t] * i + c1)), 0)
+
+    def heads(t):
+        P, w = PP[t], WN[t]
         tl = A("TL", 0, 32)
         scat(A("NT", 16, 16 + P + 512), tl, A("jr", 0, 512))
-        act(A("gf", 0, 512), ind(A("TB", 0, P + 512), tl))
         act(A("eT", 0, 512), ind(U(0, 16, 16 + P + 512), tl))
-        win = A("NT", 0, 2592)
-        if t == 0:
-            act(A("vs", 0, 512), ind(win, A("snf", 0, 32)))
-        act(A("vR", 0, P), ind(win, A("lf", nw, 2 * nw)))
-        cp(A("vL", 0, P), ind(win, A("lf", 0, nw)))
-        toN("p0", 0, w, "f1", "gf", 0, P, P + 512)
-        one("p1", 0, 3 * w, "za", A("jr", 0, 3 * w), True, False)
-        toN("p1", 0, w, "f2", "gf", 0, P, P + 512, False, False)
-        toN("p1", w, w, "f3", "gf", 0, P, P + 512, False, False)
+        act(A("e2", 0, 512), A("eT", 0, 512), AF.Identity, bias=128.75, scale=0.5)
         toS("p3", 0, "wq", "eT", 0, 512)
+
+    def news(t):
+        P, w = PP[t], WN[t]
+        ts(A("gf", 0, 512), ind(A("TB", 0, P + 512), A("TL", 0, 32)), -1536, OP.add)
+        for i, m in enumerate(("s2", "s3", "s1")):
+            toN("p6", w * i, w, m, "gf", 0, P, P + 512, False, i == 2)
+
+    def owns(t):
+        P, w = PP[t], WN[t]
         toN("p2", 0, w, "wn", "NT", 16, 0, P)
         toN("p2", w, w, "cq", "NT", 16, 0, P)
-        if t == 0:
-            toS("p4", 0, "wn", "vs", 0, 512)
-            mm("p5", [(A("p5", 0, 512), M("wn", 2), A("vs", 0, 512), True, True)])
-        act(A("vy", 0, 512), ind(A("vR", 0, P + 512), tl))
-        if cut < nw:
-            act(A("vB", 16 * cut, P), ind(win, A("lf", 2 * nw + cut, 3 * nw)))
-        cp(A("vB", 0, 16 * cut), ind(win, A("lf", 2 * nw, 2 * nw + cut)))
-        act(A("e2", 0, 512), A("eT", 0, 512), AF.Identity, bias=128.75, scale=0.5)
-        act(A("e2b", 0, 512), A("e2", 0, 512), AF.Identity, bias=-258.0)
-        toN("p1", w, w, "wn", "vR", 0, 0, P, False, False)
-        toN("p1", 0, w, "wn", "vL", 0, 0, P, False, False)
-        toN("p1", 2 * w, w, "wn", "vy", 0, P, P + 512, False, False)
-        toN("p1", 2 * w, w, "wn", "vB", 0, 0, P, False, True)
-        tt(A("old", 2 * w, 3 * w), A("old", 2 * w, 3 * w), A("p0", 0, w), OP.add)
+
+    def right_bases(t):
+        P, w = PP[t], WN[t]
+        act(A("vy", 0, 512), ind(A("vR", 0, P + 512), A("TL", 0, 32)))
+
+    def turnN(t, n, i):
+        P, w = PP[t], WN[t]
+        toN("p1", i * w, w, "wn", n, 0, 0, P, True, i < 2)
+        if i == 2:
+            toN("p1", 2 * w, w, "wn", "vy", 0, P, P + 512, False, True)
+
+    def early(t):
+        w = WN[t]
+        act(A("old", 0, 3 * w), A("p6", 0, 3 * w), AF.Identity, bias=1536.0)
         ts(A("nsp", 0, 2 * w), A("p2", 0, 2 * w), 0, OP.is_equal)
-        yield
+
+    def update(t):
+        w = WN[t]
         tt(A("lrb", 0, 3 * w), A("old", 0, 3 * w), A("p1", 0, 3 * w), OP.max)
-        tt(A("ub", 0, w), A("lrb", 2 * w, 3 * w), A("lrb", 0, w), OP.subtract)
         tt(A("ua", 0, 2 * w), A("lrb", 0, 2 * w), A("nsp", 0, 2 * w), OP.mult)
-        tt(A("uc", 0, w), A("ub", 0, w), A("nsp", 0, w), OP.mult)
+        tt(A("nsp", 2 * w, 3 * w), A("lrb", 2 * w, 3 * w), A("lrb", 0, w), OP.subtract)
         tt(A("new", 0, 2 * w), A("ua", 0, 2 * w), A("p2", 0, 2 * w), OP.add)
-        tt(A("new", 2 * w, 3 * w), A("uc", 0, w), A("lrb", 0, w), OP.add)
+        yield
+        tt(A("ua", 2 * w, 3 * w), A("nsp", 2 * w, 3 * w), A("nsp", 0, w), OP.mult)
+        tt(A("new", 2 * w, 3 * w), A("ua", 2 * w, 3 * w), A("lrb", 0, w), OP.add)
         yield
 
+    ts(R("r16", 0, 3, 0, 512), R("raw", 0, 3, 0, 512), -1536, OP.add)
+    ts(A("snl", 0, 32), A("p4", 0, 32), 1536, OP.add)
+    ghost0(0, "SS")
+    for i in (1, 2):
+        ts(R("r16", 0, 3, 512 * i, 512 * i + 512), R("raw", 0, 3, 512 * i, 512 * i + 512), -1536, OP.add)
+    for i, q in enumerate("VSV"):
+        b = "p%d" % i
+        mm(b, [(A(b, 0, 512), (X("tsel", 0, 128, 1, 0, 24), [("tsel", 0, 128)]), R("r16", 0, 3, 512 * i, 512 * i + 512), True, True)])
+        add(q, A("TB", 512 * i, 512 * i + 512), A(b, 0, 512), 1536)
+    turn(0, 0)
+    slots(0)
+    toS("p4", 0, "s2", "gs", 0, 512)
+    base_send("p4")
+    slot_legs(0)
+    turn(0, 1)
+    turn(0, 2)
+    for s in range(2):
+        act(A("snt", 16 + 272 * s, 272 + 272 * s), A("p5", 256 * s, 256 * s + 256), AF.Identity, bias=1536.0)
+    act(A("n4k", 0, 128), A("eye", 0, 128), scale=-BIG)
+    act(A("s2k", 0, 144), A("s2", 0, 144), scale=BIG)
+    act(A("mem", 0, 384), A("mem0", 0, 384), AF.Identity, bias=A("qf", 0, 1))
+    act(A("b0", 0, 32), A("p4", 0, 32))
+    act(A("dtb", 0, 2048), A("dtb", 0, 2048), AF.Identity, bias=128.75, scale=0.5)
+    iota(A("TB", V0, GH), [[1, 1024]], V0, 0)
     iota(A("ik", 0, 16), [[-1, 16]], 16, 1, False)
+    ms(U(0, 16 + V0, 16 + GH), 0.0)
+    wrapped(0, 0)
+    slot_lists(0)
+    wrapped(0, 1)
+    for n in range(6):
+        ms(A("UU", US * n, US * n + 16), 0.0)
+    cp(A("thf", 0, 1), A("thi", 0, 1))
+    ts(A("thb", 0, 1), A("thi", 0, 1), -1, OP.mult, 0.5, OP.add)
+    cp(A("wtf", 0, 1), A("wti", 0, 1))
+    ts(A("meS", 0, 160), A("c160", 0, 160), 16, OP.mult, A("qf", 0, 1), OP.add)
+    wrapped(0, 2)
+    ghost_bases("VS")
+    wait_for("Y", needs("Y", A("gbo", 0, 32)[1], []))
+    for n in range(1, 5):
+        dma("Y", U(n, 16 + V0, 16 + GH), U(0, 16 + V0, 16 + GH))
+    for _ in prep(0, True, 4):
+        pass
     sel((X("za", 16, 144, 16), [("za", 0, 144)]), A("ones", 0, 8), [[-16, 8]], OP.is_ge, 0, 1)
     sel((X("cq", 16, 144, 16), [("cq", 0, 144)]), (X("za", 16, 144, 16), [("za", 0, 144)]), [[16, 8]], OP.is_ge, 15, -1)
     sel(A("blka", 0, 128), A("ones", 0, 128), [[-16, 8], [0, 16]], OP.is_ge, 0, 1)
@@ -607,83 +674,132 @@ def rank_program(g, core, T, topo):
     fill("za", 0, 144)
     fill("dtb", 2048, 2064, 129)
     fill("zer", 0, 128)
-    fill("m4k", 0, 256, -4096)
-    cp(A("snS", 0, 32), A("snl", 0, 32))
-    ts(A("slc", 0, 32), A("meS", 0, 32), GH - 1536, OP.add)
-    cp(A("sn0", 0, 32), A("snl", 0, 32))
-    one("p3", 0, 32, "eye", A("snS", 0, 32), True, False)
-    one("p3", 0, 32, "n4k", A("slc", 0, 32), False, False)
-    toS("p3", 0, "s1k", "gs", 0, 512, False, True)
-    ts(A("snf", 0, 32), A("p3", 0, 32), 16, OP.add, 16 + GH, OP.min)
-    for c, q in enumerate(MK[0][0]):
-        marks(0, 0, c, q)
-    prep(0)
 
     def late0():
-        ts(A("me16", 0, 128), A("meS", 0, 128), -1536, OP.add)
-        ts(A("d16", 0, 8), A("meS", 0, 8), 8, OP.mult, 1024, OP.add)
+        act(A("s1k", 0, 144), A("s1", 0, 144), scale=BIG)
         ts(A("ik2", 0, 16), A("ik", 0, 16), 15, OP.bitwise_and)
-        ts(A("inc", 0, 1), A("zer", 0, 1), 0, OP.add)
+        ts(A("me16", 0, 128), A("meS", 0, 128), -1536, OP.add)
         ts(A("pq", 0, 16), A("ik2", 0, 16), 0, OP.is_equal)
-        for t in range(2):
-            ts(A("bq", t, t + 1), A("qf", 0, 1), 12 + t, OP.is_lt, 1536, OP.mult)
-        ts(A("n3", 0, 1), A("qf", 0, 1), 3, OP.not_equal)
-        tt(A("jb", 2, 3), A("pq", 2, 3), A("pq", 3, 4), OP.subtract)
+        ts(A("slc", 0, 32), A("meS", 0, 32), GH - 1536, OP.add)
+        cp(A("snS", 0, 32), A("snl", 0, 32))
 
     def late1():
-        for a in (1, 2, 3):
-            act(A("f%d" % a, 0, 144), A("s%d" % a, 0, 144))
+        ts(A("d16", 0, 128), A("c160", 0, 128), 1024, OP.add)
+        ts(A("inc", 0, 1), A("zer", 0, 1), 0, OP.add)
+        ts(A("n3", 0, 1), A("qf", 0, 1), 3, OP.not_equal)
+        tt(A("jb", 2, 3), A("pq", 2, 3), A("pq", 3, 4), OP.subtract)
+        one("p3", 0, 32, "eye", A("snS", 0, 32), True, False)
+        one("p3", 0, 32, "n4k", A("slc", 0, 32), False, False)
+        toS("p3", 0, "s1k", "gs", 0, 512, False, True)
+        act(A("n64", 0, 128), A("eye", 0, 128), scale=-64.0)
+        act(A("qn", 0, 1), A("qf", 0, 1), scale=96.0)
+        act(A("meN", 0, 96), A("c160", 0, 96), AF.Identity, bias=A("qn", 0, 1))
+
+    def late2():
+        dma("Y", (T["TB"][3:128:16, 0:V0], [("TB", 0, V0)]), A("meN", 0, 96))
         act(A("wn", 0, 144), A("cq", 0, 144), scale=A("n3", 0, 1))
         act(A("wq", 0, 144), A("cq", 0, 144), scale=A("wtf", 0, 1))
-        act(A("ncq", 0, 144), A("cq", 0, 144), scale=-BIG)
-        act(A("n64", 0, 128), A("eye", 0, 128), scale=-64.0)
+        act(A("nblk", 0, 128), A("blk", 0, 128), scale=-BIG)
         act(A("blka", 0, 128), A("eye", 0, 128), scale=32 * BIG)
         act(A("tri", 0, 128), A("tri", 0, 128), scale=BIG)
+        ts(A("snf", 0, 32), A("p3", 0, 32), 16, OP.add, 16 + GH, OP.min)
+        cp(A("sn0", 0, 32), A("snl", 0, 32))
+        tt(A("dl", 0, 32), A("st", 0, 32), A("b0", 0, 32), OP.subtract)
+        tt(A("dl", 32, 64), A("slc", 0, 32), A("st", 0, 32), OP.subtract)
         tt(A("lt", 0, 128), A("tri", 0, 128), A("blka", 0, 128), OP.add)
 
     def zs():
         for e in range(2):
             fill("Z%d" % e, 0, 256)
 
-    nc = 6
     depths(0, {0: [late0, lambda: flags0(0), lambda: bases(0, 0, 2), lambda: fill("NT", 0, 1024)],
-               1: [lambda: bases(0, 2, 4), lambda: fill("NT", 1024, 2048), lambda: codes(0)],
-               2: [lambda: bases(0, 4, 6), lambda: flags1(0), lambda: fill("NT", 2048, 2592), zs],
-               3: [late1, lambda: flags2(0), lambda: fill("vR", V0, GH)],
-               4: [lambda: olds(0)]})
+               1: [lambda: bases(0, 2, 4), lambda: fill("NT", 1024, 2048), late1, lambda: pens(0), lambda: olds(0)],
+               2: [lambda: bases(0, 4, 6), lambda: flags1(0), lambda: fill("NT", 2048, 2592), zs, lambda: codes(0)],
+               3: [late2, lambda: flags2(0), lambda: fill("vR", V0, GH), lambda: fill("m4k", 0, 256, -4096)]})
     splits(0)
-    un = update(0, 40)
-    next(un)
-    tt(A("sn1", 0, 32), A("sn0", 0, 32), A("p4", 0, 32), OP.max)
+    heads(0)
+    act(A("vs", 0, 512), ind(A("NT", 16, 16 + V0), A("snl", 0, 32)))
+    act(A("vs", 512, 1024), ind(NTW, A("snf", 0, 32)))
+    rename("V", 0, "vR", 1, 0, 96)
+    owns(0)
+    for i in range(2):
+        toS("p4", 32 * i, "wn", "vs", 512 * i, 512 * i + 512)
+    mm("p5", [(A("p5", 0, 512), M("wn", 2), A("vs", 512, 1024), True, True)])
+    rename("S", 0, "vB", 2, 0, 96)
+    news(0)
+    turnN(0, "vR", 1)
+    right_bases(0)
+    rename("S", 0, "vL", 0, 64, 96)
+    rename("V", 0, "vL", 0, 0, 64)
+    ts(A("sp", 0, 64), A("p4", 0, 64), 0, OP.is_gt)
+    tt(A("sn1", 0, 32), A("sn0", 0, 32), A("p4", 32, 64), OP.max)
+    tt(A("bx", 0, 64), A("sp", 0, 64), A("dl", 0, 64), OP.mult)
     cp(A("snl", 0, 32), A("sn1", 0, 32))
+    tt(A("sp", 0, 32), A("bx", 0, 32), A("bx", 32, 64), OP.add)
+    early(0)
+    tt(A("bx", 0, 32), A("sp", 0, 32), A("b0", 0, 32), OP.add)
+    base_send("bx")
+    turnN(0, "vB", 2)
+    turnN(0, "vL", 0)
+    weigh(0)
+    ch = children(0, "SS")
+    next(ch)
+    un = update(0)
     next(un)
-    ts(A("n16", 0, 384), A("new", 0, 384), -1536, OP.add)
-    for i in range(3):
-        dma("Y", R("r16", i, i + 1, 0, 2048), A("n16", 128 * i, 128 * i + 128))
+
+    def rows(i):
+        return (T["TB"][i:128:16, 0:2048], [("TB", 0, 2048)])
+    held = dmas([("Y", rows(i), A("new", 128 * i, 128 * i + 128)) for i in range(2)], more=True)
+    ts(A("n16", 0, 256), A("new", 0, 256), -1536, OP.add)
+    dma("Y", R("r16", 0, 1, 0, 2048), A("n16", 0, 128))
+    next(un)
+    dmas([("Y", rows(2), A("new", 256, 384))], held)
+    dma("Y", R("r16", 1, 2, 0, 2048), A("n16", 128, 256))
+    ts(A("n16", 256, 384), A("new", 256, 384), -1536, OP.add)
+    dma("Y", R("r16", 2, 3, 0, 2048), A("n16", 256, 384))
     for s in range(2):
         x = A("snt", 16 + 272 * s, 272 + 272 * s)
         tt(x, x, A("p5", 256 * s, 256 * s + 256), OP.max)
-    weigh(0)
-    children(0)
-    table(1, "SSSV")
-    base_send(1)
-    ghost0("SS")
-    lists(1)
-    for c, q in enumerate(MK[1][0]):
-        marks(1, 0, c, q)
-    prep(1)
-    depths(1, {0: [lambda: flags0(1), lambda: bases(1, 0, 3), lambda: fill("NT", 16, 1040)],
-               1: [lambda: bases(1, 3, 6), lambda: fill("NT", 1040, 2064), lambda: codes(1)],
-               2: [lambda: bases(1, 6, 8), lambda: flags1(1), zs],
-               3: [lambda: flags2(1)],
-               4: [lambda: olds(1)]})
+    next(ch)
+    ghost_bases("SS")
+    next(ch)
+    ghost0(1, "SS")
+    for i in range(3):
+        turn(1, i)
+    wrapped(1, 0)
+    slots(1)
+    wrapped(1, 1)
+    slot_legs(1)
+    pr = prep(1, False, 5)
+    next(pr)
+    slot_lists(1)
+    wrapped(1, 2)
+    next(pr)
+    depths(1, {0: [lambda: flags0(1), lambda: bases(1, 0, 2), lambda: fill("NT", 16, 1040), lambda: olds(1)],
+               1: [lambda: bases(1, 2, 5), lambda: fill("NT", 1040, 2064), lambda: pens(1)],
+               2: [lambda: bases(1, 5, 8), lambda: flags1(1), zs, lambda: codes(1)],
+               3: [lambda: flags2(1)]})
     splits(1)
-    un = update(1, 32)
-    next(un)
+    heads(1)
+    act(A("e2b", 0, 512), A("e2", 0, 512), AF.Identity, bias=-258.0)
+    news(1)
+    rename("S", 1, "vR", 1, 0, 128)
+    rename("V", 1, "vL", 0, 0, 128)
+    owns(1)
+    right_bases(1)
+    rename("S", 1, "vB", 2, 0, 128)
+    turnN(1, "vL", 0)
+    turnN(1, "vR", 1)
+    turnN(1, "vB", 2)
     weigh(1)
-    children(1)
+    for _ in children(1, "VV"):
+        pass
     dma("Y", HB("ye"), U(0, 16, 16 + GH))
+    early(1)
+    un = update(1)
     next(un)
-    for i, n in ((0, "yl"), (1, "yr"), (2, "yb")):
-        dma("YSY"[i], HB(n), A("new", 160 * i, 160 * i + 160))
+    for i, n in enumerate(("yl", "yr")):
+        dma("YS"[i], HB(n), A("new", 160 * i, 160 * i + 160))
+    next(un)
+    dma("Y", HB("yb"), A("new", 320, 480))
     wait_for("Y", {s: v for s, v in cnt.items()})

@@ -6,7 +6,7 @@ AF = ActivationFunctionType
 NR = 4
 V0 = 1536
 GH = 2560
-US = 3088
+US = 2576
 BIG = 4096.0
 
 SCRATCH = {}
@@ -24,7 +24,7 @@ def _pack(big, dtype, parts):
 MASKS = ("zl", "zr", "zb", "s0", "s1", "s2", "s3", "za", "cq")
 _pack("km", "bfloat16", [(n, 144) for n in MASKS])
 _pack("kf", "float32", (("pq", 16), ("qf", 1), ("qn", 1), ("meS", 160), ("zer", 128), ("thf", 1), ("thb", 1), ("wtf", 1), ("jb", 4),
-                        ("n3", 1), ("meN", 96), ("sn0", 32), ("sn1", 32), ("old", 480), ("val", 256), ("m4k", 256),
+                        ("n3", 2), ("gb", 1), ("meN", 96), ("sn0", 32), ("sn1", 32), ("old", 480), ("val", 256), ("m4k", 256),
                         ("sc", 512), ("t32", 32), ("lrb", 480), ("nsp", 480), ("ua", 480), ("new", 480),
                         ("big", 32), ("hb", 32), ("c160", 160), ("snt", 560), ("b0", 32), ("dl", 64), ("sp", 64), ("bx", 64)))
 _pack("ki", "int32", (("thi", 1), ("wti", 1), ("ik", 16), ("ik2", 16), ("pi", 1), ("qi", 1), ("ti", 32), ("ti2", 32),
@@ -33,12 +33,12 @@ _pack("ku", "uint16", (("li", 448), ("snl", 32), ("gbo", 32), ("bo", 32), ("ul",
                        ("snf", 32), ("eo", 64)))
 _pack("kh", "float16", (("sn16", 512), ("gs", 512), ("st", 448), ("snS", 32), ("slc", 32), ("me16", 128), ("d16", 128),
                         ("inc", 144), ("ofr", 128), ("y16", 512), ("n16", 384), ("gf", 512)))
-_pack("kb", "bfloat16", (("ones", 128), ("eye", 128), ("blk", 128), ("blka", 128), ("tri", 128), ("lt", 128), ("n64", 128), ("n4k", 128),
+_pack("kb", "bfloat16", (("ones", 480), ("e8k", 128), ("mn", 144), ("mq", 144), ("sh0", 128), ("sh1", 128), ("isg", 320), ("eye", 128), ("blk", 128), ("blka", 128), ("tri", 128), ("lt", 128), ("n64", 128), ("n4k", 128),
                          ("ts0", 128), ("tsel", 128), ("s1k", 144), ("s2k", 144), ("wn", 144), ("wq", 144), ("nblk", 128), ("mem", 384),
                          ("mem0", 384), ("kq", 256), ("jr", 512), ("go", 128), ("pen", 384), ("eT", 512), ("e2", 512), ("e2b", 512),
                          ("cT", 512), ("vs", 1024), ("vy", 512), ("fs", 1024),
                          ("sb0", 512), ("sb1", 512), ("sb2", 512), ("sb3", 512), ("sb4", 512)))
-for _n, _c, _d in (("raw", V0, "int32"), ("rsn", 512, "int32"), ("r16", 2048, "float16"), ("TB", 3072, "float32"),
+for _n, _c, _d in (("raw", V0, "int32"), ("TI", V0, "int32"), ("rsn", 512, "int32"), ("r16", 2048, "float16"), ("TB", 3072, "float32"),
                    ("Z0", 1152, "float32"), ("Z1", 1152, "float32"), ("UU", 5 * US + 16, "bfloat16"),
                    ("dtb", 2064, "bfloat16"), ("NT", 2592, "bfloat16"), ("vL", 2048, "bfloat16"), ("vR", 2560, "bfloat16"),
                    ("vB", 2048, "bfloat16"), ("dL", 2048, "bfloat16"), ("dR", 2048, "bfloat16"), ("dB", 2048, "bfloat16"),
@@ -267,14 +267,15 @@ def rank_program(g, core, T, topo):
         cnt[rs] = cnt.get(rs, 0) + len(chosen(nb_core[s], core))
         note(None, [], dst[1], rs, cnt[rs])
 
-    def ghosts(n, s):
-        return U(n, 16 + GH + 256 * s, 16 + GH + 256 * s + 256)
+    def ghosts(t, n, s):
+        return U(n, 16 + PP[t] + 256 * s, 16 + PP[t] + 256 * s + 256)
 
     def HB(n):
         return (T[n][:], [])
 
     PP, NW, WN = (V0, 2048), (96, 128), (128, 160)
     KZ = ("zl", "zr", "zb")
+    TB_ = ("p5", "p6", "p7")
 
     def L(t, i):
         return i * (NW[t] + 32) + (32 if i < 2 else 0)
@@ -286,36 +287,29 @@ def rank_program(g, core, T, topo):
 
     def clear(a, z):
         op("V", [lambda: g.vector.memset(T["km"][:, 144 * a:144 * z], 0.0)], [], [(n, 0, 144) for n in MASKS[a:z]])
-    iota(A("pi", 0, 1), [[0, 1]], 0, 1, False)
+    iota(A("TI", 1152, V0), [[0, V0 - 1152]], 0, 0, False)
+    ms(A("TI", 0, 1152), 0)
+    dmas([("Y", (T["TI"][i:128:16, :], [("TI", 0, V0)]), HB(n)) for i, n in ((2, "bs"), (0, "lt"), (1, "rt"))])
     ms(A("ones", 0, 128), 1.0)
     clear(0, 3)
     for a, n in enumerate(KZ):
         sel((X(n, 0, 144, 16), [(n, 0, 144)]), A("ones", 0, 9), [[-1, 9]], OP.is_equal, 1 - 8 * a, 1)
     dma("Y", A("thi", 0, 1), HB("th"))
     dma("Y", A("wti", 0, 1), HB("wt"))
-    dma("Y", A("dtb", 0, 2048), HB("det"))
-    clear(3, 9)
-    for a in (2, 0, 1, 3):
-        n = "s%d" % a
-        sel((X(n, 16, 144, 16), [(n, 0, 144)]), A("ones", 0, 8), [[-16, 8]], OP.is_equal, -a, 1)
-    sel(A("eye", 0, 128), A("ones", 0, 128), [[-1, 128]], OP.is_equal, 0, 1)
-    iota(A("c160", 0, 160), [[1, 160]], 0, 0)
-    iota(A("mem0", 0, 384), [[0, 24], [16, 16]], 0, 0)
-    ts(A("qi", 0, 1), A("pi", 0, 1), 15, OP.bitwise_and)
-    tt(A("ts0", 0, 128), A("zl", 16, 144), A("zr", 15, 143), OP.add)
-    cp(A("qf", 0, 1), A("qi", 0, 1))
-    tt(A("tsel", 0, 128), A("zb", 14, 142), A("ts0", 0, 128), OP.add)
-    for lo in (0, 272, 544):
-        ms(A("snt", lo, lo + 16), -1.0)
 
     ts(R("sn16", 0, 1, 0, 512), R("rsn", 0, 1, 0, 512), -1536, OP.add)
     toS("p4", 0, "zl", "sn16", 0, 512, k=(0, 1))
     mm("p5", [(A("p5", 0, 512), M("zl", 2, 8), R("sn16", 0, 1, 0, 512), True, True)])
+    clear(3, 9)
+    sel(A("tsel", 0, 128), A("ones", 0, 128), [[-1, 8], [-8, 16]], OP.is_equal, 0, 1)
+    for a in (2, 0, 1, 3):
+        n = "s%d" % a
+        sel((X(n, 16, 144, 16), [(n, 0, 144)]), A("ones", 0, 8), [[-16, 8]], OP.is_equal, -a, 1)
 
     def ghost0(t, qs):
         for q, s in zip(qs, order):
             add(q, A("sb0", 256 * s, 256 * s + 256), ind(U(0, 16, 16 + PP[t]), A("snl", 16 * s, 16 * s + 16)), 0)
-            send(s, "0", A("sb0", 256 * s, 256 * s + 256), ghosts(0, 1 - s))
+            send(s, "0", A("sb0", 256 * s, 256 * s + 256), ghosts(t, 0, 1 - s))
 
     def base_send(x):
         for s in order:
@@ -328,16 +322,16 @@ def rank_program(g, core, T, topo):
             add(q, A("TB", GH + 256 * s, GH + 256 * s + 256), ind(A("snt", 272 * s, 272 * s + 288), A("gbo", 16 * s, 16 * s + 16)), 0)
 
     def turn(t, i):
-        toS("p%d" % i, 0, KZ[i], "r16", 0, PP[t], k=(0, i + 1))
+        toS(TB_[i], 0, KZ[i], "r16", 0, PP[t], k=(0, i + 1))
 
     def wrapped(t, i):
         nw = NW[t]
         o = L(t, i)
-        ts(A("li", o, o + nw), A("p%d" % i, 0, nw), 1536, OP.add)
-        cp(A("st", o, o + nw), A("p%d" % i, 0, nw))
+        ts(A("li", o, o + nw), A(TB_[i], 0, nw), 1536, OP.add)
+        cp(A("st", o, o + nw), A(TB_[i], 0, nw))
 
     def slots(t):
-        ts(A("gs", 0, 512), ind(A("TB", 0, PP[t]), A("snl", 0, 32)), -1536, OP.add)
+        ts(A("gs", 0, 512), ind(A("TB" if t else "TI", 0, PP[t]), A("snl", 0, 32)), -1536, OP.add)
 
     def slot_legs(t):
         for i in range(2):
@@ -358,7 +352,7 @@ def rank_program(g, core, T, topo):
             act(o, x, AF.Sign, bias=A("thb", 0, 1))
         one("p%d" % c, 0, 512, "eye", o, n == 0, False)
 
-    MK = (("VVV", "VVV", "VVV", "VVV", "VVS"), ("VVVV", "VVVV", "VVVV", "VVVV", "VVVS"))
+    MK = (("--V", "VVV", "VVV", "VVV", "VVS"), ("---V", "VVVV", "VVVV", "VVVS", "VVVS"))
 
     def diff(q, n, i, t, c):
         o = L(t, i) + 16 * c
@@ -366,6 +360,21 @@ def rank_program(g, core, T, topo):
 
     def keep(b, lo, t, i, c0, c1, s1=False):
         mm(b, [(A(b, lo, lo + c1 - c0), A("eye", 0, 128), A("st", L(t, i) + c0, L(t, i) + c1), False, s1)])
+
+    def sides(t, i):
+        nw = NW[t]
+        if i < 2:
+            act(A("isg", 64 + nw * i, 64 + nw * i + nw), A(TB_[i], 0, nw), AF.Sign, bias=A("gb", 0, 1))
+        else:
+            act(A("isg", 0, 64), A("p7", 0, 64), AF.Sign, bias=A("gb", 0, 1))
+
+    def leg(b, lo, t, i, c0, c1):
+        keep(b, lo, t, i, c0, c1)
+        o = 32 * i + 32 + c0 if c0 < 0 else 64 + NW[t] * i + c0
+        one(b, lo, lo + c1 - c0, "sh%d" % t, A("isg", o, o + c1 - c0), False, False)
+
+    def legs(t, lo, hi, b):
+        ts(A("ul", lo, hi), A(b, 0, hi - lo), 1552 - (GH - PP[t]) // 2, OP.add, PP[t] + 528, OP.min)
 
     def UL(t, i, c0, c1):
         nw = NW[t]
@@ -379,59 +388,73 @@ def rank_program(g, core, T, topo):
         def slot_flags():
             one("p4", 0, 64, "n4k", A("ones", 0, 64), True, False)
             for i in range(2):
-                keep("p4", 32 * i, t, i, -32, 0)
+                leg("p4", 32 * i, t, i, -32, 0)
             for i in range(2):
                 for s in range(2):
                     o = L(t, i) - 32 + 16 * s
                     tt(A("fs", 512 * i + 256 * s, 512 * i + 256 * s + 256), ind(A("TB", 0, 3072), A("li", o, o + 16)),
                        A("snt", 16 + 272 * s, 272 + 272 * s), OP.is_equal)
-                toS("p4", 32 * i, "s2k", "fs", 512 * i, 512 * i + 512, False, i == 1)
-        for c in range(nc):
+            toS("p4", 0, "s2k", "fs", 0, 1024, False, True)
+        for c in range(3):
+            diff("S", "dL", 0, t, c)
+        if t:
+            sides(t, 1)
+        for c in range(first):
+            diff("V", "dR", 1, t, c)
+        for c in range(3, 6):
+            diff("S", "dL", 0, t, c)
+        if t:
+            slot_lists(t)
+            sides(t, 2)
+        for c in range(6, nc):
             diff("S", "dL", 0, t, c)
         for c in range(mine, nc):
             diff("S", "dR", 1, t, c)
         for b, c0, c1 in (("p5", 0, 64), ("p6", 64, nw)):
             one(b, 0, 2 * (c1 - c0), "n4k", A("mem", 0, 2 * (c1 - c0)), True, False)
             for i in range(2):
-                keep(b, (c1 - c0) * i, t, i, c0, c1)
-        if first:
-            slot_flags()
-        for c in range(4):
-            diff("V", "dR", 1, t, c)
+                leg(b, (c1 - c0) * i, t, i, c0, c1)
         toS("p5", 0, "s2k", "dL", 0, 1024, False, False)
-        toS("p5", 64, "s2k", "dR", 0, 1024, False, True)
-        if not first:
-            yield
-            slot_flags()
-        for c in range(4, mine):
+        slot_flags()
+        for c in range(first, mine):
             diff("V", "dR", 1, t, c)
+        toS("p5", 64, "s2k", "dR", 0, 1024, False, True)
         toS("p6", 0, "s2k", "dL", 1024, P, False, False)
         toS("p6", h, "s2k", "dR", 1024, P, False, True)
-        ts(A("ul", 64, 192), A("p5", 0, 128), 1552, OP.add, US, OP.min)
-        ts(A("ul", 0, 64), A("p4", 0, 64), 1552, OP.add, US, OP.min)
-        yield
+        legs(t, 0, 64, "p4")
+        legs(t, 64, 192, "p5")
 
     def depths(t, slack):
         P, nw = PP[t], NW[t]
         nc = P // 512
         for n in range(5):
             gr = "gr%d" % (n % 2)
-            win = U(n, 0, US + 16)
+            win = U(n, 0, P + 544)
             for s in range(2):
-                recv(s, str(n), ghosts(n, s))
+                recv(s, str(n), ghosts(t, n, s))
             if n < 4:
                 for s in order:
                     act(A(gr, 256 * s, 256 * s + 256), ind(win, UL(t, 1, 16 * s - 32, 16 * s - 16)))
-            for c, q in enumerate(MK[t][n]):
-                if q == "V":
-                    marks(n, c, q)
+            if n == 0:
+                for f in slack.get(-1, []):
+                    f()
+            if MK[t][n][0] == "V":
+                marks(n, 0, "V")
             if n < 4:
                 for s in order:
                     o = A("sb%d" % (n + 1), 256 * s, 256 * s + 256)
                     tt(o, ind(win, UL(t, 0, 16 * s - 32, 16 * s - 16)), A(gr, 256 * s, 256 * s + 256), OP.max)
-                    send(s, str(n + 1), o, ghosts(n + 1, 1 - s))
+                    send(s, str(n + 1), o, ghosts(t, n + 1, 1 - s))
             if n == 0:
-                ts(A("ul", 192, 64 + 2 * nw), A("p6", 0, 2 * nw - 128), 1552, OP.add, US, OP.min)
+                for f in slack.get(-2, []):
+                    f()
+            for c, q in enumerate(MK[t][n]):
+                if q == "V" and c:
+                    marks(n, c, q)
+            if n == 0:
+                legs(t, 192, 64 + 2 * nw, "p6")
+            if n == 1:
+                fill("UU", 16 + P, 16 + P + 512)
             if n == 4:
                 for c, q in enumerate(MK[t][n]):
                     if q == "S":
@@ -442,6 +465,9 @@ def rank_program(g, core, T, topo):
                 if n < 4:
                     act(r, x)
                     tt(U(n + 1, 16 + 512 * c, 16 + 512 * c + 512), y, r, OP.max)
+                    if n == 0 and c == 0:
+                        for f in slack.get(-3, []):
+                            f()
                 else:
                     o = A("in1", 512 * c, 512 * c + 512)
                     act(r, x, AF.Sign, bias=A("thb", 0, 1))
@@ -483,54 +509,54 @@ def rank_program(g, core, T, topo):
     def flags2(t):
         nw = NW[t]
         ts(A("pen", 0, nw), A("p5", 0, nw), 0, OP.not_equal)
-        ts(A("lf", 0, 3 * nw), A("p7", 0, 3 * nw), 1552, OP.add, 16 + GH, OP.min)
         one("p4", 0, nw, "n64", A("pen", 0, nw), True, False)
         for i in (1, 2):
             one("p4", 0, nw, "n64", A("pen", nw * i, nw * i + nw), False, False)
 
     def olds(t):
         P, w = PP[t], WN[t]
-        one("p6", 0, 3 * w, "za", A("dtb", 0, 3 * w), True, False)
+        one("p6", 0, 3 * w, "za", A("ones", 0, 3 * w), True, False)
         for i, m in enumerate(KZ):
             toN("p6", w * i, w, m, "r16", 0, 0, P, False, False, k=(0, i + 1))
 
     def codes(t):
-        ts(A("jb", 0, 1), A("pq", 0, 1), PP[t], OP.mult, A("pq", 3, 4), OP.add)
+        ts(A("jb", 0, 1), A("pq", 0, 1), PP[t], OP.mult, A("jb", 3, 4), OP.add)
         ts(A("jb", 1, 2), A("pq", 0, 1), PP[t], OP.mult, A("jb", 2, 3), OP.add)
         for e in range(2):
             ts((X("jr", e, 512, 2), [("jr", 0, 512)]), A("kq", 0, 256), A("pq", 1, 2), OP.mult, A("jb", e, e + 1), OP.add)
 
-    def splits(t):
+    def splits(t, gap):
         P, nw = PP[t], NW[t]
         nc, k = P // 512, nw // 16
-        halves = [("VS"[c % 2], c, 0, 512) for c in range(nc)] if nc % 2 == 0 else [("V", 0, 0, 512), ("S", 1, 0, 512), ("V", 2, 0, 256), ("S", 2, 256, 512)]
-        for q, c, lo, hi in halves:
+        for c, q in enumerate(("VVS", "VSVS")[t]):
             lift = 1 + sum(MK[t][n][c] == "S" for n in range(5))
-            add(q, A("in0", 512 * c + lo, 512 * c + hi), A("p%d" % c, lo, hi), lift)
+            add(q, A("in0", 512 * c, 512 * c + 512), A("p%d" % c, 0, 512), lift)
+            one("p%d" % c, 0, 512, "eye", A("in0", 512 * c, 512 * c + 512), True, False)
         for c, q in enumerate("VS" * nc):
             add(q, A("gr1", 256 * c, 256 * c + 256), ind(A("in0", 0, P), A("pl", 16 * c, 16 * c + 16)), 0)
-        for c in range(nc):
-            b = "p%d" % c
-            mm(b, [(A(b, 0, 512), A("eye", 0, 128), A(n, 512 * c, 512 * c + 512), n == "in0", n == "gr1") for n in ("in0", "gr1")])
-        for q, c, lo, hi in halves:
-            b, o = A("p%d" % c, lo, hi), A("in1", 512 * c + lo, 512 * c + hi)
+            if c % 2:
+                one("p%d" % (c // 2), 0, 512, "eye", A("gr1", 256 * c - 256, 256 * c + 256), False, True)
+        for c, q in enumerate(("SVS", "VSVS")[t]):
+            b, o = A("p%d" % c, 0, 512), A("in1", 512 * c, 512 * c + 512)
             if q == "S":
                 act(o, b, AF.Sign)
             else:
                 ts(o, b, 0, OP.is_gt)
         toS("p4", 0, "cq", "in1", 0, 1024, False, False)
         toS("p4", 64, "cq", "in1", 1024, P, False, True)
+        gap()
         go = A("go", 0, nw)
         ts(go, A("p4", 0, nw), 11, OP.is_ge)
         one("p5", 0, nw, "blk", go)
         one("p5", nw, 2 * nw, "eye", A("d16", 0, nw), True, False)
         one("p5", nw, 2 * nw, "nblk", go, False, True)
         for e, x in enumerate((A("me16", 0, nw), A("st", L(t, 2), L(t, 2) + nw))):
-            mm("p7", [(A("p7", nw * e, nw * e + nw), A("eye", 0, 128), x, True, False), (A("p7", nw * e, nw * e + nw), A("lt", 0, 128), go, False, True)])
+            mm("p0", [(A("p0", nw * e, nw * e + nw), A("eye", 0, 128), x, True, False), (A("p0", nw * e, nw * e + nw), A("lt", 0, 128), go, False, True)])
         scan(A("inc", 1, nw + 1), A("p5", 0, nw), A("zer", 0, nw), OP.add, OP.add)
         tt(A("ofr", 0, nw), A("inc", 0, nw), A("p5", nw, 2 * nw), OP.max)
-        act(A("val", 0, 2 * nw), A("p7", 0, 2 * nw), AF.Identity, bias=1537.0 - 32 * BIG)
+        act(A("val", 0, 2 * nw), A("p0", 0, 2 * nw), AF.Identity, bias=1537.0 - 32 * BIG)
         toS("p4", 0, "s0", "ofr", 0, nw)
+        ts(A("lf", 0, 3 * nw), A("p7", 0, 3 * nw), 1552, OP.add, 16 + GH, OP.min)
         cp(A("off", 0, k), A("p4", 0, k))
         for e in range(2):
             scat(A("Z%d" % e, 0, 1152), A("off", 0, k), A("val", nw * e, nw * e + nw))
@@ -539,6 +565,7 @@ def rank_program(g, core, T, topo):
         ts(A("y16", 0, 512), A("sc", 0, 512), 0, OP.max, BIG, OP.min)
         mm("p5", [(A("p5", 0, 32), M("cq", q), (X("y16", 256 * (q % 2) + q // 2, 256 * (q % 2) + 256, 8), [("y16", 0, 512)]), q == 0, q == 15)
                   for q in range(16)])
+        codes(t)
         ts(A("ti", 0, 32), A("p5", 0, 32), -1, OP.add)
         ts(A("ti2", 0, 32), A("ti", 0, 32), 4095, OP.bitwise_and)
         tt(A("t32", 0, 32), A("ti2", 0, 32), A("meS", nw, nw + 32), OP.min)
@@ -556,22 +583,29 @@ def rank_program(g, core, T, topo):
 
     def children(t, qs):
         P = PP[t]
-        def child(q, i, out):
-            x = ind(A("dtb", 0, 2064), A("eo", 32 * i, 32 * i + 32))
-            if q == "V":
-                tt(out, x, A("e2b", 0, 512), OP.add)
-            else:
-                y, b = A("vs", 512 * i, 512 * i + 512), "p%d" % (3 * i)
-                act(y, x)
+        x = [ind(A("dtb", 0, 2064), A("eo", 32 * i, 32 * i + 32)) for i in range(2)]
+        if qs == "VV":
+            tt(A("cT", 0, 512), x[0], A("e2b", 0, 512), OP.add)
+            yield
+            scat(U(0, 16, 16 + P + 512), A("TL", 0, 32), A("cT", 0, 512))
+            yield
+            tt(A("sb0", 0, 512), x[1], A("e2b", 0, 512), OP.add)
+            yield
+        else:
+            for i, b in enumerate(("p3", "p4")):
+                y = A("fs", 512 * i, 512 * i + 512)
+                act(y, x[i])
+                if i:
+                    yield
                 one(b, 0, 512, "eye", A("e2", 0, 512), True, False)
                 one(b, 0, 512, "eye", y, False, True)
-                act(out, A(b, 0, 512), AF.Identity, bias=-258.0)
-        child(qs[0], 0, A("cT", 0, 512))
-        yield
-        scat(U(0, 16, 16 + P + 512), A("TL", 0, 32), A("cT", 0, 512))
-        yield
-        child(qs[1], 1, U(0, 16 + P, 16 + P + 512))
-        yield
+                if i == 0:
+                    act(A("cT", 0, 512), A(b, 0, 512), AF.Identity, bias=-258.0)
+            yield
+            scat(U(0, 16, 16 + P + 512), A("TL", 0, 32), A("cT", 0, 512))
+            yield
+            act(U(0, 16 + P, 16 + P + 512), A("p4", 0, 512), AF.Identity, bias=-258.0)
+            yield
 
     NTW = A("NT", 0, 2592)
 
@@ -594,77 +628,93 @@ def rank_program(g, core, T, topo):
 
     def owns(t):
         P, w = PP[t], WN[t]
-        toN("p2", 0, w, "wn", "NT", 16, 0, P)
-        toN("p2", w, w, "cq", "NT", 16, 0, P)
+        one("p2", 0, 2 * w, "e8k", A("ones", 0, 2 * w), True, False)
+        for i, m in enumerate(("mn", "mq")):
+            toN("p2", w * i, w, m, "NT", 16, 0, P, False, i == 1)
 
     def right_bases(t):
         P, w = PP[t], WN[t]
         act(A("vy", 0, 512), ind(A("vR", 0, P + 512), A("TL", 0, 32)))
 
-    def turnN(t, n, i):
-        P, w = PP[t], WN[t]
-        toN("p1", i * w, w, "wn", n, 0, 0, P, True, i < 2)
-        if i == 2:
-            toN("p1", 2 * w, w, "wn", "vy", 0, P, P + 512, False, True)
+    def zeroN(t):
+        one("p1", 0, 3 * WN[t], "za", A("ones", 0, 3 * WN[t]), True, False)
+
+    def turnN(t, n, i, x0, x1, last=False):
+        toN("p1", i * WN[t], WN[t], "wn", n, 0 if n == "vy" else x0, x0, x1, False, last)
 
     def early(t):
         w = WN[t]
         act(A("old", 0, 3 * w), A("p6", 0, 3 * w), AF.Identity, bias=1536.0)
-        ts(A("nsp", 0, 2 * w), A("p2", 0, 2 * w), 0, OP.is_equal)
+        act(A("p7", 0, w), A("p2", 0, w), AF.Relu)
 
     def update(t):
         w = WN[t]
         tt(A("lrb", 0, 3 * w), A("old", 0, 3 * w), A("p1", 0, 3 * w), OP.max)
-        tt(A("ua", 0, 2 * w), A("lrb", 0, 2 * w), A("nsp", 0, 2 * w), OP.mult)
-        tt(A("nsp", 2 * w, 3 * w), A("lrb", 2 * w, 3 * w), A("lrb", 0, w), OP.subtract)
-        tt(A("new", 0, 2 * w), A("ua", 0, 2 * w), A("p2", 0, 2 * w), OP.add)
-        yield
-        tt(A("ua", 2 * w, 3 * w), A("nsp", 2 * w, 3 * w), A("nsp", 0, w), OP.mult)
-        tt(A("new", 2 * w, 3 * w), A("ua", 2 * w, 3 * w), A("lrb", 0, w), OP.add)
-        yield
+        tt(A("ua", 0, 2 * w), A("lrb", 0, 2 * w), A("p2", 0, 2 * w), OP.min)
+        tt(A("p0", 0, w), A("p7", 0, w), A("lrb", 0, w), OP.subtract)
+        for i in range(2):
+            act(A("new", w * i, w * i + w), A("ua", w * i, w * i + w), AF.Abs)
+        tt(A("ua", 2 * w, 3 * w), A("lrb", 2 * w, 3 * w), A("p0", 0, w), OP.min)
+        act(A("new", 2 * w, 3 * w), A("ua", 2 * w, 3 * w), AF.Abs)
 
-    ts(R("r16", 0, 3, 0, 512), R("raw", 0, 3, 0, 512), -1536, OP.add)
-    ts(A("snl", 0, 32), A("p4", 0, 32), 1536, OP.add)
-    ghost0(0, "SS")
-    for i in (1, 2):
+    def cast(i):
         ts(R("r16", 0, 3, 512 * i, 512 * i + 512), R("raw", 0, 3, 512 * i, 512 * i + 512), -1536, OP.add)
-    for i, q in enumerate("VSV"):
+    def table(i):
         b = "p%d" % i
         mm(b, [(A(b, 0, 512), (X("tsel", 0, 128, 1, 0, 24), [("tsel", 0, 128)]), R("r16", 0, 3, 512 * i, 512 * i + 512), True, True)])
-        add(q, A("TB", 512 * i, 512 * i + 512), A(b, 0, 512), 1536)
-    turn(0, 0)
-    slots(0)
-    toS("p4", 0, "s2", "gs", 0, 512)
-    base_send("p4")
-    slot_legs(0)
-    turn(0, 1)
-    turn(0, 2)
+        add("S", A("TB", 512 * i, 512 * i + 512), A(b, 0, 512), 1536)
+    ts(A("snl", 0, 32), A("p4", 0, 32), 1536, OP.add)
+    iota(A("pi", 0, 1), [[0, 1]], 0, 1, False)
+    sel(A("eye", 0, 128), A("ones", 0, 128), [[-1, 128]], OP.is_equal, 0, 1)
+    ghost0(0, "SS")
     for s in range(2):
         act(A("snt", 16 + 272 * s, 272 + 272 * s), A("p5", 256 * s, 256 * s + 256), AF.Identity, bias=1536.0)
-    act(A("n4k", 0, 128), A("eye", 0, 128), scale=-BIG)
-    act(A("s2k", 0, 144), A("s2", 0, 144), scale=BIG)
-    act(A("mem", 0, 384), A("mem0", 0, 384), AF.Identity, bias=A("qf", 0, 1))
-    act(A("b0", 0, 32), A("p4", 0, 32))
-    act(A("dtb", 0, 2048), A("dtb", 0, 2048), AF.Identity, bias=128.75, scale=0.5)
+    cast(0)
+    cast(1)
+    table(0)
+    table(1)
+    slots(0)
+    toS("p4", 0, "s2", "gs", 0, 512)
+    cast(2)
+    base_send("p4")
+    iota(A("mem0", 0, 384), [[0, 24], [16, 16]], 0, 0)
+    table(2)
+    turn(0, 0)
+    slot_legs(0)
+    turn(0, 1)
     iota(A("TB", V0, GH), [[1, 1024]], V0, 0)
+    iota(A("c160", 0, 160), [[1, 160]], 0, 0)
     iota(A("ik", 0, 16), [[-1, 16]], 16, 1, False)
-    ms(U(0, 16 + V0, 16 + GH), 0.0)
-    wrapped(0, 0)
-    slot_lists(0)
-    wrapped(0, 1)
+    ts(A("qi", 0, 1), A("pi", 0, 1), 15, OP.bitwise_and)
     for n in range(6):
         ms(A("UU", US * n, US * n + 16), 0.0)
+    cp(A("qf", 0, 1), A("qi", 0, 1))
+    ms(A("gb", 0, 1), 1536.5 - GH)
+    act(A("b0", 0, 32), A("p4", 0, 32))
+    act(A("s2k", 0, 144), A("s2", 0, 144), scale=BIG)
+    act(A("n4k", 0, 128), A("eye", 0, 128), scale=-BIG)
+    act(A("mem", 0, 384), A("mem0", 0, 384), AF.Identity, bias=A("qf", 0, 1))
+    for lo in (0, 272, 544):
+        ms(A("snt", lo, lo + 16), -1.0)
+    wrapped(0, 0)
+    for n in range(5):
+        ms(U(n, V0 + 528, V0 + 544), 0.0)
     cp(A("thf", 0, 1), A("thi", 0, 1))
     ts(A("thb", 0, 1), A("thi", 0, 1), -1, OP.mult, 0.5, OP.add)
     cp(A("wtf", 0, 1), A("wti", 0, 1))
-    ts(A("meS", 0, 160), A("c160", 0, 160), 16, OP.mult, A("qf", 0, 1), OP.add)
-    wrapped(0, 2)
+    slot_lists(0)
+    for t in range(2):
+        act(A("sh%d" % t, 0, 128), A("eye", 0, 128), scale=(PP[t] - GH) / 2)
+    sides(0, 0)
+    sides(0, 2)
+    wrapped(0, 1)
+    sides(0, 1)
+    turn(0, 2)
+    for c in range(2):
+        marks(0, c, "V")
     ghost_bases("VS")
-    wait_for("Y", needs("Y", A("gbo", 0, 32)[1], []))
-    for n in range(1, 5):
-        dma("Y", U(n, 16 + V0, 16 + GH), U(0, 16 + V0, 16 + GH))
-    for _ in prep(0, True, 4):
-        pass
+    prep(0, 2, 4)
+
     sel((X("za", 16, 144, 16), [("za", 0, 144)]), A("ones", 0, 8), [[-16, 8]], OP.is_ge, 0, 1)
     sel((X("cq", 16, 144, 16), [("cq", 0, 144)]), (X("za", 16, 144, 16), [("za", 0, 144)]), [[16, 8]], OP.is_ge, 15, -1)
     sel(A("blka", 0, 128), A("ones", 0, 128), [[-16, 8], [0, 16]], OP.is_ge, 0, 1)
@@ -677,6 +727,9 @@ def rank_program(g, core, T, topo):
 
     def late0():
         act(A("s1k", 0, 144), A("s1", 0, 144), scale=BIG)
+        act(A("meS", 0, 160), A("c160", 0, 160), AF.Identity, bias=A("qf", 0, 1), scale=16.0)
+        act(A("n64", 0, 128), A("eye", 0, 128), scale=-64.0)
+        ms(A("ones", 128, 480), 1.0)
         ts(A("ik2", 0, 16), A("ik", 0, 16), 15, OP.bitwise_and)
         ts(A("me16", 0, 128), A("meS", 0, 128), -1536, OP.add)
         ts(A("pq", 0, 16), A("ik2", 0, 16), 0, OP.is_equal)
@@ -686,120 +739,140 @@ def rank_program(g, core, T, topo):
     def late1():
         ts(A("d16", 0, 128), A("c160", 0, 128), 1024, OP.add)
         ts(A("inc", 0, 1), A("zer", 0, 1), 0, OP.add)
-        ts(A("n3", 0, 1), A("qf", 0, 1), 3, OP.not_equal)
-        tt(A("jb", 2, 3), A("pq", 2, 3), A("pq", 3, 4), OP.subtract)
+        ts(A("n3", 0, 1), A("qf", 0, 1), 3, OP.is_lt)
+        ts(A("n3", 1, 2), A("pq", 3, 4), -1, OP.add)
+        ts(A("jb", 3, 4), A("pq", 4, 5), 8192, OP.mult, A("pq", 3, 4), OP.add)
+        ts(A("jb", 2, 3), A("pq", 3, 4), -2, OP.mult, A("pq", 2, 3), OP.add)
+        tt(A("jb", 2, 3), A("jb", 2, 3), A("jb", 3, 4), OP.add)
         one("p3", 0, 32, "eye", A("snS", 0, 32), True, False)
         one("p3", 0, 32, "n4k", A("slc", 0, 32), False, False)
         toS("p3", 0, "s1k", "gs", 0, 512, False, True)
-        act(A("n64", 0, 128), A("eye", 0, 128), scale=-64.0)
         act(A("qn", 0, 1), A("qf", 0, 1), scale=96.0)
         act(A("meN", 0, 96), A("c160", 0, 96), AF.Identity, bias=A("qn", 0, 1))
 
     def late2():
         dma("Y", (T["TB"][3:128:16, 0:V0], [("TB", 0, V0)]), A("meN", 0, 96))
-        act(A("wn", 0, 144), A("cq", 0, 144), scale=A("n3", 0, 1))
-        act(A("wq", 0, 144), A("cq", 0, 144), scale=A("wtf", 0, 1))
         act(A("nblk", 0, 128), A("blk", 0, 128), scale=-BIG)
         act(A("blka", 0, 128), A("eye", 0, 128), scale=32 * BIG)
         act(A("tri", 0, 128), A("tri", 0, 128), scale=BIG)
+        tt(A("lt", 0, 128), A("tri", 0, 128), A("blka", 0, 128), OP.add)
+
+    def late3():
         ts(A("snf", 0, 32), A("p3", 0, 32), 16, OP.add, 16 + GH, OP.min)
         cp(A("sn0", 0, 32), A("snl", 0, 32))
         tt(A("dl", 0, 32), A("st", 0, 32), A("b0", 0, 32), OP.subtract)
         tt(A("dl", 32, 64), A("slc", 0, 32), A("st", 0, 32), OP.subtract)
-        tt(A("lt", 0, 128), A("tri", 0, 128), A("blka", 0, 128), OP.add)
+
+    def load_det():
+        wait_for("Y", needs("Y", ghosts(0, 4, 0)[1] + ghosts(0, 4, 1)[1], []))
+        dma("Y", A("dtb", 0, 2048), HB("det"))
 
     def zs():
         for e in range(2):
             fill("Z%d" % e, 0, 256)
 
-    depths(0, {0: [late0, lambda: flags0(0), lambda: bases(0, 0, 2), lambda: fill("NT", 0, 1024)],
+    depths(0, {-3: [lambda: wrapped(0, 2)], 0: [late0, lambda: flags0(0), lambda: bases(0, 0, 2), lambda: fill("NT", 0, 1024)],
                1: [lambda: bases(0, 2, 4), lambda: fill("NT", 1024, 2048), late1, lambda: pens(0), lambda: olds(0)],
-               2: [lambda: bases(0, 4, 6), lambda: flags1(0), lambda: fill("NT", 2048, 2592), zs, lambda: codes(0)],
-               3: [late2, lambda: flags2(0), lambda: fill("vR", V0, GH), lambda: fill("m4k", 0, 256, -4096)]})
-    splits(0)
+               2: [lambda: bases(0, 4, 6), lambda: flags1(0), lambda: fill("NT", 2048, 2592), zs],
+               3: [late2, lambda: flags2(0), lambda: fill("m4k", 0, 256, -4096), lambda: fill("vR", V0, GH)],
+               4: [load_det]})
+    splits(0, late3)
+    act(A("wq", 0, 144), A("cq", 0, 144), scale=A("wtf", 0, 1))
+    act(A("wn", 0, 144), A("cq", 0, 144), scale=A("n3", 0, 1))
+    act(A("mn", 0, 144), A("cq", 0, 144), scale=A("n3", 1, 2))
+    act(A("mq", 0, 144), A("cq", 0, 144), scale=-1.0)
+    act(A("e8k", 0, 128), A("eye", 0, 128), scale=8192.0)
+    act(A("dtb", 0, 2048), A("dtb", 0, 2048), AF.Identity, bias=128.75, scale=0.5)
     heads(0)
     act(A("vs", 0, 512), ind(A("NT", 16, 16 + V0), A("snl", 0, 32)))
     act(A("vs", 512, 1024), ind(NTW, A("snf", 0, 32)))
     rename("V", 0, "vR", 1, 0, 96)
+    zeroN(0)
     owns(0)
-    for i in range(2):
-        toS("p4", 32 * i, "wn", "vs", 512 * i, 512 * i + 512)
-    mm("p5", [(A("p5", 0, 512), M("wn", 2), A("vs", 512, 1024), True, True)])
-    rename("S", 0, "vB", 2, 0, 96)
+    toS("p4", 0, "wn", "vs", 0, 1024)
+    rename("S", 0, "vB", 2, 0, 64)
     news(0)
-    turnN(0, "vR", 1)
+    turnN(0, "vR", 1, 0, V0)
     right_bases(0)
-    rename("S", 0, "vL", 0, 64, 96)
-    rename("V", 0, "vL", 0, 0, 64)
+    rename("S", 0, "vB", 2, 64, 96)
+    early(0)
+    weigh(0)
     ts(A("sp", 0, 64), A("p4", 0, 64), 0, OP.is_gt)
     tt(A("sn1", 0, 32), A("sn0", 0, 32), A("p4", 32, 64), OP.max)
     tt(A("bx", 0, 64), A("sp", 0, 64), A("dl", 0, 64), OP.mult)
     cp(A("snl", 0, 32), A("sn1", 0, 32))
     tt(A("sp", 0, 32), A("bx", 0, 32), A("bx", 32, 64), OP.add)
-    early(0)
+    rename("V", 0, "vL", 0, 0, 64)
     tt(A("bx", 0, 32), A("sp", 0, 32), A("b0", 0, 32), OP.add)
     base_send("bx")
-    turnN(0, "vB", 2)
-    turnN(0, "vL", 0)
-    weigh(0)
+    turnN(0, "vB", 2, 0, 1024)
+    turnN(0, "vy", 2, V0, 2048)
+    turnN(0, "vL", 0, 0, 1024)
+    mm("p5", [(A("p5", 0, 512), M("wn", 2), A("vs", 512, 1024), True, True)])
+    rename("V", 0, "vL", 0, 64, 96)
+    turnN(0, "vB", 2, 1024, V0)
     ch = children(0, "SS")
     next(ch)
-    un = update(0)
-    next(un)
-
-    def rows(i):
-        return (T["TB"][i:128:16, 0:2048], [("TB", 0, 2048)])
-    held = dmas([("Y", rows(i), A("new", 128 * i, 128 * i + 128)) for i in range(2)], more=True)
-    ts(A("n16", 0, 256), A("new", 0, 256), -1536, OP.add)
-    dma("Y", R("r16", 0, 1, 0, 2048), A("n16", 0, 128))
-    next(un)
-    dmas([("Y", rows(2), A("new", 256, 384))], held)
-    dma("Y", R("r16", 1, 2, 0, 2048), A("n16", 128, 256))
-    ts(A("n16", 256, 384), A("new", 256, 384), -1536, OP.add)
-    dma("Y", R("r16", 2, 3, 0, 2048), A("n16", 256, 384))
+    turnN(0, "vL", 0, 1024, V0, True)
     for s in range(2):
         x = A("snt", 16 + 272 * s, 272 + 272 * s)
         tt(x, x, A("p5", 256 * s, 256 * s + 256), OP.max)
     next(ch)
+    update(0)
+
+    def rows(i):
+        return (T["TB"][i:128:16, 0:2048], [("TB", 0, 2048)])
+
+    def half(i):
+        ts(A("n16", 128 * i, 128 * i + 128), A("new", 128 * i, 128 * i + 128), -1536, OP.add)
+        dma("Y", R("r16", i, i + 1, 0, 2048), A("n16", 128 * i, 128 * i + 128))
+    half(0)
+    half(1)
+    dmas([("Y", rows(i), A("new", 128 * i, 128 * i + 128)) for i in range(3)])
+    half(2)
     ghost_bases("SS")
     next(ch)
+    next(ch)
     ghost0(1, "SS")
-    for i in range(3):
+    for i in range(2):
         turn(1, i)
+    for c in range(3):
+        marks(0, c, "V")
     wrapped(1, 0)
+    sides(1, 0)
     slots(1)
     wrapped(1, 1)
     slot_legs(1)
-    pr = prep(1, False, 5)
-    next(pr)
-    slot_lists(1)
-    wrapped(1, 2)
-    next(pr)
-    depths(1, {0: [lambda: flags0(1), lambda: bases(1, 0, 2), lambda: fill("NT", 16, 1040), lambda: olds(1)],
+    prep(1, 2, 5)
+    turn(1, 2)
+    depths(1, {-3: [lambda: wrapped(1, 2)], 0: [lambda: flags0(1), lambda: bases(1, 0, 2), lambda: fill("NT", 16, 1040), lambda: olds(1)],
                1: [lambda: bases(1, 2, 5), lambda: fill("NT", 1040, 2064), lambda: pens(1)],
-               2: [lambda: bases(1, 5, 8), lambda: flags1(1), zs, lambda: codes(1)],
+               2: [lambda: bases(1, 5, 8), lambda: flags1(1), zs],
                3: [lambda: flags2(1)]})
-    splits(1)
+    splits(1, lambda: None)
     heads(1)
     act(A("e2b", 0, 512), A("e2", 0, 512), AF.Identity, bias=-258.0)
-    news(1)
     rename("S", 1, "vR", 1, 0, 128)
-    rename("V", 1, "vL", 0, 0, 128)
+    zeroN(1)
     owns(1)
-    right_bases(1)
-    rename("S", 1, "vB", 2, 0, 128)
-    turnN(1, "vL", 0)
-    turnN(1, "vR", 1)
-    turnN(1, "vB", 2)
+    news(1)
     weigh(1)
-    for _ in children(1, "VV"):
-        pass
-    dma("Y", HB("ye"), U(0, 16, 16 + GH))
+    ch = children(1, "VV")
+    next(ch)
+    next(ch)
+    dma("Y", (T["ye"][:, 0:2048], []), U(0, 16, 16 + 2048))
+    right_bases(1)
     early(1)
-    un = update(1)
-    next(un)
-    for i, n in enumerate(("yl", "yr")):
-        dma("YS"[i], HB(n), A("new", 160 * i, 160 * i + 160))
-    next(un)
-    dma("Y", HB("yb"), A("new", 320, 480))
+    turnN(1, "vR", 1, 0, 2048)
+    turnN(1, "vy", 2, 2048, GH)
+    for c0, c1 in ((0, 96), (96, 128)):
+        rename("S", 1, "vB", 2, c0, c1)
+        rename("V", 1, "vL", 0, c0, c1)
+        turnN(1, "vL", 0, 16 * c0, 16 * c1)
+        turnN(1, "vB", 2, 16 * c0, 16 * c1, c1 == 128)
+    next(ch)
+    dma("Y", (T["ye"][:, 2048:GH], []), A("sb0", 0, 512))
+    update(1)
+    for i, n in enumerate(("yl", "yr", "yb")):
+        dma("Y", HB(n), A("new", 160 * i, 160 * i + 160))
     wait_for("Y", {s: v for s, v in cnt.items()})

@@ -26,20 +26,20 @@ _pack("km", "bfloat16", [(n, 144) for n in MASKS])
 _pack("kf", "float32", (("pq", 16), ("qf", 1), ("qn", 1), ("meS", 160), ("zer", 128), ("thf", 1), ("thb", 1), ("wtf", 1), ("jb", 4),
                         ("n3", 2), ("gb", 1), ("meN", 96), ("sn0", 32), ("sn1", 32), ("old", 480), ("val", 256), ("m4k", 256),
                         ("sc", 512), ("t32", 32), ("lrb", 480), ("nsp", 480), ("ua", 480), ("new", 480),
-                        ("big", 32), ("hb", 32), ("c160", 160), ("snt", 560), ("b0", 32), ("dl", 64), ("sp", 64), ("bx", 64)))
+                        ("big", 32), ("hb", 64), ("c160", 160), ("snt", 560), ("b0", 32), ("dl", 64), ("sp", 64), ("bx", 64)))
 _pack("ki", "int32", (("thi", 1), ("wti", 1), ("ik", 16), ("ik2", 16), ("pi", 1), ("qi", 1), ("ti", 32), ("ti2", 32),
                       ("hz", 64), ("hz2", 64)))
 _pack("ku", "uint16", (("li", 448), ("snl", 32), ("gbo", 32), ("bo", 32), ("ul", 320), ("pl", 128), ("off", 8), ("TL", 32), ("lf", 384),
                        ("snf", 32), ("eo", 64)))
-_pack("kh", "float16", (("sn16", 512), ("gs", 512), ("st", 448), ("snS", 32), ("slc", 32), ("me16", 128), ("d16", 128),
+_pack("kh", "float16", (("sn16", 512), ("gs", 512), ("st", 448), ("snS", 32), ("slc", 32), ("me16", 128),
                         ("inc", 144), ("ofr", 128), ("y16", 512), ("n16", 384), ("gf", 512)))
-_pack("kb", "bfloat16", (("ones", 480), ("e8k", 128), ("mn", 144), ("mq", 144), ("sh0", 128), ("sh1", 128), ("isg", 320), ("eye", 128), ("blk", 128), ("blka", 128), ("tri", 128), ("lt", 128), ("n64", 128), ("n4k", 128),
+_pack("kb", "bfloat16", (("ones", 480), ("e8k", 128), ("mn", 144), ("mq", 144), ("sh0", 128), ("sh1", 128), ("isg", 320), ("d16", 128), ("eye", 128), ("blk", 128), ("blka", 128), ("tri", 128), ("lt", 128), ("n64", 128), ("n4k", 128),
                          ("ts0", 128), ("tsel", 128), ("s1k", 144), ("s2k", 144), ("wn", 144), ("wq", 144), ("nblk", 128), ("mem", 384),
                          ("mem0", 384), ("kq", 256), ("jr", 512), ("go", 128), ("pen", 384), ("eT", 512), ("e2", 512), ("e2b", 512),
                          ("cT", 512), ("vs", 1024), ("vy", 512), ("fs", 1024),
                          ("sb0", 512), ("sb1", 512), ("sb2", 512), ("sb3", 512), ("sb4", 512)))
 for _n, _c, _d in (("raw", V0, "int32"), ("TI", V0, "int32"), ("rsn", 512, "int32"), ("r16", 2048, "float16"), ("TB", 3072, "float32"),
-                   ("Z0", 1152, "float32"), ("Z1", 1152, "float32"), ("UU", 5 * US + 16, "bfloat16"),
+                   ("Z0", 2048, "float32"), ("Z1", 2048, "float32"), ("UU", 5 * US + 16, "bfloat16"),
                    ("dtb", 2064, "bfloat16"), ("NT", 2592, "bfloat16"), ("vL", 2048, "bfloat16"), ("vR", 2560, "bfloat16"),
                    ("vB", 2048, "bfloat16"), ("dL", 2048, "bfloat16"), ("dR", 2048, "bfloat16"), ("dB", 2048, "bfloat16"),
                    ("gr0", 2560, "bfloat16"), ("gr1", 2560, "bfloat16"), ("in0", 2048, "bfloat16"),
@@ -288,6 +288,8 @@ def rank_program(g, core, T, topo):
     def clear(a, z):
         op("V", [lambda: g.vector.memset(T["km"][:, 144 * a:144 * z], 0.0)], [], [(n, 0, 144) for n in MASKS[a:z]])
     iota(A("TI", 1152, V0), [[0, V0 - 1152]], 0, 0, False)
+    iota(A("pi", 0, 1), [[0, 1]], 0, 1, False)
+    iota(A("ik", 0, 16), [[-1, 16]], 16, 1, False)
     ms(A("TI", 0, 1152), 0)
     dmas([("Y", (T["TI"][i:128:16, :], [("TI", 0, V0)]), HB(n)) for i, n in ((2, "bs"), (0, "lt"), (1, "rt"))])
     ms(A("ones", 0, 128), 1.0)
@@ -296,6 +298,10 @@ def rank_program(g, core, T, topo):
         sel((X(n, 0, 144, 16), [(n, 0, 144)]), A("ones", 0, 9), [[-1, 9]], OP.is_equal, 1 - 8 * a, 1)
     dma("Y", A("thi", 0, 1), HB("th"))
     dma("Y", A("wti", 0, 1), HB("wt"))
+    ts(A("qi", 0, 1), A("pi", 0, 1), 15, OP.bitwise_and)
+    ts(A("ik2", 0, 16), A("ik", 0, 16), 15, OP.bitwise_and)
+    cp(A("qf", 0, 1), A("qi", 0, 1))
+    ts(A("pq", 0, 16), A("ik2", 0, 16), 0, OP.is_equal)
 
     ts(R("sn16", 0, 1, 0, 512), R("rsn", 0, 1, 0, 512), -1536, OP.add)
     toS("p4", 0, "zl", "sn16", 0, 512, k=(0, 1))
@@ -343,16 +349,23 @@ def rank_program(g, core, T, topo):
             ts(A("li", o, o + 32), A("p7", 32 * i, 32 * i + 32), 1536, OP.add)
             cp(A("st", o, o + 32), A("p7", 32 * i, 32 * i + 32))
 
-    def marks(n, c, q, last=False):
+    def marks(t, n, c, q):
         o = A("in%d" % (n % 2), 512 * c, 512 * c + 512)
         x = U(n, 16 + 512 * c, 16 + 512 * c + 512)
         if q == "V":
             ts(o, x, A("thf", 0, 1), OP.is_ge)
         else:
             act(o, x, AF.Sign, bias=A("thb", 0, 1))
-        one("p%d" % c, 0, 512, "eye", o, n == 0, False)
+        for b, lo, hi in banks(t, c):
+            one(b, 0, hi - lo, "eye", A("in%d" % (n % 2), lo, hi), n == 0, False)
 
-    MK = (("--V", "VVV", "VVV", "VVV", "VVS"), ("---V", "VVVV", "VVVV", "VVVS", "VVVS"))
+    def banks(t, c):
+        lo = 512 * c
+        if t or c < 2:
+            return [("p%d" % c, lo, lo + 512)]
+        return [("p2", lo, lo + 256), ("p3", lo + 256, lo + 512)]
+
+    MK = (("-VV", "VVV", "VVV", "VVV", "VVS"), ("---V", "VVVV", "VVVV", "VVVS", "VVVS"))
 
     def diff(q, n, i, t, c):
         o = L(t, i) + 16 * c
@@ -408,21 +421,45 @@ def rank_program(g, core, T, topo):
             sides(t, 2)
         for c in range(6, nc):
             diff("S", "dL", 0, t, c)
-        for c in range(mine, nc):
+        late = range(2 if t == 0 else nc, nc)
+        for c in range(mine, late.start):
             diff("S", "dR", 1, t, c)
+        if t == 0:
+            slot_flags()
         for b, c0, c1 in (("p5", 0, 64), ("p6", 64, nw)):
             one(b, 0, 2 * (c1 - c0), "n4k", A("mem", 0, 2 * (c1 - c0)), True, False)
             for i in range(2):
                 leg(b, (c1 - c0) * i, t, i, c0, c1)
         toS("p5", 0, "s2k", "dL", 0, 1024, False, False)
-        slot_flags()
-        for c in range(first, mine):
+        if t:
+            slot_flags()
+        for c in range(first, min(mine, late.start)):
             diff("V", "dR", 1, t, c)
-        toS("p5", 64, "s2k", "dR", 0, 1024, False, True)
-        toS("p6", 0, "s2k", "dL", 1024, P, False, False)
-        toS("p6", h, "s2k", "dR", 1024, P, False, True)
         legs(t, 0, 64, "p4")
-        legs(t, 64, 192, "p5")
+
+        def rest():
+            for c in late:
+                diff("V" if c < mine else "S", "dR", 1, t, c)
+            toS("p5", 64, "s2k", "dR", 0, 1024, False, True)
+            toS("p6", 0, "s2k", "dL", 1024, P, False, False)
+            toS("p6", h, "s2k", "dR", 1024, P, False, True)
+            if t:
+                legs(t, 64, 192, "p5")
+        border(t, 0, rest)
+        if t == 0:
+            legs(t, 64, 192, "p5")
+
+    def border(t, n, between):
+        gr, win = "gr%d" % (n % 2), U(n, 0, PP[t] + 544)
+        for s in range(2):
+            recv(s, str(n), ghosts(t, n, s))
+        for s in order if n < 4 else ():
+            act(A(gr, 256 * s, 256 * s + 256), ind(win, UL(t, 1, 16 * s - 32, 16 * s - 16)))
+        between()
+        for s in order if n < 4 else ():
+            o = A("sb%d" % (n + 1), 256 * s, 256 * s + 256)
+            tt(o, ind(win, UL(t, 0, 16 * s - 32, 16 * s - 16)), A(gr, 256 * s, 256 * s + 256), OP.max)
+            send(s, str(n + 1), o, ghosts(t, n + 1, 1 - s))
 
     def depths(t, slack):
         P, nw = PP[t], NW[t]
@@ -430,27 +467,11 @@ def rank_program(g, core, T, topo):
         for n in range(5):
             gr = "gr%d" % (n % 2)
             win = U(n, 0, P + 544)
-            for s in range(2):
-                recv(s, str(n), ghosts(t, n, s))
-            if n < 4:
-                for s in order:
-                    act(A(gr, 256 * s, 256 * s + 256), ind(win, UL(t, 1, 16 * s - 32, 16 * s - 16)))
-            if n == 0:
-                for f in slack.get(-1, []):
-                    f()
-            if MK[t][n][0] == "V":
-                marks(n, 0, "V")
-            if n < 4:
-                for s in order:
-                    o = A("sb%d" % (n + 1), 256 * s, 256 * s + 256)
-                    tt(o, ind(win, UL(t, 0, 16 * s - 32, 16 * s - 16)), A(gr, 256 * s, 256 * s + 256), OP.max)
-                    send(s, str(n + 1), o, ghosts(t, n + 1, 1 - s))
-            if n == 0:
-                for f in slack.get(-2, []):
-                    f()
+            if n:
+                border(t, n, lambda: [marks(t, n, c, "V") for c in range(2)])
             for c, q in enumerate(MK[t][n]):
-                if q == "V" and c:
-                    marks(n, c, q)
+                if q == "V" and (c > 1 or n == 0):
+                    marks(t, n, c, q)
             if n == 0:
                 legs(t, 192, 64 + 2 * nw, "p6")
             if n == 1:
@@ -458,7 +479,7 @@ def rank_program(g, core, T, topo):
             if n == 4:
                 for c, q in enumerate(MK[t][n]):
                     if q == "S":
-                        marks(n, c, q)
+                        marks(t, n, c, q)
             for c in range(nc):
                 r, x = A(gr, 512 + 512 * c, 1024 + 512 * c), ind(win, UL(t, 1, 32 * c, 32 * c + 32))
                 y = ind(win, UL(t, 0, 32 * c, 32 * c + 32))
@@ -472,12 +493,14 @@ def rank_program(g, core, T, topo):
                     o = A("in1", 512 * c, 512 * c + 512)
                     act(r, x, AF.Sign, bias=A("thb", 0, 1))
                     ts(o, y, A("thf", 0, 1), OP.is_ge)
-                    one("p%d" % c, 0, 512, "eye", r, False, False)
-                    one("p%d" % c, 0, 512, "eye", o, False, True)
+                    for b, lo, hi in banks(t, c):
+                        one(b, 0, hi - lo, "eye", A(gr, 512 + lo, 512 + hi), False, False)
+                    for b, lo, hi in banks(t, c):
+                        one(b, 0, hi - lo, "eye", A("in1", lo, hi), False, True)
             if n < 4:
                 for c, q in enumerate(MK[t][n]):
                     if q == "S":
-                        marks(n, c, q)
+                        marks(t, n, c, q)
             for f in slack.get(n, []):
                 f()
 
@@ -502,13 +525,13 @@ def rank_program(g, core, T, topo):
 
     def flags1(t):
         P, nw = PP[t], NW[t]
-        one("p5", 0, nw, "n4k", A("mem", 0, nw), True, False)
-        toS("p5", 0, "s2k", "dB", 0, P, False, True)
+        one("p4", 0, nw, "n4k", A("mem", 0, nw), True, False)
+        toS("p4", 0, "s2k", "dB", 0, P, False, True)
         toS("p7", 2 * nw, "s1k", "dB", 0, P, False, True)
 
     def flags2(t):
         nw = NW[t]
-        ts(A("pen", 0, nw), A("p5", 0, nw), 0, OP.not_equal)
+        ts(A("pen", 0, nw), A("p4", 0, nw), 0, OP.not_equal)
         one("p4", 0, nw, "n64", A("pen", 0, nw), True, False)
         for i in (1, 2):
             one("p4", 0, nw, "n64", A("pen", nw * i, nw * i + nw), False, False)
@@ -523,89 +546,80 @@ def rank_program(g, core, T, topo):
         ts(A("jb", 0, 1), A("pq", 0, 1), PP[t], OP.mult, A("jb", 3, 4), OP.add)
         ts(A("jb", 1, 2), A("pq", 0, 1), PP[t], OP.mult, A("jb", 2, 3), OP.add)
         for e in range(2):
-            ts((X("jr", e, 512, 2), [("jr", 0, 512)]), A("kq", 0, 256), A("pq", 1, 2), OP.mult, A("jb", e, e + 1), OP.add)
+            yield
+            ts((X("jr", e, 512, 2), [("jr%d" % e, 0, 512)]), A("kq", 0, 256), A("pq", 1, 2), OP.mult, A("jb", e, e + 1), OP.add)
+        yield
 
     def splits(t, gap):
         P, nw = PP[t], NW[t]
         nc, k = P // 512, nw // 16
-        for c, q in enumerate(("VVS", "VSVS")[t]):
-            lift = 1 + sum(MK[t][n][c] == "S" for n in range(5))
-            add(q, A("in0", 512 * c, 512 * c + 512), A("p%d" % c, 0, 512), lift)
-            one("p%d" % c, 0, 512, "eye", A("in0", 512 * c, 512 * c + 512), True, False)
+        ps = [x for c in range(nc) for x in banks(t, c)]
+        for q, (b, lo, hi) in zip("SVSV", ps):
+            lift = 1 + sum(MK[t][n][lo // 512] == "S" for n in range(5))
+            add(q, A("in0", lo, hi), A(b, 0, hi - lo), lift)
+            one(b, 0, hi - lo, "eye", A("in0", lo, hi), True, False)
         for c, q in enumerate("VS" * nc):
             add(q, A("gr1", 256 * c, 256 * c + 256), ind(A("in0", 0, P), A("pl", 16 * c, 16 * c + 16)), 0)
-            if c % 2:
-                one("p%d" % (c // 2), 0, 512, "eye", A("gr1", 256 * c - 256, 256 * c + 256), False, True)
-        for c, q in enumerate(("SVS", "VSVS")[t]):
-            b, o = A("p%d" % c, 0, 512), A("in1", 512 * c, 512 * c + 512)
+            for b, lo, hi in ps:
+                if hi == 256 * c + 256:
+                    one(b, 0, hi - lo, "eye", A("gr1", lo, hi), False, True)
+        for q, (b, lo, hi) in zip("VSVS", ps):
             if q == "S":
-                act(o, b, AF.Sign)
+                act(A("in1", lo, hi), A(b, 0, hi - lo), AF.Sign)
             else:
-                ts(o, b, 0, OP.is_gt)
-        toS("p4", 0, "cq", "in1", 0, 1024, False, False)
-        toS("p4", 64, "cq", "in1", 1024, P, False, True)
-        gap()
+                ts(A("in1", lo, hi), A(b, 0, hi - lo), 0, OP.is_gt)
+        toS("p4", 0, "cq", "in1", 0, P - 1024, False, False)
+        toS("p4", nw - 64, "cq", "in1", P - 1024, P, False, True)
+        ts(A("lf", 0, 3 * nw), A("p7", 0, 3 * nw), 1552, OP.add, 16 + GH, OP.min)
         go = A("go", 0, nw)
         ts(go, A("p4", 0, nw), 11, OP.is_ge)
         one("p5", 0, nw, "blk", go)
         one("p5", nw, 2 * nw, "eye", A("d16", 0, nw), True, False)
         one("p5", nw, 2 * nw, "nblk", go, False, True)
         for e, x in enumerate((A("me16", 0, nw), A("st", L(t, 2), L(t, 2) + nw))):
-            mm("p0", [(A("p0", nw * e, nw * e + nw), A("eye", 0, 128), x, True, False), (A("p0", nw * e, nw * e + nw), A("lt", 0, 128), go, False, True)])
+            mm("p0", [(A("p0", nw * e, nw * e + nw), A(m, 0, 128), y, m == "eye", m == "blka") for m, y in (("eye", x), ("tri", go), ("blka", go))])
         scan(A("inc", 1, nw + 1), A("p5", 0, nw), A("zer", 0, nw), OP.add, OP.add)
         tt(A("ofr", 0, nw), A("inc", 0, nw), A("p5", nw, 2 * nw), OP.max)
         act(A("val", 0, 2 * nw), A("p0", 0, 2 * nw), AF.Identity, bias=1537.0 - 32 * BIG)
         toS("p4", 0, "s0", "ofr", 0, nw)
-        ts(A("lf", 0, 3 * nw), A("p7", 0, 3 * nw), 1552, OP.add, 16 + GH, OP.min)
         cp(A("off", 0, k), A("p4", 0, k))
         for e in range(2):
-            scat(A("Z%d" % e, 0, 1152), A("off", 0, k), A("val", nw * e, nw * e + nw))
+            scat(A("Z%d" % e, 0, 2048), A("off", 0, k), A("val", nw * e, nw * e + nw))
         for e in range(2):
             scan(A("sc", 256 * e, 256 * e + 256), A("m4k", 0, 256), A("Z%d" % e, 0, 256), OP.add, OP.max)
-        ts(A("y16", 0, 512), A("sc", 0, 512), 0, OP.max, BIG, OP.min)
+        for e in range(2):
+            ts(A("y16", 256 * e, 256 * e + 256), A("sc", 256 * e, 256 * e + 256), 0, OP.max, BIG, OP.min)
         mm("p5", [(A("p5", 0, 32), M("cq", q), (X("y16", 256 * (q % 2) + q // 2, 256 * (q % 2) + 256, 8), [("y16", 0, 512)]), q == 0, q == 15)
                   for q in range(16)])
-        codes(t)
+        gap()
+        cd = codes(t)
+        next(cd)
         ts(A("ti", 0, 32), A("p5", 0, 32), -1, OP.add)
+        next(cd)
         ts(A("ti2", 0, 32), A("ti", 0, 32), 4095, OP.bitwise_and)
+        next(cd)
         tt(A("t32", 0, 32), A("ti2", 0, 32), A("meS", nw, nw + 32), OP.min)
         cp(A("TL", 0, 32), A("t32", 0, 32))
+        ts(A("big", 0, 32), A("t32", 0, 32), PP[t], OP.is_ge, BIG, OP.mult)
 
     def weigh(t):
         nw = NW[t]
         tt(A("hz", 0, 32), A("p3", 0, 32), A("t32", 0, 32), OP.add)
         tt(A("hz", 32, 64), A("p3", 0, 32), A("meS", nw, nw + 32), OP.add)
-        ts(A("big", 0, 32), A("t32", 0, 32), PP[t], OP.is_ge, BIG, OP.mult)
+        yield
         ts(A("hz2", 0, 64), A("hz", 0, 64), 2047, OP.bitwise_and)
-        tt(A("hb", 0, 32), A("hz2", 32, 64), A("big", 0, 32), OP.add)
+        yield
         cp(A("eo", 0, 32), A("hz2", 0, 32))
+        tt(A("hb", 0, 32), A("hz2", 32, 64), A("big", 0, 32), OP.add)
+        yield
         ts(A("eo", 32, 64), A("hb", 0, 32), 2048, OP.min)
+        yield
 
-    def children(t, qs):
-        P = PP[t]
-        x = [ind(A("dtb", 0, 2064), A("eo", 32 * i, 32 * i + 32)) for i in range(2)]
-        if qs == "VV":
-            tt(A("cT", 0, 512), x[0], A("e2b", 0, 512), OP.add)
-            yield
-            scat(U(0, 16, 16 + P + 512), A("TL", 0, 32), A("cT", 0, 512))
-            yield
-            tt(A("sb0", 0, 512), x[1], A("e2b", 0, 512), OP.add)
-            yield
-        else:
-            for i, b in enumerate(("p3", "p4")):
-                y = A("fs", 512 * i, 512 * i + 512)
-                act(y, x[i])
-                if i:
-                    yield
-                one(b, 0, 512, "eye", A("e2", 0, 512), True, False)
-                one(b, 0, 512, "eye", y, False, True)
-                if i == 0:
-                    act(A("cT", 0, 512), A(b, 0, 512), AF.Identity, bias=-258.0)
-            yield
-            scat(U(0, 16, 16 + P + 512), A("TL", 0, 32), A("cT", 0, 512))
-            yield
-            act(U(0, 16 + P, 16 + P + 512), A("p4", 0, 512), AF.Identity, bias=-258.0)
-            yield
+    def details(i, b):
+        y = A("fs", 512 * i, 512 * i + 512)
+        act(y, ind(A("dtb", 0, 2064), A("eo", 32 * i, 32 * i + 32)))
+        one(b, 0, 512, "eye", A("e2", 0, 512), True, False)
+        one(b, 0, 512, "eye", y, False, True)
 
     NTW = A("NT", 0, 2592)
 
@@ -615,7 +629,7 @@ def rank_program(g, core, T, topo):
     def heads(t):
         P, w = PP[t], WN[t]
         tl = A("TL", 0, 32)
-        scat(A("NT", 16, 16 + P + 512), tl, A("jr", 0, 512))
+        scat(A("NT", 16, 16 + P + 512), tl, (X("jr", 0, 512), [("jr0", 0, 512), ("jr1", 0, 512)]))
         act(A("eT", 0, 512), ind(U(0, 16, 16 + P + 512), tl))
         act(A("e2", 0, 512), A("eT", 0, 512), AF.Identity, bias=128.75, scale=0.5)
         toS("p3", 0, "wq", "eT", 0, 512)
@@ -636,26 +650,29 @@ def rank_program(g, core, T, topo):
         P, w = PP[t], WN[t]
         act(A("vy", 0, 512), ind(A("vR", 0, P + 512), A("TL", 0, 32)))
 
-    def zeroN(t):
-        one("p1", 0, 3 * WN[t], "za", A("ones", 0, 3 * WN[t]), True, False)
+    NB = ("p1", "p0", "p5")
 
     def turnN(t, n, i, x0, x1, last=False):
-        toN("p1", i * WN[t], WN[t], "wn", n, 0 if n == "vy" else x0, x0, x1, False, last)
+        toN(NB[i], 0, WN[t], "wn", n, 0 if n == "vy" else x0, x0, x1, x0 == 0, last)
 
     def early(t):
         w = WN[t]
         act(A("old", 0, 3 * w), A("p6", 0, 3 * w), AF.Identity, bias=1536.0)
         act(A("p7", 0, w), A("p2", 0, w), AF.Relu)
 
-    def update(t):
+    def update(t, i):
         w = WN[t]
-        tt(A("lrb", 0, 3 * w), A("old", 0, 3 * w), A("p1", 0, 3 * w), OP.max)
-        tt(A("ua", 0, 2 * w), A("lrb", 0, 2 * w), A("p2", 0, 2 * w), OP.min)
-        tt(A("p0", 0, w), A("p7", 0, w), A("lrb", 0, w), OP.subtract)
-        for i in range(2):
-            act(A("new", w * i, w * i + w), A("ua", w * i, w * i + w), AF.Abs)
-        tt(A("ua", 2 * w, 3 * w), A("lrb", 2 * w, 3 * w), A("p0", 0, w), OP.min)
-        act(A("new", 2 * w, 3 * w), A("ua", 2 * w, 3 * w), AF.Abs)
+        x = A("lrb", w * i, w * i + w)
+        tt(x, A("old", w * i, w * i + w), A(NB[i], 0, w), OP.max)
+        yield
+        tt(A("ua", w * i, w * i + w), x, A("p2", w * i, w * i + w) if i < 2 else A("p7", w, 2 * w), OP.min)
+        if i == 0:
+            tt(A("p7", w, 2 * w), A("p7", 0, w), x, OP.subtract)
+        yield
+
+    def size(t, i):
+        w = WN[t]
+        act(A("new", w * i, w * i + w), A("ua", w * i, w * i + w), AF.Abs)
 
     def cast(i):
         ts(R("r16", 0, 3, 512 * i, 512 * i + 512), R("raw", 0, 3, 512 * i, 512 * i + 512), -1536, OP.add)
@@ -663,8 +680,9 @@ def rank_program(g, core, T, topo):
         b = "p%d" % i
         mm(b, [(A(b, 0, 512), (X("tsel", 0, 128, 1, 0, 24), [("tsel", 0, 128)]), R("r16", 0, 3, 512 * i, 512 * i + 512), True, True)])
         add("S", A("TB", 512 * i, 512 * i + 512), A(b, 0, 512), 1536)
+    ts(A("n3", 0, 1), A("qf", 0, 1), 3, OP.is_lt)
+    ts(A("n3", 1, 2), A("pq", 3, 4), -1, OP.add)
     ts(A("snl", 0, 32), A("p4", 0, 32), 1536, OP.add)
-    iota(A("pi", 0, 1), [[0, 1]], 0, 1, False)
     sel(A("eye", 0, 128), A("ones", 0, 128), [[-1, 128]], OP.is_equal, 0, 1)
     ghost0(0, "SS")
     for s in range(2):
@@ -684,11 +702,8 @@ def rank_program(g, core, T, topo):
     turn(0, 1)
     iota(A("TB", V0, GH), [[1, 1024]], V0, 0)
     iota(A("c160", 0, 160), [[1, 160]], 0, 0)
-    iota(A("ik", 0, 16), [[-1, 16]], 16, 1, False)
-    ts(A("qi", 0, 1), A("pi", 0, 1), 15, OP.bitwise_and)
     for n in range(6):
         ms(A("UU", US * n, US * n + 16), 0.0)
-    cp(A("qf", 0, 1), A("qi", 0, 1))
     ms(A("gb", 0, 1), 1536.5 - GH)
     act(A("b0", 0, 32), A("p4", 0, 32))
     act(A("s2k", 0, 144), A("s2", 0, 144), scale=BIG)
@@ -703,6 +718,10 @@ def rank_program(g, core, T, topo):
     ts(A("thb", 0, 1), A("thi", 0, 1), -1, OP.mult, 0.5, OP.add)
     cp(A("wtf", 0, 1), A("wti", 0, 1))
     slot_lists(0)
+    ts(A("jb", 3, 4), A("pq", 4, 5), 8192, OP.mult, A("pq", 3, 4), OP.add)
+    ts(A("jb", 2, 3), A("pq", 3, 4), -2, OP.mult, A("pq", 2, 3), OP.add)
+    cp(A("snS", 0, 32), A("snl", 0, 32))
+    tt(A("jb", 2, 3), A("jb", 2, 3), A("jb", 3, 4), OP.add)
     for t in range(2):
         act(A("sh%d" % t, 0, 128), A("eye", 0, 128), scale=(PP[t] - GH) / 2)
     sides(0, 0)
@@ -710,43 +729,39 @@ def rank_program(g, core, T, topo):
     wrapped(0, 1)
     sides(0, 1)
     turn(0, 2)
-    for c in range(2):
-        marks(0, c, "V")
+    marks(0, 0, 0, "V")
     ghost_bases("VS")
-    prep(0, 2, 4)
 
     sel((X("za", 16, 144, 16), [("za", 0, 144)]), A("ones", 0, 8), [[-16, 8]], OP.is_ge, 0, 1)
     sel((X("cq", 16, 144, 16), [("cq", 0, 144)]), (X("za", 16, 144, 16), [("za", 0, 144)]), [[16, 8]], OP.is_ge, 15, -1)
     sel(A("blka", 0, 128), A("ones", 0, 128), [[-16, 8], [0, 16]], OP.is_ge, 0, 1)
     sel(A("blk", 0, 128), A("blka", 0, 128), [[16, 8], [0, 16]], OP.is_ge, 15, -1)
     sel(A("tri", 0, 128), A("blk", 0, 128), [[1, 128]], OP.is_gt, 0, -1)
-    iota(A("kq", 0, 256), [[2, 256]], 0, 0)
     fill("za", 0, 144)
-    fill("dtb", 2048, 2064, 129)
-    fill("zer", 0, 128)
+    prep(0, 0, 4)
+
+    def consts():
+        fill("zer", 0, 128)
+        fill("ones", 128, 480, 1)
+        iota(A("kq", 0, 256), [[2, 256]], 0, 0)
+        fill("dtb", 2048, 2064, 129)
+
+    def consts2():
+        iota(A("d16", 0, 128), [[8, 128]], 1024, 0)
+        fill("NT", 0, 768)
 
     def late0():
         act(A("s1k", 0, 144), A("s1", 0, 144), scale=BIG)
         act(A("meS", 0, 160), A("c160", 0, 160), AF.Identity, bias=A("qf", 0, 1), scale=16.0)
         act(A("n64", 0, 128), A("eye", 0, 128), scale=-64.0)
-        ms(A("ones", 128, 480), 1.0)
-        ts(A("ik2", 0, 16), A("ik", 0, 16), 15, OP.bitwise_and)
         ts(A("me16", 0, 128), A("meS", 0, 128), -1536, OP.add)
-        ts(A("pq", 0, 16), A("ik2", 0, 16), 0, OP.is_equal)
         ts(A("slc", 0, 32), A("meS", 0, 32), GH - 1536, OP.add)
-        cp(A("snS", 0, 32), A("snl", 0, 32))
 
     def late1():
-        ts(A("d16", 0, 128), A("c160", 0, 128), 1024, OP.add)
         ts(A("inc", 0, 1), A("zer", 0, 1), 0, OP.add)
-        ts(A("n3", 0, 1), A("qf", 0, 1), 3, OP.is_lt)
-        ts(A("n3", 1, 2), A("pq", 3, 4), -1, OP.add)
-        ts(A("jb", 3, 4), A("pq", 4, 5), 8192, OP.mult, A("pq", 3, 4), OP.add)
-        ts(A("jb", 2, 3), A("pq", 3, 4), -2, OP.mult, A("pq", 2, 3), OP.add)
-        tt(A("jb", 2, 3), A("jb", 2, 3), A("jb", 3, 4), OP.add)
-        one("p3", 0, 32, "eye", A("snS", 0, 32), True, False)
-        one("p3", 0, 32, "n4k", A("slc", 0, 32), False, False)
-        toS("p3", 0, "s1k", "gs", 0, 512, False, True)
+        one("p5", 0, 32, "eye", A("snS", 0, 32), True, False)
+        one("p5", 0, 32, "n4k", A("slc", 0, 32), False, False)
+        toS("p5", 0, "s1k", "gs", 0, 512, False, True)
         act(A("qn", 0, 1), A("qf", 0, 1), scale=96.0)
         act(A("meN", 0, 96), A("c160", 0, 96), AF.Identity, bias=A("qn", 0, 1))
 
@@ -755,10 +770,9 @@ def rank_program(g, core, T, topo):
         act(A("nblk", 0, 128), A("blk", 0, 128), scale=-BIG)
         act(A("blka", 0, 128), A("eye", 0, 128), scale=32 * BIG)
         act(A("tri", 0, 128), A("tri", 0, 128), scale=BIG)
-        tt(A("lt", 0, 128), A("tri", 0, 128), A("blka", 0, 128), OP.add)
+        ts(A("snf", 0, 32), A("p5", 0, 32), 16, OP.add, 16 + GH, OP.min)
 
     def late3():
-        ts(A("snf", 0, 32), A("p3", 0, 32), 16, OP.add, 16 + GH, OP.min)
         cp(A("sn0", 0, 32), A("snl", 0, 32))
         tt(A("dl", 0, 32), A("st", 0, 32), A("b0", 0, 32), OP.subtract)
         tt(A("dl", 32, 64), A("slc", 0, 32), A("st", 0, 32), OP.subtract)
@@ -771,11 +785,11 @@ def rank_program(g, core, T, topo):
         for e in range(2):
             fill("Z%d" % e, 0, 256)
 
-    depths(0, {-3: [lambda: wrapped(0, 2)], 0: [late0, lambda: flags0(0), lambda: bases(0, 0, 2), lambda: fill("NT", 0, 1024)],
-               1: [lambda: bases(0, 2, 4), lambda: fill("NT", 1024, 2048), late1, lambda: pens(0), lambda: olds(0)],
-               2: [lambda: bases(0, 4, 6), lambda: flags1(0), lambda: fill("NT", 2048, 2592), zs],
-               3: [late2, lambda: flags2(0), lambda: fill("m4k", 0, 256, -4096), lambda: fill("vR", V0, GH)],
-               4: [load_det]})
+    depths(0, {-3: [lambda: wrapped(0, 2)], 0: [late0, lambda: flags0(0), lambda: bases(0, 0, 1), consts],
+               1: [lambda: bases(0, 1, 3), consts2, late1, lambda: pens(0), lambda: olds(0)],
+               2: [lambda: bases(0, 3, 6), lambda: flags1(0), lambda: fill("NT", 768, 1792)],
+               3: [late2, lambda: flags2(0), lambda: fill("m4k", 0, 256, -4096), zs, lambda: fill("NT", 1792, 2592)],
+               4: [load_det, lambda: fill("vR", V0, GH)]})
     splits(0, late3)
     act(A("wq", 0, 144), A("cq", 0, 144), scale=A("wtf", 0, 1))
     act(A("wn", 0, 144), A("cq", 0, 144), scale=A("n3", 0, 1))
@@ -783,61 +797,71 @@ def rank_program(g, core, T, topo):
     act(A("mq", 0, 144), A("cq", 0, 144), scale=-1.0)
     act(A("e8k", 0, 128), A("eye", 0, 128), scale=8192.0)
     act(A("dtb", 0, 2048), A("dtb", 0, 2048), AF.Identity, bias=128.75, scale=0.5)
-    heads(0)
-    act(A("vs", 0, 512), ind(A("NT", 16, 16 + V0), A("snl", 0, 32)))
-    act(A("vs", 512, 1024), ind(NTW, A("snf", 0, 32)))
-    rename("V", 0, "vR", 1, 0, 96)
-    zeroN(0)
-    owns(0)
-    toS("p4", 0, "wn", "vs", 0, 1024)
-    rename("S", 0, "vB", 2, 0, 64)
-    news(0)
-    turnN(0, "vR", 1, 0, V0)
-    right_bases(0)
-    rename("S", 0, "vB", 2, 64, 96)
-    early(0)
-    weigh(0)
-    ts(A("sp", 0, 64), A("p4", 0, 64), 0, OP.is_gt)
-    tt(A("sn1", 0, 32), A("sn0", 0, 32), A("p4", 32, 64), OP.max)
-    tt(A("bx", 0, 64), A("sp", 0, 64), A("dl", 0, 64), OP.mult)
-    cp(A("snl", 0, 32), A("sn1", 0, 32))
-    tt(A("sp", 0, 32), A("bx", 0, 32), A("bx", 32, 64), OP.add)
-    rename("V", 0, "vL", 0, 0, 64)
-    tt(A("bx", 0, 32), A("sp", 0, 32), A("b0", 0, 32), OP.add)
-    base_send("bx")
-    turnN(0, "vB", 2, 0, 1024)
-    turnN(0, "vy", 2, V0, 2048)
-    turnN(0, "vL", 0, 0, 1024)
-    mm("p5", [(A("p5", 0, 512), M("wn", 2), A("vs", 512, 1024), True, True)])
-    rename("V", 0, "vL", 0, 64, 96)
-    turnN(0, "vB", 2, 1024, V0)
-    ch = children(0, "SS")
-    next(ch)
-    turnN(0, "vL", 0, 1024, V0, True)
-    for s in range(2):
-        x = A("snt", 16 + 272 * s, 272 + 272 * s)
-        tt(x, x, A("p5", 256 * s, 256 * s + 256), OP.max)
-    next(ch)
-    update(0)
 
     def rows(i):
-        return (T["TB"][i:128:16, 0:2048], [("TB", 0, 2048)])
+        return ("Y", (T["TB"][i:128:16, 0:2048], [("TB", 0, 2048)]), A("new", 128 * i, 128 * i + 128))
 
     def half(i):
         ts(A("n16", 128 * i, 128 * i + 128), A("new", 128 * i, 128 * i + 128), -1536, OP.add)
         dma("Y", R("r16", i, i + 1, 0, 2048), A("n16", 128 * i, 128 * i + 128))
+    heads(0)
+    act(A("vs", 0, 512), ind(A("NT", 16, 16 + V0), A("snl", 0, 32)))
+    act(A("vs", 512, 1024), ind(NTW, A("snf", 0, 32)))
+    owns(0)
+    news(0)
+    rename("V", 0, "vR", 1, 0, 96)
+    toS("p4", 0, "wn", "vs", 0, 1024)
+    rename("S", 0, "vL", 0, 0, 64)
+    turnN(0, "vR", 1, 0, V0, True)
+    right_bases(0)
+    rename("S", 0, "vL", 0, 64, 96)
+    early(0)
+    rename("S", 0, "vB", 2, 64, 96)
+    rename("V", 0, "vB", 2, 0, 64)
+    turnN(0, "vL", 0, 0, V0, True)
+    turnN(0, "vB", 2, 0, 1024)
+    turnN(0, "vy", 2, V0, 2048)
+    turnN(0, "vB", 2, 1024, V0, True)
+    wg, up = weigh(0), [update(0, i) for i in range(3)]
+    ts(A("sp", 0, 64), A("p4", 0, 64), 0, OP.is_gt)
+    next(wg)
+    tt(A("bx", 0, 64), A("sp", 0, 64), A("dl", 0, 64), OP.mult)
+    next(wg)
+    tt(A("sn1", 0, 32), A("sn0", 0, 32), A("p4", 32, 64), OP.max)
+    tt(A("sp", 0, 32), A("bx", 0, 32), A("bx", 32, 64), OP.add)
+    next(wg)
+    tt(A("bx", 0, 32), A("sp", 0, 32), A("b0", 0, 32), OP.add)
+    next(wg)
+    details(0, "p3")
+    next(up[1])
+    base_send("bx")
+    next(up[0])
+    next(up[1])
+    cp(A("snl", 0, 32), A("sn1", 0, 32))
+    next(up[0])
+    size(0, 0)
+    size(0, 1)
+    mm("p0", [(A("p0", 0, 512), M("wn", 2), A("vs", 512, 1024), True, True)])
+    next(up[2])
     half(0)
+    next(up[2])
+    size(0, 2)
     half(1)
-    dmas([("Y", rows(i), A("new", 128 * i, 128 * i + 128)) for i in range(3)])
+    dmas([rows(i) for i in range(3)])
+    act(A("cT", 0, 512), A("p3", 0, 512), AF.Identity, bias=-258.0)
     half(2)
+    details(1, "p4")
+    for s in range(2):
+        x = A("snt", 16 + 272 * s, 272 + 272 * s)
+        tt(x, x, A("p0", 256 * s, 256 * s + 256), OP.max)
+    scat(U(0, 16, 16 + 2048), A("TL", 0, 32), A("cT", 0, 512))
     ghost_bases("SS")
-    next(ch)
-    next(ch)
+    act(U(0, 16 + V0, 16 + 2048), A("p4", 0, 512), AF.Identity, bias=-258.0)
     ghost0(1, "SS")
-    for i in range(2):
-        turn(1, i)
+    turn(1, 0)
+    turn(1, 1)
     for c in range(3):
-        marks(0, c, "V")
+        marks(1, 0, c, "V")
     wrapped(1, 0)
     sides(1, 0)
     slots(1)
@@ -845,34 +869,52 @@ def rank_program(g, core, T, topo):
     slot_legs(1)
     prep(1, 2, 5)
     turn(1, 2)
-    depths(1, {-3: [lambda: wrapped(1, 2)], 0: [lambda: flags0(1), lambda: bases(1, 0, 2), lambda: fill("NT", 16, 1040), lambda: olds(1)],
-               1: [lambda: bases(1, 2, 5), lambda: fill("NT", 1040, 2064), lambda: pens(1)],
-               2: [lambda: bases(1, 5, 8), lambda: flags1(1), zs],
+    depths(1, {-3: [lambda: wrapped(1, 2)], 0: [lambda: flags0(1), lambda: bases(1, 0, 3), lambda: fill("NT", 16, 1040), lambda: olds(1)],
+               1: [lambda: bases(1, 3, 6), lambda: fill("NT", 1040, 2064), lambda: pens(1)],
+               2: [lambda: bases(1, 6, 8), lambda: flags1(1), zs],
                3: [lambda: flags2(1)]})
     splits(1, lambda: None)
+    act(A("dtb", 0, 2064), A("dtb", 0, 2064), AF.Identity, bias=-258.0)
+
+    def out(i):
+        size(1, i)
+        dma("Y", HB(("yl", "yr", "yb")[i]), A("new", 160 * i, 160 * i + 160))
     heads(1)
-    act(A("e2b", 0, 512), A("e2", 0, 512), AF.Identity, bias=-258.0)
     rename("S", 1, "vR", 1, 0, 128)
-    zeroN(1)
     owns(1)
+    wg, up = weigh(1), [update(1, i) for i in range(3)]
+    next(wg)
     news(1)
-    weigh(1)
-    ch = children(1, "VV")
-    next(ch)
-    next(ch)
+    next(wg)
+    rename("V", 1, "vL", 0, 0, 32)
+    next(wg)
+    x = [ind(A("dtb", 0, 2064), A("eo", 32 * i, 32 * i + 32)) for i in range(2)]
+    tt(A("cT", 0, 512), x[0], A("e2", 0, 512), OP.add)
+    next(wg)
+    rename("V", 1, "vL", 0, 32, 48)
+    scat(U(0, 16, 16 + GH), A("TL", 0, 32), A("cT", 0, 512))
     dma("Y", (T["ye"][:, 0:2048], []), U(0, 16, 16 + 2048))
+    turnN(1, "vR", 1, 0, 2048, True)
     right_bases(1)
     early(1)
-    turnN(1, "vR", 1, 0, 2048)
+    rename("S", 1, "vL", 0, 96, 128)
+    next(up[1])
+    rename("V", 1, "vL", 0, 48, 96)
+    next(up[1])
+    rename("S", 1, "vB", 2, 0, 64)
+    out(1)
+    turnN(1, "vL", 0, 0, 2048, True)
+    turnN(1, "vB", 2, 0, 1024)
     turnN(1, "vy", 2, 2048, GH)
-    for c0, c1 in ((0, 96), (96, 128)):
-        rename("S", 1, "vB", 2, c0, c1)
-        rename("V", 1, "vL", 0, c0, c1)
-        turnN(1, "vL", 0, 16 * c0, 16 * c1)
-        turnN(1, "vB", 2, 16 * c0, 16 * c1, c1 == 128)
-    next(ch)
+    rename("V", 1, "vB", 2, 96, 128)
+    rename("S", 1, "vB", 2, 64, 96)
+    next(up[0])
+    turnN(1, "vB", 2, 1024, 2048, True)
+    tt(A("sb0", 0, 512), x[1], A("e2", 0, 512), OP.add)
     dma("Y", (T["ye"][:, 2048:GH], []), A("sb0", 0, 512))
-    update(1)
-    for i, n in enumerate(("yl", "yr", "yb")):
-        dma("Y", HB(n), A("new", 160 * i, 160 * i + 160))
+    next(up[0])
+    out(0)
+    next(up[2])
+    next(up[2])
+    out(2)
     wait_for("Y", {s: v for s, v in cnt.items()})

import numpy as np
from concourse.mybir import dt, AluOpType, AxisListType, ActivationFunctionType

OP = AluOpType
AF = ActivationFunctionType
NR = 4
V0 = 1536
GH = 2560
US = 2576
BIG = 4096.0

SCRATCH = {}
PK = {}


def _pack(big, dtype, parts):
    o = 0
    for n, c in parts:
        PK[n] = (big, o)
        o += (c + 15) // 16 * 16
    SCRATCH[big] = ("sbuf", [128, o], dtype)


MASKS = ("zl", "zr", "zb", "s0", "s1", "s2", "s3", "za", "cq")
_pack("km", "bfloat16", [(n, 144) for n in MASKS])
_pack("kf", "float32", (("pq", 16), ("qf", 1), ("qn", 1), ("meS", 160), ("zer", 128), ("thf", 1), ("thb", 1), ("wtf", 1), ("jb", 4),
                        ("n3", 2), ("gb", 1), ("meN", 96), ("sn0", 32), ("sn1", 32), ("old", 480), ("val", 256), ("m4k", 256),
                        ("sc", 512), ("t32", 32), ("lrb", 480), ("nsp", 480), ("ua", 480), ("new", 480),
                        ("big", 32), ("hb", 64), ("c160", 160), ("snt", 560), ("b0", 32), ("dl", 64), ("sp", 64), ("bx", 64)))
_pack("ki", "int32", (("thi", 1), ("wti", 1), ("ik", 16), ("ik2", 16), ("pi", 1), ("qi", 1), ("ti", 32), ("ti2", 32),
                      ("hz", 64), ("hz2", 64)))
_pack("ku", "uint16", (("li", 448), ("snl", 32), ("gbo", 32), ("bo", 32), ("ul", 320), ("pl", 128), ("off", 8), ("TL", 32), ("lf", 384),
                       ("snf", 32), ("eo", 64)))
_pack("kh", "float16", (("sn16", 512), ("gs", 512), ("st", 448), ("snS", 32), ("slc", 32), ("me16", 128),
                        ("inc", 144), ("ofr", 128), ("y16", 512), ("n16", 384), ("gf", 512)))
_pack("kb", "bfloat16", (("ones", 480), ("e8k", 128), ("mn", 144), ("mq", 144), ("sh0", 128), ("sh1", 128), ("isg", 320), ("d16", 128), ("eye", 128), ("blk", 128), ("blka", 128), ("tri", 128), ("lt", 128), ("n64", 128), ("n4k", 128),
                         ("ts0", 128), ("tsel", 128), ("s1k", 144), ("s2k", 144), ("wn", 144), ("wq", 144), ("nblk", 128), ("mem", 384),
                         ("mem0", 384), ("kq", 256), ("jr", 512), ("go", 128), ("pen", 384), ("eT", 512), ("e2", 512), ("e2b", 512),
                         ("cT", 512), ("vs", 1024), ("vy", 512), ("fs", 1024),
                         ("sb0", 512), ("sb1", 512), ("sb2", 512), ("sb3", 512), ("sb4", 512)))
for _n, _c, _d in (("raw", V0, "int32"), ("TI", V0, "int32"), ("rsn", 512, "int32"), ("r16", 2048, "float16"), ("TB", 3072, "float32"),
                   ("Z0", 2048, "float32"), ("Z1", 2048, "float32"), ("UU", 5 * US + 16, "bfloat16"),
                   ("dtb", 2064, "bfloat16"), ("NT", 2592, "bfloat16"), ("vL", 2048, "bfloat16"), ("vR", 2560, "bfloat16"),
                   ("vB", 2048, "bfloat16"), ("dL", 2048, "bfloat16"), ("dR", 2048, "bfloat16"), ("dB", 2048, "bfloat16"),
                   ("gr0", 2560, "bfloat16"), ("gr1", 2560, "bfloat16"), ("in0", 2048, "bfloat16"),
                   ("in1", 2048, "bfloat16")):
    SCRATCH[_n] = ("sbuf", [128, _c], _d)
for _n in range(8):
    SCRATCH["p%d" % _n] = ("psum", [128, 512], "float32")

KINDS = ["b", "0", "1", "2", "3", "4"]
SEMAPHORES = (["cv", "cs", "cp", "cg"] + ["d%d" % i for i in range(32)]
              + ["r%s%d" % (k, s) for k in KINDS for s in range(2)] + ["l%s%d" % (k, s) for k in KINDS for s in range(2)])


def _is_psum(n):
    return len(n) == 2 and n[0] == "p" and n[1].isdigit()


def rank_program(g, core, T, topo):
    rank = T.rank_of(core)
    if rank is None:
        return
    nb_core = [T.cores[(rank - 1) % NR], T.cores[(rank + 1) % NR]]
    order = sorted(range(2), key=lambda s: nb_core[s] in topo.cores_of(core))

    Q = {"V": g.vector, "S": g.scalar, "P": g.tensor, "G": g, "Y": g.sync}
    SEM = {"V": "cv", "S": "cs", "P": "cp", "G": "cg"}
    cnt = {}
    known = {q: {} for q in Q}
    snaps = {}
    hist = {}

    def wait_for(q, need):
        for s in sorted(need):
            v = need[s]
            if known[q].get(s, 0) >= v:
                continue
            Q[q].wait_ge(T.sem[s], v)
            known[q][s] = v
            for s2, v2 in snaps.get((s, v), {}).items():
                if known[q].get(s2, 0) < v2:
                    known[q][s2] = v2

    def needs(q, reads, writes):
        need = {}
        for regs, w in ((reads, 0), (writes, 1)):
            for n, lo, hi in regs:
                ps = _is_psum(n)
                for e in hist.get(n, []):
                    if not ps and (e[0] >= hi or lo >= e[1]):
                        continue
                    if ps:
                        if e[5] == q and (q == "P" or not (w or e[2])):
                            continue
                    elif not (w or e[2]):
                        continue
                    if need.get(e[3], 0) < e[4]:
                        need[e[3]] = e[4]
        return need

    def note(q, reads, writes, sem, val):
        snaps[(sem, val)] = dict(known[q]) if q else {}
        for regs, w in ((writes, 1), (reads, 0)):
            for n, lo, hi in regs:
                old = hist.get(n, [])
                if w:
                    old = [e for e in old if not (lo <= e[0] and e[1] <= hi)]
                else:
                    old = [e for e in old if not (e[2] == 0 and e[3] == sem and lo <= e[0] and e[1] <= hi)]
                old.append((lo, hi, w, sem, val, q))
                hist[n] = old

    def op(q, fns, reads, writes):
        wait_for(q, needs(q, reads, writes))
        s = SEM[q]
        for f in fns:
            f().then_inc(T.sem[s], 1)
            cnt[s] = cnt.get(s, 0) + 1
        note(q, reads, writes, s, cnt[s])

    ndma = [0]

    def dmas(jobs, done=None, more=False):
        done = [] if done is None else done
        for q, out, in_ in jobs:
            wait_for(q, needs(q, in_[1], out[1]))
            s = "d%d" % ndma[0]
            ndma[0] += 1
            Q[q].dma_start(out[0], in_[0]).then_inc(T.sem[s], 16)
            cnt[s] = 16
            snaps[(s, 16)] = dict(known[q])
            done.append((q, out, in_, s))
        if more:
            return done
        for q, out, in_, s in done:
            for regs, w in ((out[1], 1), (in_[1], 0)):
                for n, lo, hi in regs:
                    hist.setdefault(n, []).append((lo, hi, w, s, 16, q))

    def dma(q, out, in_):
        dmas([(q, out, in_)])

    def X(n, lo, hi, st=1, p0=0, p1=128):
        if n in PK:
            t, o = T[PK[n][0]], PK[n][1]
        else:
            t, o = T[n], 0
        return t[p0:p1, o + lo:o + hi] if st == 1 else t[p0:p1, o + lo:o + hi:st]

    def A(n, lo, hi, st=1):
        return (X(n, lo, hi, st), [(n, lo, hi)])

    def R(n, k0, k1, lo, hi, st=1):
        return (X(n, lo, hi, st, 8 * k0, 8 * k1), [("%s:%d" % (n, k), lo, hi) for k in range(k0, k1)])

    def U(n, lo, hi):
        return A("UU", US * n + lo, US * n + hi)

    def ind(w, o):
        return (w[0].indirect(o[0]), w[1] + o[1])

    def tt(out, a, b, f):
        op("V", [lambda: g.vector.tensor_tensor(out[0], a[0], b[0], f)], a[1] + b[1], out[1])

    def ts(out, a, s1, f1, s2=None, f2=None):
        r = list(a[1])
        v = []
        for s in (s1, s2):
            if isinstance(s, tuple):
                r += s[1]
                s = s[0]
            v.append(s)
        if f2 is None:
            op("V", [lambda: g.vector.tensor_scalar(out[0], a[0], v[0], None, f1)], r, out[1])
        else:
            op("V", [lambda: g.vector.tensor_scalar(out[0], a[0], v[0], v[1], f1, f2)], r, out[1])

    def cp(out, a):
        op("V", [lambda: g.vector.tensor_copy(out[0], a[0])], a[1], out[1])

    def scat(w, o, a):
        op("V", [lambda: g.vector.tensor_copy(w[0].indirect(o[0]), a[0])], a[1] + o[1], w[1])

    def scan(out, a, b, f0, f1):
        op("V", [lambda: g.vector.tensor_tensor_scan(out[0], a[0], b[0], 0.0, f0, f1)], a[1] + b[1], out[1])

    def ms(out, v):
        op("V", [lambda: g.vector.memset(out[0], v)], [], out[1])

    def act(out, a, f=AF.Copy, bias=0.0, scale=1.0):
        r = list(a[1])
        sc = scale
        if isinstance(scale, tuple):
            r += scale[1]
            sc = scale[0]
        bi = bias
        if isinstance(bias, tuple):
            r += bias[1]
            bi = bias[0]
        op("S", [lambda: g.scalar.activation(out[0], a[0], f, bias=bi, scale=sc)], r, out[1])

    def add(q, out, a, v):
        if q == "S":
            act(out, a, AF.Identity, bias=float(v))
        else:
            ts(out, a, v, OP.add)

    def iota(out, pattern, base, cm, small=True):
        if small:
            op("G", [lambda: g.iota(out[0], pattern, base, cm, allow_small_or_imprecise_dtypes=True)], [], out[1])
        else:
            op("G", [lambda: g.iota(out[0], pattern, base, cm)], [], out[1])

    def fill(n, lo, hi, v=0):
        iota(A(n, lo, hi), [[0, hi - lo]], v, 0)

    def sel(out, a, pattern, cmp, base, cm):
        op("G", [lambda: g.affine_select(out[0], a[0], pattern, cmp, 0.0, base, cm)], a[1], out[1])

    def mm(b, jobs):
        fns, rd = [], []
        for o, l, r, s0, s1 in jobs:
            fns.append(lambda o=o, l=l, r=r, s0=s0, s1=s1: g.tensor.matmul(o[0], l[0], r[0], s0, s1))
            for x in l[1] + r[1]:
                if x not in rd:
                    rd.append(x)
        op("P", fns, rd, [(b, 0, 512)])

    def M(m, q, k=128):
        return (X(m, 16 - q, 144 - q, 1, 0, k), [(m, 0, 144)])

    def one(b, lo, hi, m, x, s0=True, s1=True):
        mm(b, [(A(b, lo, hi), A(m, 0, 128), x, s0, s1)])

    def toS(b, lo, m, n, c0, c1, s0=True, s1=True, k=None):
        js = []
        for q in range(16):
            x = (X(n, c0 + q, c1, 16), [(n, c0, c1)]) if k is None else R(n, k[0], k[1], c0 + q, c1, 16)
            js.append((A(b, lo, lo + (c1 - c0) // 16), M(m, q, 128 if k is None else 8 * k[1]), x, s0 and q == 0, s1 and q == 15))
        mm(b, js)

    def toN(b, lo, w, m, n, c0, x0, x1, s0=True, s1=True, k=None):
        ps = [(q, max(x0, w * q), min(x1, w * q + w)) for q in range(16)]
        ps = sorted([p for p in ps if p[1] < p[2]], key=lambda p: p[1] - p[2])
        js = []
        for i, (q, a, z) in enumerate(ps):
            x = A(n, c0 + a - x0, c0 + z - x0) if k is None else R(n, k[0], k[1], c0 + a - x0, c0 + z - x0)
            js.append((A(b, lo + a - w * q, lo + z - w * q), M(m, q, 128 if k is None else 8 * k[1]), x, s0 and i == 0, s1 and i == len(ps) - 1))
        mm(b, js)

    def chosen(src, dst):
        return topo.engines(src, dst)[-8:]

    def send(s, kind, src, dst):
        d = nb_core[s]
        wait_for("G", needs("G", src[1], []))
        rid, pid = topo.addr(d, core)
        es = chosen(core, d)
        ls = "l%s%d" % (kind, s)
        g.remote_dma(dst[0], src[0], T.sem["r%s%d" % (kind, 1 - s)], T.sem[ls], pid, rid, sum(1 << e for e in es))
        cnt[ls] = cnt.get(ls, 0) + len(es)
        note("G", src[1], [], ls, cnt[ls])

    def recv(s, kind, dst):
        rs = "r%s%d" % (kind, s)
        cnt[rs] = cnt.get(rs, 0) + len(chosen(nb_core[s], core))
        note(None, [], dst[1], rs, cnt[rs])

    def ghosts(t, n, s):
        return U(n, 16 + PP[t] + 256 * s, 16 + PP[t] + 256 * s + 256)

    def HB(n):
        return (T[n][:], [])

    PP, NW, WN = (V0, 2048), (96, 128), (128, 160)
    KZ = ("zl", "zr", "zb")
    TB_ = ("p5", "p6", "p7")

    def L(t, i):
        return i * (NW[t] + 32) + (32 if i < 2 else 0)

    dma("Y", R("rsn", 0, 1, 0, 512), HB("snd"))
    for i, (q, n) in enumerate((("S", "lt"), ("Y", "rt"), ("S", "bs"))):
        dma(q, R("raw", i, i + 1, 0, V0), HB(n))
    dma("S", U(0, 16, 16 + V0), HB("err"))

    def clear(a, z):
        op("V", [lambda: g.vector.memset(T["km"][:, 144 * a:144 * z], 0.0)], [], [(n, 0, 144) for n in MASKS[a:z]])
    iota(A("TI", 1152, V0), [[0, V0 - 1152]], 0, 0, False)
    iota(A("pi", 0, 1), [[0, 1]], 0, 1, False)
    iota(A("ik", 0, 16), [[-1, 16]], 16, 1, False)
    ms(A("TI", 0, 1152), 0)
    dmas([("Y", (T["TI"][i:128:16, :], [("TI", 0, V0)]), HB(n)) for i, n in ((2, "bs"), (0, "lt"), (1, "rt"))])
    ms(A("ones", 0, 128), 1.0)
    clear(0, 3)
    for a, n in enumerate(KZ):
        sel((X(n, 0, 144, 16), [(n, 0, 144)]), A("ones", 0, 9), [[-1, 9]], OP.is_equal, 1 - 8 * a, 1)
    dma("Y", A("thi", 0, 1), HB("th"))
    dma("Y", A("wti", 0, 1), HB("wt"))
    ts(A("qi", 0, 1), A("pi", 0, 1), 15, OP.bitwise_and)
    ts(A("ik2", 0, 16), A("ik", 0, 16), 15, OP.bitwise_and)
    cp(A("qf", 0, 1), A("qi", 0, 1))
    ts(A("pq", 0, 16), A("ik2", 0, 16), 0, OP.is_equal)

    ts(R("sn16", 0, 1, 0, 512), R("rsn", 0, 1, 0, 512), -1536, OP.add)
    toS("p4", 0, "zl", "sn16", 0, 512, k=(0, 1))
    mm("p5", [(A("p5", 0, 512), M("zl", 2, 8), R("sn16", 0, 1, 0, 512), True, True)])
    clear(3, 9)
    sel(A("tsel", 0, 128), A("ones", 0, 128), [[-1, 8], [-8, 16]], OP.is_equal, 0, 1)
    for a in (2, 0, 1, 3):
        n = "s%d" % a
        sel((X(n, 16, 144, 16), [(n, 0, 144)]), A("ones", 0, 8), [[-16, 8]], OP.is_equal, -a, 1)

    def ghost0(t, qs):
        for q, s in zip(qs, order):
            add(q, A("sb0", 256 * s, 256 * s + 256), ind(U(0, 16, 16 + PP[t]), A("snl", 16 * s, 16 * s + 16)), 0)
            send(s, "0", A("sb0", 256 * s, 256 * s + 256), ghosts(t, 0, 1 - s))

    def base_send(x):
        for s in order:
            ts(A("bo", 16 * s, 16 * s + 16), A(x, 16 * s, 16 * s + 16), 16 - 1024 - 256 * s, OP.add, 272, OP.min)
            send(s, "b", A("bo", 16 * s, 16 * s + 16), A("gbo", 16 * (1 - s), 16 * (1 - s) + 16))

    def ghost_bases(qs):
        for q, s in zip(qs, order[::-1]):
            recv(s, "b", A("gbo", 16 * s, 16 * s + 16))
            add(q, A("TB", GH + 256 * s, GH + 256 * s + 256), ind(A("snt", 272 * s, 272 * s + 288), A("gbo", 16 * s, 16 * s + 16)), 0)

    def turn(t, i):
        toS(TB_[i], 0, KZ[i], "r16", 0, PP[t], k=(0, i + 1))

    def wrapped(t, i):
        nw = NW[t]
        o = L(t, i)
        ts(A("li", o, o + nw), A(TB_[i], 0, nw), 1536, OP.add)
        cp(A("st", o, o + nw), A(TB_[i], 0, nw))

    def slots(t):
        ts(A("gs", 0, 512), ind(A("TB" if t else "TI", 0, PP[t]), A("snl", 0, 32)), -1536, OP.add)

    def slot_legs(t):
        for i in range(2):
            toS("p7", 32 * i, "s%d" % i, "gs", 0, 512)

    def slot_lists(t):
        for i in range(2):
            o = L(t, i) - 32
            ts(A("li", o, o + 32), A("p7", 32 * i, 32 * i + 32), 1536, OP.add)
            cp(A("st", o, o + 32), A("p7", 32 * i, 32 * i + 32))

    def marks(t, n, c, q):
        o = A("in%d" % (n % 2), 512 * c, 512 * c + 512)
        x = U(n, 16 + 512 * c, 16 + 512 * c + 512)
        if q == "V":
            ts(o, x, A("thf", 0, 1), OP.is_ge)
        else:
            act(o, x, AF.Sign, bias=A("thb", 0, 1))
        for b, lo, hi in banks(t, c):
            one(b, 0, hi - lo, "eye", A("in%d" % (n % 2), lo, hi), n == 0, False)

    def banks(t, c):
        lo = 512 * c
        if t or c < 2:
            return [("p%d" % c, lo, lo + 512)]
        return [("p2", lo, lo + 256), ("p3", lo + 256, lo + 512)]

    MK = (("-VV", "VVV", "VVV", "VVV", "VVS"), ("---V", "VVVV", "VVVV", "VVVS", "VVVS"))

    def diff(q, n, i, t, c):
        o = L(t, i) + 16 * c
        add(q, A(n, 256 * c, 256 * c + 256), ind(A("TB", 0, 3072), A("li", o, o + 16)), -256 * c)

    def keep(b, lo, t, i, c0, c1, s1=False):
        mm(b, [(A(b, lo, lo + c1 - c0), A("eye", 0, 128), A("st", L(t, i) + c0, L(t, i) + c1), False, s1)])

    def sides(t, i):
        nw = NW[t]
        if i < 2:
            act(A("isg", 64 + nw * i, 64 + nw * i + nw), A(TB_[i], 0, nw), AF.Sign, bias=A("gb", 0, 1))
        else:
            act(A("isg", 0, 64), A("p7", 0, 64), AF.Sign, bias=A("gb", 0, 1))

    def leg(b, lo, t, i, c0, c1):
        keep(b, lo, t, i, c0, c1)
        o = 32 * i + 32 + c0 if c0 < 0 else 64 + NW[t] * i + c0
        one(b, lo, lo + c1 - c0, "sh%d" % t, A("isg", o, o + c1 - c0), False, False)

    def legs(t, lo, hi, b):
        ts(A("ul", lo, hi), A(b, 0, hi - lo), 1552 - (GH - PP[t]) // 2, OP.add, PP[t] + 528, OP.min)

    def UL(t, i, c0, c1):
        nw = NW[t]
        o = 32 * i + 32 + c0 if c0 < 0 else 64 + 64 * i + c0 if c0 < 64 else 192 + (nw - 64) * i + c0 - 64
        return A("ul", o, o + c1 - c0)

    def prep(t, first, mine):
        P, nw = PP[t], NW[t]
        nc, h = P // 256, nw - 64

        def slot_flags():
            one("p4", 0, 64, "n4k", A("ones", 0, 64), True, False)
            for i in range(2):
                leg("p4", 32 * i, t, i, -32, 0)
            for i in range(2):
                for s in range(2):
                    o = L(t, i) - 32 + 16 * s
                    tt(A("fs", 512 * i + 256 * s, 512 * i + 256 * s + 256), ind(A("TB", 0, 3072), A("li", o, o + 16)),
                       A("snt", 16 + 272 * s, 272 + 272 * s), OP.is_equal)
            toS("p4", 0, "s2k", "fs", 0, 1024, False, True)
        for c in range(3):
            diff("S", "dL", 0, t, c)
        if t:
            sides(t, 1)
        for c in range(first):
            diff("V", "dR", 1, t, c)
        for c in range(3, 6):
            diff("S", "dL", 0, t, c)
        if t:
            slot_lists(t)
            sides(t, 2)
        for c in range(6, nc):
            diff("S", "dL", 0, t, c)
        late = range(2 if t == 0 else nc, nc)
        for c in range(mine, late.start):
            diff("S", "dR", 1, t, c)
        if t == 0:
            slot_flags()
        for b, c0, c1 in (("p5", 0, 64), ("p6", 64, nw)):
            one(b, 0, 2 * (c1 - c0), "n4k", A("mem", 0, 2 * (c1 - c0)), True, False)
            for i in range(2):
                leg(b, (c1 - c0) * i, t, i, c0, c1)
        toS("p5", 0, "s2k", "dL", 0, 1024, False, False)
        if t:
            slot_flags()
        for c in range(first, min(mine, late.start)):
            diff("V", "dR", 1, t, c)
        legs(t, 0, 64, "p4")

        def rest():
            for c in late:
                diff("V" if c < mine else "S", "dR", 1, t, c)
            toS("p5", 64, "s2k", "dR", 0, 1024, False, True)
            toS("p6", 0, "s2k", "dL", 1024, P, False, False)
            toS("p6", h, "s2k", "dR", 1024, P, False, True)
            if t:
                legs(t, 64, 192, "p5")
        border(t, 0, rest)
        if t == 0:
            legs(t, 64, 192, "p5")

    def border(t, n, between):
        gr, win = "gr%d" % (n % 2), U(n, 0, PP[t] + 544)
        for s in range(2):
            recv(s, str(n), ghosts(t, n, s))
        for s in order if n < 4 else ():
            act(A(gr, 256 * s, 256 * s + 256), ind(win, UL(t, 1, 16 * s - 32, 16 * s - 16)))
        between()
        for s in order if n < 4 else ():
            o = A("sb%d" % (n + 1), 256 * s, 256 * s + 256)
            tt(o, ind(win, UL(t, 0, 16 * s - 32, 16 * s - 16)), A(gr, 256 * s, 256 * s + 256), OP.max)
            send(s, str(n + 1), o, ghosts(t, n + 1, 1 - s))

    def depths(t, slack):
        P, nw = PP[t], NW[t]
        nc = P // 512
        for n in range(5):
            gr = "gr%d" % (n % 2)
            win = U(n, 0, P + 544)
            if n:
                border(t, n, lambda: [marks(t, n, c, "V") for c in range(2)])
            for c, q in enumerate(MK[t][n]):
                if q == "V" and (c > 1 or n == 0):
                    marks(t, n, c, q)
            if n == 0:
                legs(t, 192, 64 + 2 * nw, "p6")
            if n == 1:
                fill("UU", 16 + P, 16 + P + 512)
            if n == 4:
                for c, q in enumerate(MK[t][n]):
                    if q == "S":
                        marks(t, n, c, q)
            for c in range(nc):
                r, x = A(gr, 512 + 512 * c, 1024 + 512 * c), ind(win, UL(t, 1, 32 * c, 32 * c + 32))
                y = ind(win, UL(t, 0, 32 * c, 32 * c + 32))
                if n < 4:
                    act(r, x)
                    tt(U(n + 1, 16 + 512 * c, 16 + 512 * c + 512), y, r, OP.max)
                    if n == 0 and c == 0:
                        for f in slack.get(-3, []):
                            f()
                else:
                    o = A("in1", 512 * c, 512 * c + 512)
                    act(r, x, AF.Sign, bias=A("thb", 0, 1))
                    ts(o, y, A("thf", 0, 1), OP.is_ge)
                    for b, lo, hi in banks(t, c):
                        one(b, 0, hi - lo, "eye", A(gr, 512 + lo, 512 + hi), False, False)
                    for b, lo, hi in banks(t, c):
                        one(b, 0, hi - lo, "eye", A("in1", lo, hi), False, True)
            if n < 4:
                for c, q in enumerate(MK[t][n]):
                    if q == "S":
                        marks(t, n, c, q)
            for f in slack.get(n, []):
                f()

    def flags0(t):
        P, nw = PP[t], NW[t]
        one("p7", 0, 3 * nw, "n4k", A("mem", 0, 3 * nw), True, False)
        for i in range(3):
            keep("p7", nw * i, t, i, 0, nw)
        toS("p7", 0, "s1k", "dL", 0, P, False, False)
        toS("p7", nw, "s1k", "dR", 0, P, False, False)

    def bases(t, c0, c1):
        for c in range(c0, c1):
            diff("S", "dB", 2, t, c)

    def pens(t):
        P, nw = PP[t], NW[t]
        b = A("st", L(t, 2), L(t, 2) + nw)
        ts(A("pl", 0, nw), b, 1536, OP.add, P - 1, OP.min)
        ts(A("pen", nw, 2 * nw), b, GH - 1536, OP.is_ge)
        tt(A("pen", 2 * nw, 3 * nw), A("me16", 0, nw), b, OP.is_ge)

    def flags1(t):
        P, nw = PP[t], NW[t]
        one("p4", 0, nw, "n4k", A("mem", 0, nw), True, False)
        toS("p4", 0, "s2k", "dB", 0, P, False, True)
        toS("p7", 2 * nw, "s1k", "dB", 0, P, False, True)

    def flags2(t):
        nw = NW[t]
        ts(A("pen", 0, nw), A("p4", 0, nw), 0, OP.not_equal)
        one("p4", 0, nw, "n64", A("pen", 0, nw), True, False)
        for i in (1, 2):
            one("p4", 0, nw, "n64", A("pen", nw * i, nw * i + nw), False, False)

    def olds(t):
        P, w = PP[t], WN[t]
        one("p6", 0, 3 * w, "za", A("ones", 0, 3 * w), True, False)
        for i, m in enumerate(KZ):
            toN("p6", w * i, w, m, "r16", 0, 0, P, False, False, k=(0, i + 1))

    def codes(t):
        ts(A("jb", 0, 1), A("pq", 0, 1), PP[t], OP.mult, A("jb", 3, 4), OP.add)
        ts(A("jb", 1, 2), A("pq", 0, 1), PP[t], OP.mult, A("jb", 2, 3), OP.add)
        for e in range(2):
            yield
            ts((X("jr", e, 512, 2), [("jr%d" % e, 0, 512)]), A("kq", 0, 256), A("pq", 1, 2), OP.mult, A("jb", e, e + 1), OP.add)
        yield

    def splits(t, gap):
        P, nw = PP[t], NW[t]
        nc, k = P // 512, nw // 16
        ps = [x for c in range(nc) for x in banks(t, c)]
        for q, (b, lo, hi) in zip("SVSV", ps):
            lift = 1 + sum(MK[t][n][lo // 512] == "S" for n in range(5))
            add(q, A("in0", lo, hi), A(b, 0, hi - lo), lift)
            one(b, 0, hi - lo, "eye", A("in0", lo, hi), True, False)
        for c, q in enumerate("VS" * nc):
            add(q, A("gr1", 256 * c, 256 * c + 256), ind(A("in0", 0, P), A("pl", 16 * c, 16 * c + 16)), 0)
            for b, lo, hi in ps:
                if hi == 256 * c + 256:
                    one(b, 0, hi - lo, "eye", A("gr1", lo, hi), False, True)
        for q, (b, lo, hi) in zip("VSVS", ps):
            if q == "S":
                act(A("in1", lo, hi), A(b, 0, hi - lo), AF.Sign)
            else:
                ts(A("in1", lo, hi), A(b, 0, hi - lo), 0, OP.is_gt)
        toS("p4", 0, "cq", "in1", 0, P - 1024, False, False)
        toS("p4", nw - 64, "cq", "in1", P - 1024, P, False, True)
        ts(A("lf", 0, 3 * nw), A("p7", 0, 3 * nw), 1552, OP.add, 16 + GH, OP.min)
        go = A("go", 0, nw)
        ts(go, A("p4", 0, nw), 11, OP.is_ge)
        one("p5", 0, nw, "blk", go)
        one("p5", nw, 2 * nw, "eye", A("d16", 0, nw), True, False)
        one("p5", nw, 2 * nw, "nblk", go, False, True)
        for e, x in enumerate((A("me16", 0, nw), A("st", L(t, 2), L(t, 2) + nw))):
            mm("p0", [(A("p0", nw * e, nw * e + nw), A(m, 0, 128), y, m == "eye", m == "blka") for m, y in (("eye", x), ("tri", go), ("blka", go))])
        scan(A("inc", 1, nw + 1), A("p5", 0, nw), A("zer", 0, nw), OP.add, OP.add)
        tt(A("ofr", 0, nw), A("inc", 0, nw), A("p5", nw, 2 * nw), OP.max)
        act(A("val", 0, 2 * nw), A("p0", 0, 2 * nw), AF.Identity, bias=1537.0 - 32 * BIG)
        toS("p4", 0, "s0", "ofr", 0, nw)
        cp(A("off", 0, k), A("p4", 0, k))
        for e in range(2):
            scat(A("Z%d" % e, 0, 2048), A("off", 0, k), A("val", nw * e, nw * e + nw))
        for e in range(2):
            scan(A("sc", 256 * e, 256 * e + 256), A("m4k", 0, 256), A("Z%d" % e, 0, 256), OP.add, OP.max)
        for e in range(2):
            ts(A("y16", 256 * e, 256 * e + 256), A("sc", 256 * e, 256 * e + 256), 0, OP.max, BIG, OP.min)
        mm("p5", [(A("p5", 0, 32), M("cq", q), (X("y16", 256 * (q % 2) + q // 2, 256 * (q % 2) + 256, 8), [("y16", 0, 512)]), q == 0, q == 15)
                  for q in range(16)])
        gap()
        cd = codes(t)
        next(cd)
        ts(A("ti", 0, 32), A("p5", 0, 32), -1, OP.add)
        next(cd)
        ts(A("ti2", 0, 32), A("ti", 0, 32), 4095, OP.bitwise_and)
        next(cd)
        tt(A("t32", 0, 32), A("ti2", 0, 32), A("meS", nw, nw + 32), OP.min)
        cp(A("TL", 0, 32), A("t32", 0, 32))
        ts(A("big", 0, 32), A("t32", 0, 32), PP[t], OP.is_ge, BIG, OP.mult)

    def weigh(t):
        nw = NW[t]
        tt(A("hz", 0, 32), A("p3", 0, 32), A("t32", 0, 32), OP.add)
        tt(A("hz", 32, 64), A("p3", 0, 32), A("meS", nw, nw + 32), OP.add)
        yield
        ts(A("hz2", 0, 64), A("hz", 0, 64), 2047, OP.bitwise_and)
        yield
        cp(A("eo", 0, 32), A("hz2", 0, 32))
        tt(A("hb", 0, 32), A("hz2", 32, 64), A("big", 0, 32), OP.add)
        yield
        ts(A("eo", 32, 64), A("hb", 0, 32), 2048, OP.min)
        yield

    def details(i, b):
        y = A("fs", 512 * i, 512 * i + 512)
        act(y, ind(A("dtb", 0, 2064), A("eo", 32 * i, 32 * i + 32)))
        one(b, 0, 512, "eye", A("e2", 0, 512), True, False)
        one(b, 0, 512, "eye", y, False, True)

    NTW = A("NT", 0, 2592)

    def rename(q, t, n, i, c0, c1):
        add(q, A(n, 16 * c0, 16 * c1), ind(NTW, A("lf", NW[t] * i + c0, NW[t] * i + c1)), 0)

    def heads(t):
        P, w = PP[t], WN[t]
        tl = A("TL", 0, 32)
        scat(A("NT", 16, 16 + P + 512), tl, (X("jr", 0, 512), [("jr0", 0, 512), ("jr1", 0, 512)]))
        act(A("eT", 0, 512), ind(U(0, 16, 16 + P + 512), tl))
        act(A("e2", 0, 512), A("eT", 0, 512), AF.Identity, bias=128.75, scale=0.5)
        toS("p3", 0, "wq", "eT", 0, 512)

    def news(t):
        P, w = PP[t], WN[t]
        ts(A("gf", 0, 512), ind(A("TB", 0, P + 512), A("TL", 0, 32)), -1536, OP.add)
        for i, m in enumerate(("s2", "s3", "s1")):
            toN("p6", w * i, w, m, "gf", 0, P, P + 512, False, i == 2)

    def owns(t):
        P, w = PP[t], WN[t]
        one("p2", 0, 2 * w, "e8k", A("ones", 0, 2 * w), True, False)
        for i, m in enumerate(("mn", "mq")):
            toN("p2", w * i, w, m, "NT", 16, 0, P, False, i == 1)

    def right_bases(t):
        P, w = PP[t], WN[t]
        act(A("vy", 0, 512), ind(A("vR", 0, P + 512), A("TL", 0, 32)))

    NB = ("p1", "p0", "p5")

    def turnN(t, n, i, x0, x1, last=False):
        toN(NB[i], 0, WN[t], "wn", n, 0 if n == "vy" else x0, x0, x1, x0 == 0, last)

    def early(t):
        w = WN[t]
        act(A("old", 0, 3 * w), A("p6", 0, 3 * w), AF.Identity, bias=1536.0)
        act(A("p7", 0, w), A("p2", 0, w), AF.Relu)

    def update(t, i):
        w = WN[t]
        x = A("lrb", w * i, w * i + w)
        tt(x, A("old", w * i, w * i + w), A(NB[i], 0, w), OP.max)
        yield
        tt(A("ua", w * i, w * i + w), x, A("p2", w * i, w * i + w) if i < 2 else A("p7", w, 2 * w), OP.min)
        if i == 0:
            tt(A("p7", w, 2 * w), A("p7", 0, w), x, OP.subtract)
        yield

    def size(t, i):
        w = WN[t]
        act(A("new", w * i, w * i + w), A("ua", w * i, w * i + w), AF.Abs)

    def cast(i):
        ts(R("r16", 0, 3, 512 * i, 512 * i + 512), R("raw", 0, 3, 512 * i, 512 * i + 512), -1536, OP.add)
    def table(i):
        b = "p%d" % i
        mm(b, [(A(b, 0, 512), (X("tsel", 0, 128, 1, 0, 24), [("tsel", 0, 128)]), R("r16", 0, 3, 512 * i, 512 * i + 512), True, True)])
        add("S", A("TB", 512 * i, 512 * i + 512), A(b, 0, 512), 1536)
    ts(A("n3", 0, 1), A("qf", 0, 1), 3, OP.is_lt)
    ts(A("n3", 1, 2), A("pq", 3, 4), -1, OP.add)
    ts(A("snl", 0, 32), A("p4", 0, 32), 1536, OP.add)
    sel(A("eye", 0, 128), A("ones", 0, 128), [[-1, 128]], OP.is_equal, 0, 1)
    ghost0(0, "SS")
    for s in range(2):
        act(A("snt", 16 + 272 * s, 272 + 272 * s), A("p5", 256 * s, 256 * s + 256), AF.Identity, bias=1536.0)
    cast(0)
    cast(1)
    table(0)
    table(1)
    slots(0)
    toS("p4", 0, "s2", "gs", 0, 512)
    cast(2)
    base_send("p4")
    iota(A("mem0", 0, 384), [[0, 24], [16, 16]], 0, 0)
    table(2)
    turn(0, 0)
    slot_legs(0)
    turn(0, 1)
    iota(A("TB", V0, GH), [[1, 1024]], V0, 0)
    iota(A("c160", 0, 160), [[1, 160]], 0, 0)
    for n in range(6):
        ms(A("UU", US * n, US * n + 16), 0.0)
    ms(A("gb", 0, 1), 1536.5 - GH)
    act(A("b0", 0, 32), A("p4", 0, 32))
    act(A("s2k", 0, 144), A("s2", 0, 144), scale=BIG)
    act(A("n4k", 0, 128), A("eye", 0, 128), scale=-BIG)
    act(A("mem", 0, 384), A("mem0", 0, 384), AF.Identity, bias=A("qf", 0, 1))
    for lo in (0, 272, 544):
        ms(A("snt", lo, lo + 16), -1.0)
    wrapped(0, 0)
    for n in range(5):
        ms(U(n, V0 + 528, V0 + 544), 0.0)
    cp(A("thf", 0, 1), A("thi", 0, 1))
    ts(A("thb", 0, 1), A("thi", 0, 1), -1, OP.mult, 0.5, OP.add)
    cp(A("wtf", 0, 1), A("wti", 0, 1))
    slot_lists(0)
    ts(A("jb", 3, 4), A("pq", 4, 5), 8192, OP.mult, A("pq", 3, 4), OP.add)
    ts(A("jb", 2, 3), A("pq", 3, 4), -2, OP.mult, A("pq", 2, 3), OP.add)
    cp(A("snS", 0, 32), A("snl", 0, 32))
    tt(A("jb", 2, 3), A("jb", 2, 3), A("jb", 3, 4), OP.add)
    for t in range(2):
        act(A("sh%d" % t, 0, 128), A("eye", 0, 128), scale=(PP[t] - GH) / 2)
    sides(0, 0)
    sides(0, 2)
    wrapped(0, 1)
    sides(0, 1)
    turn(0, 2)
    marks(0, 0, 0, "V")
    ghost_bases("VS")

    sel((X("za", 16, 144, 16), [("za", 0, 144)]), A("ones", 0, 8), [[-16, 8]], OP.is_ge, 0, 1)
    sel((X("cq", 16, 144, 16), [("cq", 0, 144)]), (X("za", 16, 144, 16), [("za", 0, 144)]), [[16, 8]], OP.is_ge, 15, -1)
    sel(A("blka", 0, 128), A("ones", 0, 128), [[-16, 8], [0, 16]], OP.is_ge, 0, 1)
    sel(A("blk", 0, 128), A("blka", 0, 128), [[16, 8], [0, 16]], OP.is_ge, 15, -1)
    sel(A("tri", 0, 128), A("blk", 0, 128), [[1, 128]], OP.is_gt, 0, -1)
    fill("za", 0, 144)
    prep(0, 0, 4)

    def consts():
        fill("zer", 0, 128)
        fill("ones", 128, 480, 1)
        iota(A("kq", 0, 256), [[2, 256]], 0, 0)
        fill("dtb", 2048, 2064, 129)

    def consts2():
        iota(A("d16", 0, 128), [[8, 128]], 1024, 0)
        fill("NT", 0, 768)

    def late0():
        act(A("s1k", 0, 144), A("s1", 0, 144), scale=BIG)
        act(A("meS", 0, 160), A("c160", 0, 160), AF.Identity, bias=A("qf", 0, 1), scale=16.0)
        act(A("n64", 0, 128), A("eye", 0, 128), scale=-64.0)
        ts(A("me16", 0, 128), A("meS", 0, 128), -1536, OP.add)
        ts(A("slc", 0, 32), A("meS", 0, 32), GH - 1536, OP.add)

    def late1():
        ts(A("inc", 0, 1), A("zer", 0, 1), 0, OP.add)
        one("p5", 0, 32, "eye", A("snS", 0, 32), True, False)
        one("p5", 0, 32, "n4k", A("slc", 0, 32), False, False)
        toS("p5", 0, "s1k", "gs", 0, 512, False, True)
        act(A("qn", 0, 1), A("qf", 0, 1), scale=96.0)
        act(A("meN", 0, 96), A("c160", 0, 96), AF.Identity, bias=A("qn", 0, 1))

    def late2():
        dma("Y", (T["TB"][3:128:16, 0:V0], [("TB", 0, V0)]), A("meN", 0, 96))
        act(A("nblk", 0, 128), A("blk", 0, 128), scale=-BIG)
        act(A("blka", 0, 128), A("eye", 0, 128), scale=32 * BIG)
        act(A("tri", 0, 128), A("tri", 0, 128), scale=BIG)
        ts(A("snf", 0, 32), A("p5", 0, 32), 16, OP.add, 16 + GH, OP.min)

    def late3():
        cp(A("sn0", 0, 32), A("snl", 0, 32))
        tt(A("dl", 0, 32), A("st", 0, 32), A("b0", 0, 32), OP.subtract)
        tt(A("dl", 32, 64), A("slc", 0, 32), A("st", 0, 32), OP.subtract)

    def load_det():
        wait_for("Y", needs("Y", ghosts(0, 4, 0)[1] + ghosts(0, 4, 1)[1], []))
        dma("Y", A("dtb", 0, 2048), HB("det"))

    def zs():
        for e in range(2):
            fill("Z%d" % e, 0, 256)

    depths(0, {-3: [lambda: wrapped(0, 2)], 0: [late0, lambda: flags0(0), lambda: bases(0, 0, 1), consts],
               1: [lambda: bases(0, 1, 3), consts2, late1, lambda: pens(0), lambda: olds(0)],
               2: [lambda: bases(0, 3, 6), lambda: flags1(0), lambda: fill("NT", 768, 1792)],
               3: [late2, lambda: flags2(0), lambda: fill("m4k", 0, 256, -4096), zs, lambda: fill("NT", 1792, 2592)],
               4: [load_det, lambda: fill("vR", V0, GH)]})
    splits(0, late3)
    act(A("wq", 0, 144), A("cq", 0, 144), scale=A("wtf", 0, 1))
    act(A("wn", 0, 144), A("cq", 0, 144), scale=A("n3", 0, 1))
    act(A("mn", 0, 144), A("cq", 0, 144), scale=A("n3", 1, 2))
    act(A("mq", 0, 144), A("cq", 0, 144), scale=-1.0)
    act(A("e8k", 0, 128), A("eye", 0, 128), scale=8192.0)
    act(A("dtb", 0, 2048), A("dtb", 0, 2048), AF.Identity, bias=128.75, scale=0.5)

    def rows(i):
        return ("Y", (T["TB"][i:128:16, 0:2048], [("TB", 0, 2048)]), A("new", 128 * i, 128 * i + 128))

    def half(i):
        ts(A("n16", 128 * i, 128 * i + 128), A("new", 128 * i, 128 * i + 128), -1536, OP.add)
        dma("Y", R("r16", i, i + 1, 0, 2048), A("n16", 128 * i, 128 * i + 128))
    heads(0)
    act(A("vs", 0, 512), ind(A("NT", 16, 16 + V0), A("snl", 0, 32)))
    act(A("vs", 512, 1024), ind(NTW, A("snf", 0, 32)))
    owns(0)
    news(0)
    rename("V", 0, "vR", 1, 0, 96)
    toS("p4", 0, "wn", "vs", 0, 1024)
    rename("S", 0, "vL", 0, 0, 64)
    turnN(0, "vR", 1, 0, V0, True)
    right_bases(0)
    rename("S", 0, "vL", 0, 64, 96)
    early(0)
    rename("S", 0, "vB", 2, 64, 96)
    rename("V", 0, "vB", 2, 0, 64)
    turnN(0, "vL", 0, 0, V0, True)
    turnN(0, "vB", 2, 0, 1024)
    turnN(0, "vy", 2, V0, 2048)
    turnN(0, "vB", 2, 1024, V0, True)
    wg, up = weigh(0), [update(0, i) for i in range(3)]
    ts(A("sp", 0, 64), A("p4", 0, 64), 0, OP.is_gt)
    next(wg)
    tt(A("bx", 0, 64), A("sp", 0, 64), A("dl", 0, 64), OP.mult)
    next(wg)
    tt(A("sn1", 0, 32), A("sn0", 0, 32), A("p4", 32, 64), OP.max)
    tt(A("sp", 0, 32), A("bx", 0, 32), A("bx", 32, 64), OP.add)
    next(wg)
    tt(A("bx", 0, 32), A("sp", 0, 32), A("b0", 0, 32), OP.add)
    next(wg)
    details(0, "p3")
    next(up[1])
    base_send("bx")
    next(up[0])
    next(up[1])
    cp(A("snl", 0, 32), A("sn1", 0, 32))
    next(up[0])
    size(0, 0)
    size(0, 1)
    mm("p0", [(A("p0", 0, 512), M("wn", 2), A("vs", 512, 1024), True, True)])
    next(up[2])
    half(0)
    next(up[2])
    size(0, 2)
    half(1)
    dmas([rows(i) for i in range(3)])
    act(A("cT", 0, 512), A("p3", 0, 512), AF.Identity, bias=-258.0)
    half(2)
    details(1, "p4")
    for s in range(2):
        x = A("snt", 16 + 272 * s, 272 + 272 * s)
        tt(x, x, A("p0", 256 * s, 256 * s + 256), OP.max)
    scat(U(0, 16, 16 + 2048), A("TL", 0, 32), A("cT", 0, 512))
    ghost_bases("SS")
    act(U(0, 16 + V0, 16 + 2048), A("p4", 0, 512), AF.Identity, bias=-258.0)
    ghost0(1, "SS")
    turn(1, 0)
    turn(1, 1)
    for c in range(3):
        marks(1, 0, c, "V")
    wrapped(1, 0)
    sides(1, 0)
    slots(1)
    wrapped(1, 1)
    slot_legs(1)
    prep(1, 2, 5)
    turn(1, 2)
    depths(1, {-3: [lambda: wrapped(1, 2)], 0: [lambda: flags0(1), lambda: bases(1, 0, 3), lambda: fill("NT", 16, 1040), lambda: olds(1)],
               1: [lambda: bases(1, 3, 6), lambda: fill("NT", 1040, 2064), lambda: pens(1)],
               2: [lambda: bases(1, 6, 8), lambda: flags1(1), zs],
               3: [lambda: flags2(1)]})
    splits(1, lambda: None)
    act(A("dtb", 0, 2064), A("dtb", 0, 2064), AF.Identity, bias=-258.0)

    def out(i):
        size(1, i)
        dma("Y", HB(("yl", "yr", "yb")[i]), A("new", 160 * i, 160 * i + 160))
    heads(1)
    rename("S", 1, "vR", 1, 0, 128)
    owns(1)
    wg, up = weigh(1), [update(1, i) for i in range(3)]
    next(wg)
    news(1)
    next(wg)
    rename("V", 1, "vL", 0, 0, 32)
    next(wg)
    x = [ind(A("dtb", 0, 2064), A("eo", 32 * i, 32 * i + 32)) for i in range(2)]
    tt(A("cT", 0, 512), x[0], A("e2", 0, 512), OP.add)
    next(wg)
    rename("V", 1, "vL", 0, 32, 48)
    scat(U(0, 16, 16 + GH), A("TL", 0, 32), A("cT", 0, 512))
    dma("Y", (T["ye"][:, 0:2048], []), U(0, 16, 16 + 2048))
    turnN(1, "vR", 1, 0, 2048, True)
    right_bases(1)
    early(1)
    rename("S", 1, "vL", 0, 96, 128)
    next(up[1])
    rename("V", 1, "vL", 0, 48, 96)
    next(up[1])
    rename("S", 1, "vB", 2, 0, 64)
    out(1)
    turnN(1, "vL", 0, 0, 2048, True)
    turnN(1, "vB", 2, 0, 1024)
    turnN(1, "vy", 2, 2048, GH)
    rename("V", 1, "vB", 2, 96, 128)
    rename("S", 1, "vB", 2, 64, 96)
    next(up[0])
    turnN(1, "vB", 2, 1024, 2048, True)
    tt(A("sb0", 0, 512), x[1], A("e2", 0, 512), OP.add)
    dma("Y", (T["ye"][:, 2048:GH], []), A("sb0", 0, 512))
    next(up[0])
    out(0)
    next(up[2])
    next(up[2])
    out(2)
    wait_for("Y", {s: v for s, v in cnt.items()})
